import numpy as np
import ml_dtypes


def mxq(x, axis, fmt="e4m3"):
    dtype, down = {"e4m3": (ml_dtypes.float8_e4m3fn, 7), "e5m2": (ml_dtypes.float8_e5m2, 14)}[fmt]
    v = np.moveaxis(np.asarray(x, np.float32).astype(ml_dtypes.bfloat16).astype(np.float64), axis, -1)
    blocks = v.reshape(v.shape[:-1] + (-1, 32))
    amax = np.abs(blocks).max(-1, keepdims=True)
    byte = np.maximum(np.where(amax > 0, np.frexp(amax)[1] - 1 + 127, 0) - down, 1)
    scale = np.exp2(byte - 127.0)
    codes = (blocks / scale).astype(np.float32).astype(dtype).astype(np.float64)
    return np.moveaxis((codes * scale).reshape(v.shape), -1, axis)


WIDE = False


def mx_kscale(k):
    if not WIDE:
        return np.ones(k)
    levels = np.array([10, -10, 5, -5, 0])
    if k % 512:
        return np.exp2(np.random.permutation(np.resize(levels, k // 32))).repeat(32)
    a = np.empty((k // 512, 16))
    for p in range(k // 512):
        a[p, :8] = np.random.permutation(np.resize(levels, 8))
        for g in range(8):
            far = levels[np.abs(levels - a[p, g]) >= 10]
            a[p, g + 8] = far[np.random.randint(len(far))]
    return np.exp2(a.ravel()).repeat(32)


def f64(x):
    return np.asarray(x).astype(np.float64)


def striped(idx):
    return np.tile(idx.reshape(-1, 16).T, (8, 1)).astype(np.uint16)


def unstriped(offs):
    return offs[:16].T.reshape(-1).astype(np.int64)


E2M1 = np.array([0.0, 0.5, 1.0, 1.5, 2.0, 3.0, 4.0, 6.0, -0.0, -0.5, -1.0, -1.5, -2.0, -3.0, -4.0, -6.0])


def pack_weight(w, fmt):
    k, n = w.shape
    w = f64(np.asarray(w, np.float32).astype(ml_dtypes.bfloat16)).reshape(k // 32, 32, n)
    amax = np.abs(w).max(1)
    if fmt == "e4m3":
        byte = np.frexp(amax)[1] - 1 + 127 - 7
    else:
        mant, ex = np.frexp(amax / 6.0)
        byte = np.where(mant > 0.5, ex, ex - 1) + 127
    byte = np.clip(np.where(amax > 0, byte, 1), 1, 254)
    scaled = (w * np.exp2(127.0 - byte)[:, None, :]).reshape(k, n).astype(np.float32)
    by_word = np.ascontiguousarray(scaled.reshape(k // 512, 128, 4, n).transpose(0, 1, 3, 2))
    if fmt == "e4m3":
        words = by_word.astype(ml_dtypes.float8_e4m3fn).view(np.uint8)
    else:
        c = by_word.astype(ml_dtypes.float4_e2m1fn).view(np.uint8) & 0xF
        words = (c[..., 0::2] | (c[..., 1::2] << 4)).reshape(k // 512, 128, 2 * n)
    return np.ascontiguousarray(words), np.ascontiguousarray(byte.astype(np.uint8).reshape(k // 512, 16, n))


def unpack_weight(words, scales, fmt):
    g, _, n = scales.shape
    words = np.ascontiguousarray(words).reshape(g, 128, n, -1)
    if fmt == "e4m3":
        vals = words.view(ml_dtypes.float8_e4m3fn).astype(np.float64)
    else:
        nib = np.empty((g, 128, n, 4), np.uint8)
        nib[..., 0::2] = words & 0xF
        nib[..., 1::2] = words >> 4
        vals = E2M1[nib]
    vals = vals * np.repeat(np.exp2(scales.astype(np.float64) - 127.0), 8, axis=1)[..., None]
    return vals.transpose(0, 1, 3, 2).reshape(g * 512, n)


def gelu(v):
    return 0.5 * v * (1.0 + np.tanh(np.sqrt(2.0 / np.pi) * (v + 0.044715 * v**3)))


K, T, S, T2, S2, N = 1024, 2048, 1024, 4096, 1024, 256

def setup_inputs():
    n = np.random.standard_normal
    s = mx_kscale(K)[:, None]
    u = mx_kscale(S)[:, None]
    tab_words, tab_scales = pack_weight(n((K, T)) * s / np.sqrt(K), "e4m3")
    tab2_words, tab2_scales = pack_weight(n((K, T2)) / s, "e4m3")
    w4_words, w4_scales = pack_weight(2.0 * n((S, N)) / np.sqrt(S) / u, "e2m1")
    return {
        "tab_words": tab_words, "tab_scales": tab_scales,
        "tab2_words": tab2_words, "tab2_scales": tab2_scales,
        "offs": striped(np.random.permutation(T)[:S]),
        "offs2": striped(np.random.permutation(T2)[:S2]),
        "fresh": (np.exp(-np.random.random(S)) * u[:, 0]).astype(np.float32),
        "w4_words": w4_words, "w4_scales": w4_scales,
        "wd": (n((S, N)) / np.sqrt(S) / u).astype(np.float32),
        "gate": (1.0 / (1.0 + np.exp(-n((N, S2))))).astype(np.float32),
    }

def reference(tab_words, tab_scales, tab2_words, tab2_scales, offs, offs2, fresh, w4_words, w4_scales, wd, gate):
    v = unpack_weight(tab_words, tab_scales, "e4m3")[:, unstriped(offs)]
    v2 = unpack_weight(tab2_words, tab2_scales, "e4m3")[:, unstriped(offs2)]
    A = v.T @ v2
    z = f64(fresh)[:, None] * np.tanh(A)
    zq = mxq(z, 0, "e4m3")
    w4 = unpack_weight(w4_words, w4_scales, "e2m1")
    wdq = mxq(f64(wd), 0, "e4m3")
    y = w4.T @ zq + wdq.T @ zq
    return f64(gate) * y

@@ -1,0 +1,289 @@
+from contextlib import ExitStack
+
+import concourse.mybir as mybir
+
+K, T, S, T2, S2, N = 1024, 2048, 1024, 4096, 1024, 256
+FLOPS = 2 * K * S * S2 + 2 * 2 * S * N * S2
+
+F32 = mybir.dt.float32
+BF16 = mybir.dt.bfloat16
+I32 = mybir.dt.int32
+U32 = mybir.dt.uint32
+U16 = mybir.dt.uint16
+U8 = mybir.dt.uint8
+FP8X4 = mybir.dt.float8_e4m3fn_x4
+FP4X4 = mybir.dt.float4_e2m1fn_x4
+MULT = mybir.AluOpType.mult
+TANH = mybir.ActivationFunctionType.Tanh
+
+P = 128
+HALF = 512
+QUART = 256
+A_BANKS = 6
+G_COLS = 0
+ART_ROW = (0, 4)
+RDR_ROW = (8, 12)
+
+
+def tile_list_fresh_news_sections_kernel(
+    tc, tab_words, tab_scales, tab2_words, tab2_scales, offs, offs2, fresh, w4_words, w4_scales, wd, gate, out
+):
+    nc = tc.nc
+    with ExitStack() as ctx:
+        keep = ctx.enter_context(tc.tile_pool(name="keep", bufs=1))
+        ring = ctx.enter_context(tc.tile_pool(name="ring", bufs=4))
+        psum_a = ctx.enter_context(tc.psum_pool(name="psum_a", bufs=A_BANKS))
+        psum_y = ctx.enter_context(tc.psum_pool(name="psum_y", bufs=2))
+
+        def held(name, shape, dtype):
+            return keep.tile(shape, dtype, name=name, align_bytes=256)
+
+        art_list = keep.tile([P, S // 16], U16, name="art_list")
+        rdr_list = keep.tile([P, S2 // 16], U16, name="rdr_list")
+        art_tab = [held("art_tab%d" % a, [P, T], I32) for a in range(2)]
+        rdr_tab = [held("rdr_tab%d" % a, [P, T2], I32) for a in range(2)]
+        art_tab_sc = held("art_tab_sc", [P, T // 4], I32)
+        rdr_tab_sc = held("rdr_tab_sc", [P, T2 // 4], I32)
+        w4_sc = held("w4_sc", [P, 2, N // 4], I32)
+        w4_codes = held("w4_codes", [P, 2, 2 * N], U8)
+        fresh_sb = held("fresh_sb", [P, 2, 4], F32)
+        wd_raw = [held("wd_raw%d" % b, [P, 4, N], F32) for b in range(2)]
+        gate_sb = [held("gate_sb%d" % h, [P, 2, HALF], F32) for h in range(2)]
+        warm = held("warm", [P, 2], F32)
+
+        nc.vector.memset(rdr_tab_sc[:], 0)
+        nc.vector.memset(art_tab_sc[:], 0)
+        nc.vector.memset(w4_sc[:], 0)
+        nc.vector.memset(warm[:, 0:1], 0.0)
+
+        def words(table, a):
+            return table[a].rearrange("p t i -> p (t i)").bitcast(I32)
+
+        nc.sync.dma_start(art_list[:], offs)
+        for q in range(4):
+            nc.scalar.dma_start(
+                art_tab_sc[32 * q + ART_ROW[0] : 32 * q + ART_ROW[0] + 8, :], tab_scales[:, 4 * q : 4 * q + 4, :].bitcast(I32)
+            )
+        for q in range(4):
+            nc.gpsimd.dma_start(
+                rdr_tab_sc[32 * q + RDR_ROW[0] : 32 * q + RDR_ROW[0] + 8, :], tab2_scales[:, 4 * q : 4 * q + 4, :].bitcast(I32)
+            )
+        nc.scalar.activation(out=warm[:, 1:2], in_=warm[:, 0:1], func=TANH)
+        nc.sync.dma_start(art_tab[0][:], words(tab_words, 0))
+        nc.sync.dma_start(art_tab[1][:], words(tab_words, 1))
+        nc.sync.dma_start(rdr_list[:], offs2)
+        nc.sync.dma_start(rdr_tab[0][:], words(tab2_words, 0))
+        nc.sync.dma_start(rdr_tab[1][:], words(tab2_words, 1))
+        nc.sync.dma_start(fresh_sb[:], fresh.rearrange("(b p t) -> p b t", b=2, t=4))
+        for b in range(2):
+            nc.sync.dma_start(wd_raw[b][:], wd[HALF * b : HALF * (b + 1), :].rearrange("(p t) n -> p t n", t=4))
+        nc.sync.dma_start(w4_codes[:].bitcast(I32), w4_words.rearrange("a p c -> p a c").bitcast(I32))
+        for q in range(4):
+            nc.sync.dma_start(
+                w4_sc[32 * q : 32 * q + 4, :, :], w4_scales[:, 4 * q : 4 * q + 4, :].rearrange("a r c -> r a c").bitcast(I32)
+            )
+        for h in range(2):
+            nc.sync.dma_start(gate_sb[h][:], gate[:, HALF * h : HALF * (h + 1)].rearrange("(n p) j -> p n j", p=P))
+
+        art_sc_listed = held("art_sc_listed", [P, S], U8)
+        art_sc = held("art_sc", [P, S], U8)
+        rdr_sc = held("rdr_sc", [P, S2], U8)
+        art = [[held("art%d%d" % (a, b), [P, HALF], U32) for b in range(2)] for a in range(2)]
+        rdr = [[held("rdr%d%d" % (a, h), [P, HALF], U32) for h in range(2)] for a in range(2)]
+
+        def part(lst, c):
+            return lst[:, 32 * c : 32 * (c + 1)]
+
+        def gather_art(a, b):
+            nc.vector.tensor_copy(
+                art[a][b][:].rearrange("p (t m) -> p m t", t=4), art_tab[a][:].bitcast(U32).indirect(part(art_list, b))
+            )
+
+        def gather_rdr(a, h):
+            nc.vector.tensor_copy(rdr[a][h][:], rdr_tab[a][:].bitcast(U32).indirect(part(rdr_list, h)))
+
+        gather_art(0, 0)
+        gather_art(0, 1)
+        nc.vector.tensor_copy(art_sc_listed[:], art_tab_sc[:].bitcast(U8).indirect(art_list[:]))
+        gather_art(1, 0)
+        nc.vector.tensor_copy(
+            art_sc[:].rearrange("p (b t m) -> p b t m", b=2, t=4), art_sc_listed[:].rearrange("p (b m t) -> p b t m", b=2, t=4)
+        )
+        gather_art(1, 1)
+        nc.vector.tensor_copy(rdr_sc[:], rdr_tab_sc[:].bitcast(U8).indirect(rdr_list[:]))
+        gather_rdr(0, 1)
+        gather_rdr(0, 0)
+        gather_rdr(1, 0)
+        gather_rdr(1, 1)
+
+        steps = [(0, b, q) for b in range(2) for q in range(2)] + [(1, b, q) for q in range(2) for b in range(2)]
+        units = [(h, b, q, u) for (h, b, q) in steps for u in range(2)]
+
+        def match_pass(bank, unit, e, a):
+            h, b, q, u = unit
+            t = 2 * u + e
+            nc.tensor.matmul_mx(
+                out=bank[:, e, :],
+                lhsT=art[a][b][:, P * t : P * (t + 1)].bitcast(FP8X4),
+                lhsT_scale=art_sc[ART_ROW[a] :, HALF * b + P * t : HALF * b + P * (t + 1)],
+                rhs=rdr[a][h][:, QUART * q : QUART * (q + 1)].bitcast(FP8X4),
+                rhs_scale=rdr_sc[RDR_ROW[a] :, HALF * h + QUART * q : HALF * h + QUART * (q + 1)],
+                start=(a == 0),
+                stop=(a == 1),
+            )
+
+        banks = {}
+        for unit in units[:A_BANKS]:
+            banks[unit] = psum_a.tile([P, 2, QUART], F32, name="a_bank")
+            match_pass(banks[unit], unit, 0, 0)
+
+        wd_bf = [held("wd_bf%d" % b, [P, N, 4], BF16) for b in range(2)]
+        wd_codes = held("wd_codes", [P, 2 * N], U32)
+        wd_sc = held("wd_sc", [P, 2 * N], U8)
+        z_codes = {(h, b): held("z_codes%d%d" % (h, b), [P, HALF], U32) for h in range(2) for b in range(2)}
+        z_sc = {(h, b): held("z_sc%d%d" % (h, b), [P, HALF], U8) for h in range(2) for b in range(2)}
+        z_bf = {}
+        y_bank = {}
+
+        def match(step):
+            h, b, q = step
+            bounded = ring.tile([P, 2, QUART, 2], F32, name="bounded")
+            for u in range(2):
+                unit = (h, b, q, u)
+                if unit not in banks:
+                    banks[unit] = psum_a.tile([P, 2, QUART], F32, name="a_bank")
+                    match_pass(banks[unit], unit, 0, 0)
+                match_pass(banks[unit], unit, 0, 1)
+                match_pass(banks[unit], unit, 1, 0)
+                match_pass(banks[unit], unit, 1, 1)
+                nc.scalar.activation(out=bounded[:, u, :, :], in_=banks[unit][:].rearrange("p e j -> p j e"), func=TANH)
+            z_bf[step] = ring.tile([P, QUART * 4], BF16, name="z_bf", align_bytes=64)
+            nc.vector.tensor_tensor(
+                z_bf[step][:].rearrange("p (j u e) -> p j u e", u=2, e=2),
+                bounded[:].rearrange("p u j e -> p j u e"),
+                fresh_sb[:, b, :].rearrange("p (u e) -> p u e", u=2).unsqueeze(1).to_broadcast([P, QUART, 2, 2]),
+                MULT,
+            )
+
+        def quantise(step):
+            h, b, q = step
+            cols = slice(QUART * q, QUART * (q + 1))
+            nc.vector.quantize_mx(out=z_codes[h, b][:, cols].bitcast(FP8X4), scales=z_sc[h, b][:, cols], in_=z_bf[step][:])
+
+        def sections(h, b):
+            for n in range(2):
+                if b == 0:
+                    y_bank[h, n] = psum_y.tile([P, HALF], F32, name="y_bank")
+                nc.tensor.matmul_mx(
+                    out=y_bank[h, n][:],
+                    lhsT=w4_codes[:, b, 2 * P * n : 2 * P * (n + 1)].bitcast(FP4X4),
+                    lhsT_scale=w4_sc[:, b, :].bitcast(U8)[:, P * n : P * (n + 1)],
+                    rhs=z_codes[h, b][:].bitcast(FP8X4),
+                    rhs_scale=z_sc[h, b][:],
+                    start=(b == 0),
+                    stop=False,
+                )
+                cols = slice(N * b + P * n, N * b + P * (n + 1))
+                nc.tensor.matmul_mx(
+                    out=y_bank[h, n][:],
+                    lhsT=wd_codes[:, cols].bitcast(FP8X4),
+                    lhsT_scale=wd_sc[:, cols],
+                    rhs=z_codes[h, b][:].bitcast(FP8X4),
+                    rhs_scale=z_sc[h, b][:],
+                    start=False,
+                    stop=(b == 1),
+                )
+
+        def finish(h):
+            for n in range(2):
+                res = ring.tile([P, HALF], F32, name="res")
+                nc.vector.tensor_tensor(res[:], y_bank[h, n][:], gate_sb[h][:, n, :], MULT)
+                nc.sync.dma_start(out[P * n : P * (n + 1), HALF * h : HALF * (h + 1)], res[:])
+
+        def narrow_passes(dst, b, n, col):
+            cols = slice(col, col + P)
+            nc.tensor.matmul_mx(
+                out=dst,
+                lhsT=w4_codes[:, b, 2 * P * n : 2 * P * (n + 1)].bitcast(FP4X4),
+                lhsT_scale=w4_sc[:, b, :].bitcast(U8)[:, P * n : P * (n + 1)],
+                rhs=z_codes[1, b][:, cols].bitcast(FP8X4),
+                rhs_scale=z_sc[1, b][:, cols],
+                start=(b == 0),
+                stop=False,
+            )
+            wcols = slice(N * b + P * n, N * b + P * (n + 1))
+            nc.tensor.matmul_mx(
+                out=dst,
+                lhsT=wd_codes[:, wcols].bitcast(FP8X4),
+                lhsT_scale=wd_sc[:, wcols],
+                rhs=z_codes[1, b][:, cols].bitcast(FP8X4),
+                rhs_scale=z_sc[1, b][:, cols],
+                start=False,
+                stop=(b == 1),
+            )
+
+        def third_quarter():
+            for n in range(2):
+                bank = psum_y.tile([P, 2, P], F32, name="y_bank")
+                for c in range(2):
+                    for b in range(2):
+                        narrow_passes(bank[:, c, :], b, n, P * c)
+                y_bank["third", n] = bank
+
+        def finish_third():
+            res = ring.tile([P, 2, QUART], F32, name="res")
+            for n in range(2):
+                nc.vector.tensor_tensor(
+                    res[:, n, :], y_bank["third", n][:].rearrange("p c j -> p (c j)"), gate_sb[1][:, n, 0:QUART], MULT
+                )
+            nc.sync.dma_start(out[:, HALF : HALF + QUART].rearrange("(n p) j -> p n j", p=P), res[:])
+
+        def last_quarter(b):
+            for n in range(2):
+                for c in range(2):
+                    if b == 0:
+                        y_bank["last", n, c] = psum_a.tile([P, P], F32, name="a_bank")
+                    narrow_passes(y_bank["last", n, c][:], b, n, QUART + P * c)
+
+        def finish_last():
+            for n in range(2):
+                res = ring.tile([P, QUART], F32, name="res")
+                for c in range(2):
+                    nc.vector.tensor_tensor(
+                        res[:, P * c : P * (c + 1)],
+                        y_bank["last", n, c][:],
+                        gate_sb[1][:, n, QUART + P * c : QUART + P * (c + 1)],
+                        MULT,
+                    )
+                (nc.sync, nc.scalar)[n].dma_start(out[P * n : P * (n + 1), HALF + QUART :], res[:])
+
+        def quantise_wd(b):
+            cols = slice(N * b, N * (b + 1))
+            nc.vector.quantize_mx(
+                out=wd_codes[:, cols].bitcast(FP8X4), scales=wd_sc[:, cols], in_=wd_bf[b][:].rearrange("p n t -> p (n t)")
+            )
+
+        nc.vector.tensor_copy(out=wd_bf[0][:], in_=wd_raw[0][:].rearrange("p t n -> p n t"))
+
+        for s, step in enumerate(steps):
+            match(step)
+            if s > 0:
+                quantise(steps[s - 1])
+            if s == 0:
+                quantise_wd(0)
+            if s == 1:
+                nc.scalar.copy(out=wd_bf[1][:], in_=wd_raw[1][:].rearrange("p t n -> p n t"))
+            if s == 3:
+                quantise_wd(1)
+                sections(0, 0)
+            if s == 5:
+                sections(0, 1)
+            if s == 6:
+                finish(0)
+            if s == 7:
+                third_quarter()
+                last_quarter(0)
+        quantise(steps[-1])
+        finish_third()
+        last_quarter(1)
+        finish_last()

@@ -51,30 +51,41 @@ def tile_list_fresh_news_sections_kernel(
         gate_sb = [held("gate_sb%d" % h, [P, 2, HALF], F32) for h in range(2)]
         warm = held("warm", [P, 2], F32)
 
+        nc.gpsimd.memset(art_tab_sc[:], 0)
         nc.vector.memset(rdr_tab_sc[:], 0)
-        nc.vector.memset(art_tab_sc[:], 0)
         nc.vector.memset(w4_sc[:], 0)
         nc.vector.memset(warm[:, 0:1], 0.0)
+        nc.scalar.activation(out=warm[:, 1:2], in_=warm[:, 0:1], func=TANH)
 
         def words(table, a):
             return table[a].rearrange("p t i -> p (t i)").bitcast(I32)
 
+        def scale_rows(queue, tile, row, table):
+            for q in range(4):
+                queue.dma_start(tile[32 * q + row : 32 * q + row + 8, :], table[:, 4 * q : 4 * q + 4, :].bitcast(I32))
+
+        def scale_rows4(queue, tile, rows, table, a):
+            for q in range(4):
+                queue.dma_start(tile[32 * q + rows[a] : 32 * q + rows[a] + 4, :], table[a, 4 * q : 4 * q + 4, :].bitcast(I32))
+
+        def rdr_rows(a, q):
+            row = 32 * q + RDR_ROW[a]
+            nc.sync.dma_start(rdr_tab_sc[row : row + 4, :], tab2_scales[a, 4 * q : 4 * q + 4, :].bitcast(I32))
+
+        rows = [(a, q) for a in range(2) for q in range(4)]
         nc.sync.dma_start(art_list[:], offs)
-        for q in range(4):
-            nc.scalar.dma_start(
-                art_tab_sc[32 * q + ART_ROW[0] : 32 * q + ART_ROW[0] + 8, :], tab_scales[:, 4 * q : 4 * q + 4, :].bitcast(I32)
-            )
-        for q in range(4):
-            nc.gpsimd.dma_start(
-                rdr_tab_sc[32 * q + RDR_ROW[0] : 32 * q + RDR_ROW[0] + 8, :], tab2_scales[:, 4 * q : 4 * q + 4, :].bitcast(I32)
-            )
-        nc.scalar.activation(out=warm[:, 1:2], in_=warm[:, 0:1], func=TANH)
+        nc.sync.dma_start(rdr_list[:], offs2)
+        scale_rows(nc.sync, art_tab_sc, ART_ROW[0], tab_scales)
         nc.sync.dma_start(art_tab[0][:], words(tab_words, 0))
         nc.sync.dma_start(art_tab[1][:], words(tab_words, 1))
-        nc.sync.dma_start(rdr_list[:], offs2)
+        for a, q in rows[:6]:
+            rdr_rows(a, q)
         nc.sync.dma_start(rdr_tab[0][:], words(tab2_words, 0))
+        for a, q in rows[6:]:
+            rdr_rows(a, q)
         nc.sync.dma_start(rdr_tab[1][:], words(tab2_words, 1))
         nc.sync.dma_start(fresh_sb[:], fresh.rearrange("(b p t) -> p b t", b=2, t=4))
+
         for b in range(2):
             nc.sync.dma_start(wd_raw[b][:], wd[HALF * b : HALF * (b + 1), :].rearrange("(p t) n -> p t n", t=4))
         nc.sync.dma_start(w4_codes[:].bitcast(I32), w4_words.rearrange("a p c -> p a c").bitcast(I32))
@@ -87,7 +98,7 @@ def tile_list_fresh_news_sections_kernel(
 
         art_sc_listed = held("art_sc_listed", [P, S], U8)
         art_sc = held("art_sc", [P, S], U8)
-        rdr_sc = held("rdr_sc", [P, S2], U8)
+        rdr_sc = [held("rdr_sc%d" % h, [P, HALF], U8) for h in range(2)]
         art = [[held("art%d%d" % (a, b), [P, HALF], U32) for b in range(2)] for a in range(2)]
         rdr = [[held("rdr%d%d" % (a, h), [P, HALF], U32) for h in range(2)] for a in range(2)]
 
@@ -102,15 +113,26 @@ def tile_list_fresh_news_sections_kernel(
         def gather_rdr(a, h):
             nc.vector.tensor_copy(rdr[a][h][:], rdr_tab[a][:].bitcast(U32).indirect(part(rdr_list, h)))
 
+        def gather_art_sc():
+            nc.vector.tensor_copy(art_sc_listed[:], art_tab_sc[:].bitcast(U8).indirect(art_list[:]))
+
+        def sort_art_sc():
+            nc.vector.tensor_copy(
+                art_sc[:].rearrange("p (b t m) -> p b t m", b=2, t=4),
+                art_sc_listed[:].rearrange("p (b m t) -> p b t m", b=2, t=4),
+            )
+
+        def gather_rdr_sc(h):
+            nc.vector.tensor_copy(rdr_sc[h][:], rdr_tab_sc[:].bitcast(U8).indirect(part(rdr_list, h)))
+
+        gather_art_sc()
         gather_art(0, 0)
+        sort_art_sc()
         gather_art(0, 1)
-        nc.vector.tensor_copy(art_sc_listed[:], art_tab_sc[:].bitcast(U8).indirect(art_list[:]))
         gather_art(1, 0)
-        nc.vector.tensor_copy(
-            art_sc[:].rearrange("p (b t m) -> p b t m", b=2, t=4), art_sc_listed[:].rearrange("p (b m t) -> p b t m", b=2, t=4)
-        )
         gather_art(1, 1)
-        nc.vector.tensor_copy(rdr_sc[:], rdr_tab_sc[:].bitcast(U8).indirect(rdr_list[:]))
+        gather_rdr_sc(0)
+        gather_rdr_sc(1)
         gather_rdr(0, 1)
         gather_rdr(0, 0)
         gather_rdr(1, 0)
@@ -127,7 +149,7 @@ def tile_list_fresh_news_sections_kernel(
                 lhsT=art[a][b][:, P * t : P * (t + 1)].bitcast(FP8X4),
                 lhsT_scale=art_sc[ART_ROW[a] :, HALF * b + P * t : HALF * b + P * (t + 1)],
                 rhs=rdr[a][h][:, QUART * q : QUART * (q + 1)].bitcast(FP8X4),
-                rhs_scale=rdr_sc[RDR_ROW[a] :, HALF * h + QUART * q : HALF * h + QUART * (q + 1)],
+                rhs_scale=rdr_sc[h][RDR_ROW[a] :, QUART * q : QUART * (q + 1)],
                 start=(a == 0),
                 stop=(a == 1),
             )
@@ -263,18 +285,16 @@ def tile_list_fresh_news_sections_kernel(
                 out=wd_codes[:, cols].bitcast(FP8X4), scales=wd_sc[:, cols], in_=wd_bf[b][:].rearrange("p n t -> p (n t)")
             )
 
-        nc.vector.tensor_copy(out=wd_bf[0][:], in_=wd_raw[0][:].rearrange("p t n -> p n t"))
 
         for s, step in enumerate(steps):
             match(step)
             if s > 0:
                 quantise(steps[s - 1])
-            if s == 0:
-                quantise_wd(0)
-            if s == 1:
-                nc.scalar.copy(out=wd_bf[1][:], in_=wd_raw[1][:].rearrange("p t n -> p n t"))
+            if s in (1, 2):
+                nc.scalar.copy(out=wd_bf[s - 1][:], in_=wd_raw[s - 1][:].rearrange("p t n -> p n t"))
+            if s in (2, 3):
+                quantise_wd(s - 2)
             if s == 3:
-                quantise_wd(1)
                 sections(0, 0)
             if s == 5:
                 sections(0, 1)

@@ -17,12 +17,18 @@ MULT = mybir.AluOpType.mult
 TANH = mybir.ActivationFunctionType.Tanh
 
 P = 128
+PACK = 4
 HALF = 512
-QUART = 256
-A_BANKS = 6
-G_COLS = 0
+QUARTER = 256
+QUADRANTS = 4
+MATCH_BANKS = 6
 ART_ROW = (0, 4)
 RDR_ROW = (8, 12)
+STEPS = (
+    [(0, b, first, QUARTER) for b in range(2) for first in (0, QUARTER)]
+    + [(1, 0, 0, QUARTER), (1, 1, 0, QUARTER), (1, 0, QUARTER, QUARTER)]
+    + [(1, 1, QUARTER, P), (1, 1, QUARTER + P, P)]
+)
 
 
 def tile_list_fresh_news_sections_kernel(
@@ -32,66 +38,56 @@ def tile_list_fresh_news_sections_kernel(
     with ExitStack() as ctx:
         keep = ctx.enter_context(tc.tile_pool(name="keep", bufs=1))
         ring = ctx.enter_context(tc.tile_pool(name="ring", bufs=4))
-        psum_a = ctx.enter_context(tc.psum_pool(name="psum_a", bufs=A_BANKS))
-        psum_y = ctx.enter_context(tc.psum_pool(name="psum_y", bufs=2))
+        psum_match = ctx.enter_context(tc.psum_pool(name="psum_match", bufs=MATCH_BANKS))
+        psum_sum = ctx.enter_context(tc.psum_pool(name="psum_sum", bufs=2))
 
         def held(name, shape, dtype):
             return keep.tile(shape, dtype, name=name, align_bytes=256)
 
         art_list = keep.tile([P, S // 16], U16, name="art_list")
         rdr_list = keep.tile([P, S2 // 16], U16, name="rdr_list")
-        art_tab = [held("art_tab%d" % a, [P, T], I32) for a in range(2)]
-        rdr_tab = [held("rdr_tab%d" % a, [P, T2], I32) for a in range(2)]
-        art_tab_sc = held("art_tab_sc", [P, T // 4], I32)
-        rdr_tab_sc = held("rdr_tab_sc", [P, T2 // 4], I32)
+        art_table = [held("art_table%d" % a, [P, T], I32) for a in range(2)]
+        rdr_table = [held("rdr_table%d" % a, [P, T2], I32) for a in range(2)]
+        art_table_sc = held("art_table_sc", [P, T // 4], I32)
+        rdr_table_sc = held("rdr_table_sc", [P, T2 // 4], I32)
         w4_sc = held("w4_sc", [P, 2, N // 4], I32)
         w4_codes = held("w4_codes", [P, 2, 2 * N], U8)
-        fresh_sb = held("fresh_sb", [P, 2, 4], F32)
-        wd_raw = [held("wd_raw%d" % b, [P, 4, N], F32) for b in range(2)]
+        fresh_sb = held("fresh_sb", [P, 2 * PACK], F32)
+        wd_raw = [held("wd_raw%d" % b, [P, PACK, N], F32) for b in range(2)]
         gate_sb = [held("gate_sb%d" % h, [P, 2, HALF], F32) for h in range(2)]
         warm = held("warm", [P, 2], F32)
 
-        nc.gpsimd.memset(art_tab_sc[:], 0)
-        nc.vector.memset(rdr_tab_sc[:], 0)
+        nc.vector.memset(art_table_sc[:], 0)
+        nc.vector.memset(rdr_table_sc[:], 0)
         nc.vector.memset(w4_sc[:], 0)
         nc.vector.memset(warm[:, 0:1], 0.0)
-        nc.scalar.activation(out=warm[:, 1:2], in_=warm[:, 0:1], func=TANH)
 
-        def words(table, a):
+        def table_words(table, a):
             return table[a].rearrange("p t i -> p (t i)").bitcast(I32)
 
-        def scale_rows(queue, tile, row, table):
-            for q in range(4):
-                queue.dma_start(tile[32 * q + row : 32 * q + row + 8, :], table[:, 4 * q : 4 * q + 4, :].bitcast(I32))
-
-        def scale_rows4(queue, tile, rows, table, a):
-            for q in range(4):
-                queue.dma_start(tile[32 * q + rows[a] : 32 * q + rows[a] + 4, :], table[a, 4 * q : 4 * q + 4, :].bitcast(I32))
-
-        def rdr_rows(a, q):
-            row = 32 * q + RDR_ROW[a]
-            nc.sync.dma_start(rdr_tab_sc[row : row + 4, :], tab2_scales[a, 4 * q : 4 * q + 4, :].bitcast(I32))
-
-        rows = [(a, q) for a in range(2) for q in range(4)]
         nc.sync.dma_start(art_list[:], offs)
         nc.sync.dma_start(rdr_list[:], offs2)
-        scale_rows(nc.sync, art_tab_sc, ART_ROW[0], tab_scales)
-        nc.sync.dma_start(art_tab[0][:], words(tab_words, 0))
-        nc.sync.dma_start(art_tab[1][:], words(tab_words, 1))
-        for a, q in rows[:6]:
-            rdr_rows(a, q)
-        nc.sync.dma_start(rdr_tab[0][:], words(tab2_words, 0))
-        for a, q in rows[6:]:
-            rdr_rows(a, q)
-        nc.sync.dma_start(rdr_tab[1][:], words(tab2_words, 1))
-        nc.sync.dma_start(fresh_sb[:], fresh.rearrange("(b p t) -> p b t", b=2, t=4))
-
+        for q in range(QUADRANTS):
+            row = 32 * q + ART_ROW[0]
+            nc.sync.dma_start(art_table_sc[row : row + 8, :], tab_scales[:, 4 * q : 4 * q + 4, :].bitcast(I32))
+        for q, queue in enumerate((nc.sync, nc.sync, nc.gpsimd, nc.gpsimd)):
+            row = 32 * q + RDR_ROW[0]
+            queue.dma_start(rdr_table_sc[row : row + 8, :], tab2_scales[:, 4 * q : 4 * q + 4, :].bitcast(I32))
+        nc.scalar.activation(out=warm[:, 1:2], in_=warm[:, 0:1], func=TANH)
+        for a in range(2):
+            nc.sync.dma_start(art_table[a][:], table_words(tab_words, a))
+        nc.sync.dma_start(
+            fresh_sb[:].rearrange("p (b t) -> p b t", b=2), fresh.rearrange("(b p t) -> p b t", b=2, t=PACK)
+        )
+        for a in range(2):
+            nc.sync.dma_start(rdr_table[a][:], table_words(tab2_words, a))
         for b in range(2):
-            nc.sync.dma_start(wd_raw[b][:], wd[HALF * b : HALF * (b + 1), :].rearrange("(p t) n -> p t n", t=4))
-        nc.sync.dma_start(w4_codes[:].bitcast(I32), w4_words.rearrange("a p c -> p a c").bitcast(I32))
-        for q in range(4):
+            nc.sync.dma_start(wd_raw[b][:], wd[HALF * b : HALF * (b + 1), :].rearrange("(p t) n -> p t n", t=PACK))
+        nc.sync.dma_start(w4_codes[:].bitcast(I32), w4_words.rearrange("b p c -> p b c").bitcast(I32))
+        for q in range(QUADRANTS):
             nc.sync.dma_start(
-                w4_sc[32 * q : 32 * q + 4, :, :], w4_scales[:, 4 * q : 4 * q + 4, :].rearrange("a r c -> r a c").bitcast(I32)
+                w4_sc[32 * q : 32 * q + 4, :, :],
+                w4_scales[:, 4 * q : 4 * q + 4, :].rearrange("b r c -> r b c").bitcast(I32),
             )
         for h in range(2):
             nc.sync.dma_start(gate_sb[h][:], gate[:, HALF * h : HALF * (h + 1)].rearrange("(n p) j -> p n j", p=P))
@@ -102,208 +98,171 @@ def tile_list_fresh_news_sections_kernel(
         art = [[held("art%d%d" % (a, b), [P, HALF], U32) for b in range(2)] for a in range(2)]
         rdr = [[held("rdr%d%d" % (a, h), [P, HALF], U32) for h in range(2)] for a in range(2)]
 
-        def part(lst, c):
-            return lst[:, 32 * c : 32 * (c + 1)]
-
-        def gather_art(a, b):
-            nc.vector.tensor_copy(
-                art[a][b][:].rearrange("p (t m) -> p m t", t=4), art_tab[a][:].bitcast(U32).indirect(part(art_list, b))
-            )
-
-        def gather_rdr(a, h):
-            nc.vector.tensor_copy(rdr[a][h][:], rdr_tab[a][:].bitcast(U32).indirect(part(rdr_list, h)))
-
-        def gather_art_sc():
-            nc.vector.tensor_copy(art_sc_listed[:], art_tab_sc[:].bitcast(U8).indirect(art_list[:]))
-
-        def sort_art_sc():
-            nc.vector.tensor_copy(
-                art_sc[:].rearrange("p (b t m) -> p b t m", b=2, t=4),
-                art_sc_listed[:].rearrange("p (b m t) -> p b t m", b=2, t=4),
-            )
+        def list_half(offsets, half):
+            return offsets[:, 32 * half : 32 * (half + 1)]
 
         def gather_rdr_sc(h):
-            nc.vector.tensor_copy(rdr_sc[h][:], rdr_tab_sc[:].bitcast(U8).indirect(part(rdr_list, h)))
+            nc.vector.tensor_copy(rdr_sc[h][:], rdr_table_sc[:].bitcast(U8).indirect(list_half(rdr_list, h)))
 
-        gather_art_sc()
-        gather_art(0, 0)
-        sort_art_sc()
-        gather_art(0, 1)
-        gather_art(1, 0)
-        gather_art(1, 1)
-        gather_rdr_sc(0)
-        gather_rdr_sc(1)
-        gather_rdr(0, 1)
-        gather_rdr(0, 0)
-        gather_rdr(1, 0)
-        gather_rdr(1, 1)
+        def gather_rdr(a, h):
+            nc.vector.tensor_copy(rdr[a][h][:], rdr_table[a][:].bitcast(U32).indirect(list_half(rdr_list, h)))
 
-        steps = [(0, b, q) for b in range(2) for q in range(2)] + [(1, b, q) for q in range(2) for b in range(2)]
-        units = [(h, b, q, u) for (h, b, q) in steps for u in range(2)]
+        nc.vector.tensor_copy(art_sc_listed[:], art_table_sc[:].bitcast(U8).indirect(art_list[:]))
+        nc.vector.tensor_copy(
+            art_sc[:].rearrange("p (b t m) -> p b t m", b=2, t=PACK),
+            art_sc_listed[:].rearrange("p (b m t) -> p b t m", b=2, t=PACK),
+        )
+        for h in range(2):
+            gather_rdr_sc(h)
+        for a in range(2):
+            for b in range(2):
+                nc.vector.tensor_copy(
+                    art[a][b][:].rearrange("p (t m) -> p m t", t=PACK),
+                    art_table[a][:].bitcast(U32).indirect(list_half(art_list, b)),
+                )
+        for a, h in ((0, 1), (0, 0), (1, 0), (1, 1)):
+            gather_rdr(a, h)
 
-        def match_pass(bank, unit, e, a):
-            h, b, q, u = unit
-            t = 2 * u + e
+        def match_pass(bank, step, t, a):
+            h, b, first, width = step
             nc.tensor.matmul_mx(
-                out=bank[:, e, :],
+                out=bank[:, t % (HALF // width), :],
                 lhsT=art[a][b][:, P * t : P * (t + 1)].bitcast(FP8X4),
                 lhsT_scale=art_sc[ART_ROW[a] :, HALF * b + P * t : HALF * b + P * (t + 1)],
-                rhs=rdr[a][h][:, QUART * q : QUART * (q + 1)].bitcast(FP8X4),
-                rhs_scale=rdr_sc[h][RDR_ROW[a] :, QUART * q : QUART * (q + 1)],
+                rhs=rdr[a][h][:, first : first + width].bitcast(FP8X4),
+                rhs_scale=rdr_sc[h][RDR_ROW[a] :, first : first + width],
                 start=(a == 0),
                 stop=(a == 1),
             )
 
         banks = {}
-        for unit in units[:A_BANKS]:
-            banks[unit] = psum_a.tile([P, 2, QUART], F32, name="a_bank")
-            match_pass(banks[unit], unit, 0, 0)
 
-        wd_bf = [held("wd_bf%d" % b, [P, N, 4], BF16) for b in range(2)]
-        wd_codes = held("wd_codes", [P, 2 * N], U32)
-        wd_sc = held("wd_sc", [P, 2 * N], U8)
+        def open_bank(step, u, pool, tag):
+            side = HALF // step[3]
+            banks[step, u] = pool.tile([P, side, step[3]], F32, name=tag)
+            match_pass(banks[step, u], step, side * u, 0)
+
+        for u in range(2):
+            open_bank(STEPS[0], u, psum_sum, "sum_bank")
+        for step, u in [(step, u) for step in STEPS[1:4] for u in range(2)][:MATCH_BANKS]:
+            open_bank(step, u, psum_match, "match_bank")
+
         z_codes = {(h, b): held("z_codes%d%d" % (h, b), [P, HALF], U32) for h in range(2) for b in range(2)}
         z_sc = {(h, b): held("z_sc%d%d" % (h, b), [P, HALF], U8) for h in range(2) for b in range(2)}
         z_bf = {}
-        y_bank = {}
 
         def match(step):
-            h, b, q = step
-            bounded = ring.tile([P, 2, QUART, 2], F32, name="bounded")
-            for u in range(2):
-                unit = (h, b, q, u)
-                if unit not in banks:
-                    banks[unit] = psum_a.tile([P, 2, QUART], F32, name="a_bank")
-                    match_pass(banks[unit], unit, 0, 0)
-                match_pass(banks[unit], unit, 0, 1)
-                match_pass(banks[unit], unit, 1, 0)
-                match_pass(banks[unit], unit, 1, 1)
-                nc.scalar.activation(out=bounded[:, u, :, :], in_=banks[unit][:].rearrange("p e j -> p j e"), func=TANH)
-            z_bf[step] = ring.tile([P, QUART * 4], BF16, name="z_bf", align_bytes=64)
+            b, width = step[1], step[3]
+            side = HALF // width
+            bounded = ring.tile([P, PACK // side, width, side], F32, name="bounded")
+            for u in range(PACK // side):
+                if (step, u) not in banks:
+                    open_bank(step, u, psum_match, "match_bank")
+                match_pass(banks[step, u], step, side * u, 1)
+                for t in range(side * u + 1, side * (u + 1)):
+                    for a in range(2):
+                        match_pass(banks[step, u], step, t, a)
+                nc.scalar.activation(out=bounded[:, u, :, :], in_=banks[step, u][:].rearrange("p e j -> p j e"), func=TANH)
+            z_bf[step] = ring.tile([P, width * PACK], BF16, name="z_bf", align_bytes=64)
             nc.vector.tensor_tensor(
-                z_bf[step][:].rearrange("p (j u e) -> p j u e", u=2, e=2),
+                z_bf[step][:].rearrange("p (j u e) -> p j u e", u=PACK // side, e=side),
                 bounded[:].rearrange("p u j e -> p j u e"),
-                fresh_sb[:, b, :].rearrange("p (u e) -> p u e", u=2).unsqueeze(1).to_broadcast([P, QUART, 2, 2]),
+                fresh_sb[:, PACK * b : PACK * (b + 1)]
+                .rearrange("p (u e) -> p u e", e=side)
+                .unsqueeze(1)
+                .to_broadcast([P, width, PACK // side, side]),
                 MULT,
             )
 
-        def quantise(step):
-            h, b, q = step
-            cols = slice(QUART * q, QUART * (q + 1))
+        def quantise_z(step):
+            h, b, first, width = step
+            cols = slice(first, first + width)
             nc.vector.quantize_mx(out=z_codes[h, b][:, cols].bitcast(FP8X4), scales=z_sc[h, b][:, cols], in_=z_bf[step][:])
 
-        def sections(h, b):
+        wd_bf = [held("wd_bf%d" % b, [P, N, PACK], BF16) for b in range(2)]
+        wd_codes = [held("wd_codes%d" % b, [P, N], U32) for b in range(2)]
+        wd_sc = [held("wd_sc%d" % b, [P, N], U8) for b in range(2)]
+
+        nc.scalar.copy(out=wd_bf[0][:], in_=wd_raw[0][:].rearrange("p t n -> p n t"))
+        nc.vector.tensor_copy(out=wd_bf[1][:], in_=wd_raw[1][:].rearrange("p t n -> p n t"))
+        for b in range(2):
+            nc.vector.quantize_mx(
+                out=wd_codes[b][:].bitcast(FP8X4), scales=wd_sc[b][:], in_=wd_bf[b][:].rearrange("p n t -> p (n t)")
+            )
+
+        def section_passes(acc, h, b, n, cols):
+            rows = slice(P * n, P * (n + 1))
+            for codes, scales, last in (
+                (w4_codes[:, b, 2 * P * n : 2 * P * (n + 1)].bitcast(FP4X4), w4_sc[:, b, :].bitcast(U8)[:, rows], False),
+                (wd_codes[b][:, rows].bitcast(FP8X4), wd_sc[b][:, rows], True),
+            ):
+                nc.tensor.matmul_mx(
+                    out=acc,
+                    lhsT=codes,
+                    lhsT_scale=scales,
+                    rhs=z_codes[h, b][:, cols].bitcast(FP8X4),
+                    rhs_scale=z_sc[h, b][:, cols],
+                    start=(b == 0 and not last),
+                    stop=(b == 1 and last),
+                )
+
+        sums = {}
+
+        def first_half(b):
             for n in range(2):
                 if b == 0:
-                    y_bank[h, n] = psum_y.tile([P, HALF], F32, name="y_bank")
-                nc.tensor.matmul_mx(
-                    out=y_bank[h, n][:],
-                    lhsT=w4_codes[:, b, 2 * P * n : 2 * P * (n + 1)].bitcast(FP4X4),
-                    lhsT_scale=w4_sc[:, b, :].bitcast(U8)[:, P * n : P * (n + 1)],
-                    rhs=z_codes[h, b][:].bitcast(FP8X4),
-                    rhs_scale=z_sc[h, b][:],
-                    start=(b == 0),
-                    stop=False,
-                )
-                cols = slice(N * b + P * n, N * b + P * (n + 1))
-                nc.tensor.matmul_mx(
-                    out=y_bank[h, n][:],
-                    lhsT=wd_codes[:, cols].bitcast(FP8X4),
-                    lhsT_scale=wd_sc[:, cols],
-                    rhs=z_codes[h, b][:].bitcast(FP8X4),
-                    rhs_scale=z_sc[h, b][:],
-                    start=False,
-                    stop=(b == 1),
-                )
+                    sums["half", n] = psum_sum.tile([P, HALF], F32, name="sum_bank")
+                section_passes(sums["half", n][:], 0, b, n, slice(0, HALF))
 
-        def finish(h):
+        def store_first_half():
             for n in range(2):
-                res = ring.tile([P, HALF], F32, name="res")
-                nc.vector.tensor_tensor(res[:], y_bank[h, n][:], gate_sb[h][:, n, :], MULT)
-                nc.sync.dma_start(out[P * n : P * (n + 1), HALF * h : HALF * (h + 1)], res[:])
-
-        def narrow_passes(dst, b, n, col):
-            cols = slice(col, col + P)
-            nc.tensor.matmul_mx(
-                out=dst,
-                lhsT=w4_codes[:, b, 2 * P * n : 2 * P * (n + 1)].bitcast(FP4X4),
-                lhsT_scale=w4_sc[:, b, :].bitcast(U8)[:, P * n : P * (n + 1)],
-                rhs=z_codes[1, b][:, cols].bitcast(FP8X4),
-                rhs_scale=z_sc[1, b][:, cols],
-                start=(b == 0),
-                stop=False,
-            )
-            wcols = slice(N * b + P * n, N * b + P * (n + 1))
-            nc.tensor.matmul_mx(
-                out=dst,
-                lhsT=wd_codes[:, wcols].bitcast(FP8X4),
-                lhsT_scale=wd_sc[:, wcols],
-                rhs=z_codes[1, b][:, cols].bitcast(FP8X4),
-                rhs_scale=z_sc[1, b][:, cols],
-                start=False,
-                stop=(b == 1),
-            )
+                scores = ring.tile([P, HALF], F32, name="scores")
+                nc.vector.tensor_tensor(scores[:], sums["half", n][:], gate_sb[0][:, n, :], MULT)
+                nc.sync.dma_start(out[P * n : P * (n + 1), 0:HALF], scores[:])
 
         def third_quarter():
             for n in range(2):
-                bank = psum_y.tile([P, 2, P], F32, name="y_bank")
+                sums["third", n] = psum_sum.tile([P, QUARTER], F32, name="sum_bank")
                 for c in range(2):
                     for b in range(2):
-                        narrow_passes(bank[:, c, :], b, n, P * c)
-                y_bank["third", n] = bank
+                        section_passes(sums["third", n][:, P * c : P * (c + 1)], 1, b, n, slice(P * c, P * (c + 1)))
 
-        def finish_third():
-            res = ring.tile([P, 2, QUART], F32, name="res")
+        def store_third_quarter(n):
+            scores = ring.tile([P, QUARTER], F32, name="scores")
+            nc.vector.tensor_tensor(scores[:], sums["third", n][:], gate_sb[1][:, n, 0:QUARTER], MULT)
+            nc.sync.dma_start(out[P * n : P * (n + 1), HALF : HALF + QUARTER], scores[:])
+
+        def last_eighth(c, b):
             for n in range(2):
-                nc.vector.tensor_tensor(
-                    res[:, n, :], y_bank["third", n][:].rearrange("p c j -> p (c j)"), gate_sb[1][:, n, 0:QUART], MULT
-                )
-            nc.sync.dma_start(out[:, HALF : HALF + QUART].rearrange("(n p) j -> p n j", p=P), res[:])
+                if b == 0:
+                    sums["last", c, n] = psum_match.tile([P, P], F32, name="match_bank")
+                section_passes(sums["last", c, n][:], 1, b, n, slice(QUARTER + P * c, QUARTER + P * (c + 1)))
 
-        def last_quarter(b):
+        def store_last_eighth(c):
+            first = QUARTER + P * c
+            scores = ring.tile([P, 2, P], F32, name="scores")
             for n in range(2):
-                for c in range(2):
-                    if b == 0:
-                        y_bank["last", n, c] = psum_a.tile([P, P], F32, name="a_bank")
-                    narrow_passes(y_bank["last", n, c][:], b, n, QUART + P * c)
-
-        def finish_last():
-            for n in range(2):
-                res = ring.tile([P, QUART], F32, name="res")
-                for c in range(2):
-                    nc.vector.tensor_tensor(
-                        res[:, P * c : P * (c + 1)],
-                        y_bank["last", n, c][:],
-                        gate_sb[1][:, n, QUART + P * c : QUART + P * (c + 1)],
-                        MULT,
-                    )
-                (nc.sync, nc.scalar)[n].dma_start(out[P * n : P * (n + 1), HALF + QUART :], res[:])
-
-        def quantise_wd(b):
-            cols = slice(N * b, N * (b + 1))
-            nc.vector.quantize_mx(
-                out=wd_codes[:, cols].bitcast(FP8X4), scales=wd_sc[:, cols], in_=wd_bf[b][:].rearrange("p n t -> p (n t)")
+                nc.vector.tensor_tensor(scores[:, n, :], sums["last", c, n][:], gate_sb[1][:, n, first : first + P], MULT)
+            nc.scalar.dma_start(
+                out[:, HALF + first : HALF + first + P].rearrange("(n p) j -> p n j", p=P), scores[:]
             )
 
-
-        for s, step in enumerate(steps):
+        behind_step = {
+            3: [lambda: first_half(0)],
+            5: [lambda: first_half(1)],
+            6: [store_first_half],
+            7: [third_quarter],
+            8: [lambda: last_eighth(0, 0), lambda: last_eighth(1, 0), lambda: last_eighth(0, 1)],
+        }
+        for s, step in enumerate(STEPS):
             match(step)
             if s > 0:
-                quantise(steps[s - 1])
-            if s in (1, 2):
-                nc.scalar.copy(out=wd_bf[s - 1][:], in_=wd_raw[s - 1][:].rearrange("p t n -> p n t"))
-            if s in (2, 3):
-                quantise_wd(s - 2)
-            if s == 3:
-                sections(0, 0)
-            if s == 5:
-                sections(0, 1)
-            if s == 6:
-                finish(0)
-            if s == 7:
-                third_quarter()
-                last_quarter(0)
-        quantise(steps[-1])
-        finish_third()
-        last_quarter(1)
-        finish_last()
+                quantise_z(STEPS[s - 1])
+            for work in behind_step.get(s, []):
+                work()
+        store_third_quarter(0)
+        quantise_z(STEPS[-1])
+        last_eighth(1, 1)
+        store_third_quarter(1)
+        for c in range(2):
+            store_last_eighth(c)

@@ -15,6 +15,7 @@ FP8X4 = mybir.dt.float8_e4m3fn_x4
 FP4X4 = mybir.dt.float4_e2m1fn_x4
 MULT = mybir.AluOpType.mult
 TANH = mybir.ActivationFunctionType.Tanh
+COPY = mybir.ActivationFunctionType.Copy
 
 P = 128
 PACK = 4
@@ -29,6 +30,7 @@ STEPS = (
     + [(1, 0, 0, QUARTER), (1, 1, 0, QUARTER), (1, 0, QUARTER, QUARTER)]
     + [(1, 1, QUARTER, P), (1, 1, QUARTER + P, P)]
 )
+SCALAR_STEPS = [STEPS[s] for s in (5, 6)]
 
 
 def tile_list_fresh_news_sections_kernel(
@@ -38,6 +40,7 @@ def tile_list_fresh_news_sections_kernel(
     with ExitStack() as ctx:
         keep = ctx.enter_context(tc.tile_pool(name="keep", bufs=1))
         ring = ctx.enter_context(tc.tile_pool(name="ring", bufs=4))
+        results = ctx.enter_context(tc.tile_pool(name="results", bufs=8))
         psum_match = ctx.enter_context(tc.psum_pool(name="psum_match", bufs=MATCH_BANKS))
         psum_sum = ctx.enter_context(tc.psum_pool(name="psum_sum", bufs=2))
 
@@ -70,19 +73,19 @@ def tile_list_fresh_news_sections_kernel(
         for q in range(QUADRANTS):
             row = 32 * q + ART_ROW[0]
             nc.sync.dma_start(art_table_sc[row : row + 8, :], tab_scales[:, 4 * q : 4 * q + 4, :].bitcast(I32))
-        for q, queue in enumerate((nc.sync, nc.sync, nc.gpsimd, nc.gpsimd)):
-            row = 32 * q + RDR_ROW[0]
-            queue.dma_start(rdr_table_sc[row : row + 8, :], tab2_scales[:, 4 * q : 4 * q + 4, :].bitcast(I32))
+        for r in range(4):
+            for a in range(2):
+                nc.sync.dma_start(rdr_table_sc[RDR_ROW[a] + r : P : 32, :], tab2_scales[a, r:16:4, :].bitcast(I32))
         nc.scalar.activation(out=warm[:, 1:2], in_=warm[:, 0:1], func=TANH)
         for a in range(2):
             nc.sync.dma_start(art_table[a][:], table_words(tab_words, a))
-        nc.sync.dma_start(
-            fresh_sb[:].rearrange("p (b t) -> p b t", b=2), fresh.rearrange("(b p t) -> p b t", b=2, t=PACK)
-        )
         for a in range(2):
             nc.sync.dma_start(rdr_table[a][:], table_words(tab2_words, a))
         for b in range(2):
             nc.sync.dma_start(wd_raw[b][:], wd[HALF * b : HALF * (b + 1), :].rearrange("(p t) n -> p t n", t=PACK))
+        nc.sync.dma_start(
+            fresh_sb[:].rearrange("p (b t) -> p b t", b=2), fresh.rearrange("(b p t) -> p b t", b=2, t=PACK)
+        )
         nc.sync.dma_start(w4_codes[:].bitcast(I32), w4_words.rearrange("b p c -> p b c").bitcast(I32))
         for q in range(QUADRANTS):
             nc.sync.dma_start(
@@ -151,10 +154,16 @@ def tile_list_fresh_news_sections_kernel(
         z_sc = {(h, b): held("z_sc%d%d" % (h, b), [P, HALF], U8) for h in range(2) for b in range(2)}
         z_bf = {}
 
+        def interleave(columns, rows):
+            nc.vector.tensor_copy(
+                out=columns.rearrange("p (g i) t -> p g t i", i=4), in_=rows.rearrange("p t (g i) -> p g t i", i=4)
+            )
+
         def match(step):
             b, width = step[1], step[3]
             side = HALF // width
-            bounded = ring.tile([P, PACK // side, width, side], F32, name="bounded")
+            on_scalar = step in SCALAR_STEPS
+            bounded = ring.tile([P, PACK // side, HALF], F32, name="bounded")
             for u in range(PACK // side):
                 if (step, u) not in banks:
                     open_bank(step, u, psum_match, "match_bank")
@@ -162,17 +171,32 @@ def tile_list_fresh_news_sections_kernel(
                 for t in range(side * u + 1, side * (u + 1)):
                     for a in range(2):
                         match_pass(banks[step, u], step, t, a)
-                nc.scalar.activation(out=bounded[:, u, :, :], in_=banks[step, u][:].rearrange("p e j -> p j e"), func=TANH)
+                order = "p e j -> p e j" if on_scalar else "p e j -> p j e"
+                products = banks[step, u][:].rearrange(order)
+                nc.scalar.activation(
+                    out=bounded[:, u, :].rearrange("p (x y) -> p x y", y=products.shape[2]), in_=products, func=TANH
+                )
             z_bf[step] = ring.tile([P, width * PACK], BF16, name="z_bf", align_bytes=64)
-            nc.vector.tensor_tensor(
-                z_bf[step][:].rearrange("p (j u e) -> p j u e", u=PACK // side, e=side),
-                bounded[:].rearrange("p u j e -> p j u e"),
-                fresh_sb[:, PACK * b : PACK * (b + 1)]
-                .rearrange("p (u e) -> p u e", e=side)
-                .unsqueeze(1)
-                .to_broadcast([P, width, PACK // side, side]),
-                MULT,
-            )
+            if on_scalar:
+                z_rows = ring.tile([P, PACK, width], BF16, name="z_rows")
+                for t in range(PACK):
+                    nc.scalar.activation(
+                        out=z_rows[:, t, :],
+                        in_=bounded[:, t // side, width * (t % side) : width * (t % side + 1)],
+                        func=COPY,
+                        scale=fresh_sb[:, PACK * b + t : PACK * b + t + 1],
+                    )
+                interleave(z_bf[step][:].rearrange("p (j t) -> p j t", t=PACK), z_rows[:])
+            else:
+                nc.vector.tensor_tensor(
+                    z_bf[step][:].rearrange("p (j u e) -> p j u e", u=PACK // side, e=side),
+                    bounded[:].rearrange("p u (j e) -> p j u e", e=side),
+                    fresh_sb[:, PACK * b : PACK * (b + 1)]
+                    .rearrange("p (u e) -> p u e", e=side)
+                    .unsqueeze(1)
+                    .to_broadcast([P, width, PACK // side, side]),
+                    MULT,
+                )
 
         def quantise_z(step):
             h, b, first, width = step
@@ -184,7 +208,7 @@ def tile_list_fresh_news_sections_kernel(
         wd_sc = [held("wd_sc%d" % b, [P, N], U8) for b in range(2)]
 
         nc.scalar.copy(out=wd_bf[0][:], in_=wd_raw[0][:].rearrange("p t n -> p n t"))
-        nc.vector.tensor_copy(out=wd_bf[1][:], in_=wd_raw[1][:].rearrange("p t n -> p n t"))
+        interleave(wd_bf[1][:], wd_raw[1][:])
         for b in range(2):
             nc.vector.quantize_mx(
                 out=wd_codes[b][:].bitcast(FP8X4), scales=wd_sc[b][:], in_=wd_bf[b][:].rearrange("p n t -> p (n t)")
@@ -216,7 +240,7 @@ def tile_list_fresh_news_sections_kernel(
 
         def store_first_half():
             for n in range(2):
-                scores = ring.tile([P, HALF], F32, name="scores")
+                scores = results.tile([P, HALF], F32, name="scores")
                 nc.vector.tensor_tensor(scores[:], sums["half", n][:], gate_sb[0][:, n, :], MULT)
                 nc.sync.dma_start(out[P * n : P * (n + 1), 0:HALF], scores[:])
 
@@ -228,7 +252,7 @@ def tile_list_fresh_news_sections_kernel(
                         section_passes(sums["third", n][:, P * c : P * (c + 1)], 1, b, n, slice(P * c, P * (c + 1)))
 
         def store_third_quarter(n):
-            scores = ring.tile([P, QUARTER], F32, name="scores")
+            scores = results.tile([P, QUARTER], F32, name="scores")
             nc.vector.tensor_tensor(scores[:], sums["third", n][:], gate_sb[1][:, n, 0:QUARTER], MULT)
             nc.sync.dma_start(out[P * n : P * (n + 1), HALF : HALF + QUARTER], scores[:])
 
@@ -240,12 +264,10 @@ def tile_list_fresh_news_sections_kernel(
 
         def store_last_eighth(c):
             first = QUARTER + P * c
-            scores = ring.tile([P, 2, P], F32, name="scores")
-            for n in range(2):
-                nc.vector.tensor_tensor(scores[:, n, :], sums["last", c, n][:], gate_sb[1][:, n, first : first + P], MULT)
-            nc.scalar.dma_start(
-                out[:, HALF + first : HALF + first + P].rearrange("(n p) j -> p n j", p=P), scores[:]
-            )
+            for n, queue in enumerate((nc.sync, nc.scalar)):
+                scores = results.tile([P, P], F32, name="scores")
+                nc.vector.tensor_tensor(scores[:], sums["last", c, n][:], gate_sb[1][:, n, first : first + P], MULT)
+                queue.dma_start(out[P * n : P * (n + 1), HALF + first : HALF + first + P], scores[:])
 
         behind_step = {
             3: [lambda: first_half(0)],

@@ -23,14 +23,14 @@ HALF = 512
 QUARTER = 256
 QUADRANTS = 4
 MATCH_BANKS = 6
-ART_ROW = (0, 4)
-RDR_ROW = (8, 12)
+SC_FIRST = 96
+PLANE_ROW = (12, 0)
 STEPS = (
     [(0, b, first, QUARTER) for b in range(2) for first in (0, QUARTER)]
     + [(1, 0, 0, QUARTER), (1, 1, 0, QUARTER), (1, 0, QUARTER, QUARTER)]
     + [(1, 1, QUARTER, P), (1, 1, QUARTER + P, P)]
 )
-SCALAR_STEPS = [STEPS[s] for s in (5, 6)]
+SCALAR_STEPS = [STEPS[s] for s in (2, 5)]
 
 
 def tile_list_fresh_news_sections_kernel(
@@ -51,41 +51,80 @@ def tile_list_fresh_news_sections_kernel(
         rdr_list = keep.tile([P, S2 // 16], U16, name="rdr_list")
         art_table = [held("art_table%d" % a, [P, T], I32) for a in range(2)]
         rdr_table = [held("rdr_table%d" % a, [P, T2], I32) for a in range(2)]
-        art_table_sc = held("art_table_sc", [P, T // 4], I32)
-        rdr_table_sc = held("rdr_table_sc", [P, T2 // 4], I32)
         w4_sc = held("w4_sc", [P, 2, N // 4], I32)
         w4_codes = held("w4_codes", [P, 2, 2 * N], U8)
-        fresh_sb = held("fresh_sb", [P, 2 * PACK], F32)
         wd_raw = [held("wd_raw%d" % b, [P, PACK, N], F32) for b in range(2)]
         gate_sb = [held("gate_sb%d" % h, [P, 2, HALF], F32) for h in range(2)]
+        art_table_sc = held("art_table_sc", [P, T // 4], I32)
+        rdr_table_sc = held("rdr_table_sc", [P, T2 // 4], I32)
+        plane1 = held("plane1", [P, (S + S2) // 4], I32)
+        fresh_sb = held("fresh_sb", [P, 2 * PACK], F32)
         warm = held("warm", [P, 2], F32)
 
-        nc.vector.memset(art_table_sc[:], 0)
-        nc.vector.memset(rdr_table_sc[:], 0)
-        nc.vector.memset(w4_sc[:], 0)
         nc.vector.memset(warm[:, 0:1], 0.0)
+        nc.vector.memset(art_table_sc[0:SC_FIRST, :], 0)
+        nc.vector.memset(rdr_table_sc[0:SC_FIRST, :], 0)
+        nc.vector.memset(plane1[:], 0)
+        nc.vector.memset(w4_sc[:], 0)
 
         def table_words(table, a):
             return table[a].rearrange("p t i -> p (t i)").bitcast(I32)
 
         nc.sync.dma_start(art_list[:], offs)
+        nc.sync.dma_start(art_table_sc[SC_FIRST:P, :], tab_scales.rearrange("a q t -> (a q) t").bitcast(I32))
         nc.sync.dma_start(rdr_list[:], offs2)
-        for q in range(QUADRANTS):
-            row = 32 * q + ART_ROW[0]
-            nc.sync.dma_start(art_table_sc[row : row + 8, :], tab_scales[:, 4 * q : 4 * q + 4, :].bitcast(I32))
-        for r in range(4):
-            for a in range(2):
-                nc.sync.dma_start(rdr_table_sc[RDR_ROW[a] + r : P : 32, :], tab2_scales[a, r:16:4, :].bitcast(I32))
-        nc.scalar.activation(out=warm[:, 1:2], in_=warm[:, 0:1], func=TANH)
-        for a in range(2):
-            nc.sync.dma_start(art_table[a][:], table_words(tab_words, a))
-        for a in range(2):
-            nc.sync.dma_start(rdr_table[a][:], table_words(tab2_words, a))
-        for b in range(2):
-            nc.sync.dma_start(wd_raw[b][:], wd[HALF * b : HALF * (b + 1), :].rearrange("(p t) n -> p t n", t=PACK))
+        nc.sync.dma_start(rdr_table_sc[SC_FIRST:P, :], tab2_scales.rearrange("a q t -> (a q) t").bitcast(I32))
         nc.sync.dma_start(
             fresh_sb[:].rearrange("p (b t) -> p b t", b=2), fresh.rearrange("(b p t) -> p b t", b=2, t=PACK)
         )
+        nc.scalar.activation(out=warm[:, 1:2], in_=warm[:, 0:1], func=TANH)
+        nc.sync.dma_start(rdr_table[0][:], table_words(tab2_words, 0))
+        for a in range(2):
+            nc.sync.dma_start(art_table[a][:], table_words(tab_words, a))
+        nc.sync.dma_start(rdr_table[1][:, 0:T], table_words(tab2_words, 1)[:, 0:T])
+
+        art_sc_listed = held("art_sc_listed", [P, S], U8)
+        rdr_sc_listed = held("rdr_sc_listed", [P, S2], U8)
+        plane0 = held("plane0", [P, (S + S2) // 4], I32)
+        art = [[held("art%d%d" % (a, b), [P, HALF], U32) for b in range(2)] for a in range(2)]
+        rdr = [[held("rdr%d%d" % (a, h), [P, HALF], U32) for h in range(2)] for a in range(2)]
+
+        def list_half(offsets, half):
+            return offsets[:, 32 * half : 32 * (half + 1)]
+
+        def gather_rdr(a, h):
+            nc.vector.tensor_copy(rdr[a][h][:], rdr_table[a][:].bitcast(U32).indirect(list_half(rdr_list, h)))
+
+        def gather_art(a, b):
+            nc.vector.tensor_copy(
+                art[a][b][:].rearrange("p (t m) -> p m t", t=PACK),
+                art_table[a][:].bitcast(U32).indirect(list_half(art_list, b)),
+            )
+
+        nc.vector.tensor_copy(art_sc_listed[:], art_table_sc[:].bitcast(U8).indirect(art_list[:]))
+        nc.vector.tensor_copy(rdr_sc_listed[:], rdr_table_sc[:].bitcast(U8).indirect(rdr_list[:]))
+        nc.vector.tensor_copy(
+            plane0[:].bitcast(U8)[:, 0:S].rearrange("p (b t m) -> p b t m", b=2, t=PACK),
+            art_sc_listed[:].rearrange("p (b m t) -> p b t m", b=2, t=PACK),
+        )
+        nc.vector.tensor_copy(plane0[:, S // 4 :], rdr_sc_listed[:].bitcast(I32))
+        for q in range(QUADRANTS - 1):
+            row = 32 * q + PLANE_ROW[0]
+            nc.sync.dma_start(plane0[row : row + 4, :], plane0[SC_FIRST + 4 * q : SC_FIRST + 4 * q + 4, :])
+        nc.sync.dma_start(rdr_table[1][:, T:T2], table_words(tab2_words, 1)[:, T:T2])
+        for r in range(4):
+            nc.sync.dma_start(plane1[r:P:32, :], plane0[SC_FIRST + 16 + r : P : 4, :])
+        planes = [plane0[:].bitcast(U8), plane1[:].bitcast(U8)]
+
+        gather_rdr(0, 0)
+        gather_art(0, 0)
+        gather_art(0, 1)
+        gather_rdr(0, 1)
+        gather_art(1, 0)
+        gather_art(1, 1)
+
+        for b in range(2):
+            nc.sync.dma_start(wd_raw[b][:], wd[HALF * b : HALF * (b + 1), :].rearrange("(p t) n -> p t n", t=PACK))
         nc.sync.dma_start(w4_codes[:].bitcast(I32), w4_words.rearrange("b p c -> p b c").bitcast(I32))
         for q in range(QUADRANTS):
             nc.sync.dma_start(
@@ -95,47 +134,19 @@ def tile_list_fresh_news_sections_kernel(
         for h in range(2):
             nc.sync.dma_start(gate_sb[h][:], gate[:, HALF * h : HALF * (h + 1)].rearrange("(n p) j -> p n j", p=P))
 
-        art_sc_listed = held("art_sc_listed", [P, S], U8)
-        art_sc = held("art_sc", [P, S], U8)
-        rdr_sc = [held("rdr_sc%d" % h, [P, HALF], U8) for h in range(2)]
-        art = [[held("art%d%d" % (a, b), [P, HALF], U32) for b in range(2)] for a in range(2)]
-        rdr = [[held("rdr%d%d" % (a, h), [P, HALF], U32) for h in range(2)] for a in range(2)]
-
-        def list_half(offsets, half):
-            return offsets[:, 32 * half : 32 * (half + 1)]
-
-        def gather_rdr_sc(h):
-            nc.vector.tensor_copy(rdr_sc[h][:], rdr_table_sc[:].bitcast(U8).indirect(list_half(rdr_list, h)))
-
-        def gather_rdr(a, h):
-            nc.vector.tensor_copy(rdr[a][h][:], rdr_table[a][:].bitcast(U32).indirect(list_half(rdr_list, h)))
-
-        nc.vector.tensor_copy(art_sc_listed[:], art_table_sc[:].bitcast(U8).indirect(art_list[:]))
-        nc.vector.tensor_copy(
-            art_sc[:].rearrange("p (b t m) -> p b t m", b=2, t=PACK),
-            art_sc_listed[:].rearrange("p (b m t) -> p b t m", b=2, t=PACK),
-        )
-        for h in range(2):
-            gather_rdr_sc(h)
-        for a in range(2):
-            for b in range(2):
-                nc.vector.tensor_copy(
-                    art[a][b][:].rearrange("p (t m) -> p m t", t=PACK),
-                    art_table[a][:].bitcast(U32).indirect(list_half(art_list, b)),
-                )
-        for a, h in ((0, 1), (0, 0), (1, 0), (1, 1)):
-            gather_rdr(a, h)
+        gather_rdr(1, 0)
+        gather_rdr(1, 1)
 
         def match_pass(bank, step, t, a):
             h, b, first, width = step
             nc.tensor.matmul_mx(
                 out=bank[:, t % (HALF // width), :],
                 lhsT=art[a][b][:, P * t : P * (t + 1)].bitcast(FP8X4),
-                lhsT_scale=art_sc[ART_ROW[a] :, HALF * b + P * t : HALF * b + P * (t + 1)],
+                lhsT_scale=planes[a][PLANE_ROW[a] :, HALF * b + P * t : HALF * b + P * (t + 1)],
                 rhs=rdr[a][h][:, first : first + width].bitcast(FP8X4),
-                rhs_scale=rdr_sc[h][RDR_ROW[a] :, first : first + width],
-                start=(a == 0),
-                stop=(a == 1),
+                rhs_scale=planes[a][PLANE_ROW[a] :, S + HALF * h + first : S + HALF * h + first + width],
+                start=(a == 0 and t % (HALF // width) == 0),
+                stop=(a == 1 and (t + 1) % (HALF // width) == 0),
             )
 
         banks = {}
@@ -143,7 +154,8 @@ def tile_list_fresh_news_sections_kernel(
         def open_bank(step, u, pool, tag):
             side = HALF // step[3]
             banks[step, u] = pool.tile([P, side, step[3]], F32, name=tag)
-            match_pass(banks[step, u], step, side * u, 0)
+            for t in range(side * u, side * (u + 1)):
+                match_pass(banks[step, u], step, t, 0)
 
         for u in range(2):
             open_bank(STEPS[0], u, psum_sum, "sum_bank")
@@ -167,10 +179,8 @@ def tile_list_fresh_news_sections_kernel(
             for u in range(PACK // side):
                 if (step, u) not in banks:
                     open_bank(step, u, psum_match, "match_bank")
-                match_pass(banks[step, u], step, side * u, 1)
-                for t in range(side * u + 1, side * (u + 1)):
-                    for a in range(2):
-                        match_pass(banks[step, u], step, t, a)
+                for t in range(side * u, side * (u + 1)):
+                    match_pass(banks[step, u], step, t, 1)
                 order = "p e j -> p e j" if on_scalar else "p e j -> p j e"
                 products = banks[step, u][:].rearrange(order)
                 nc.scalar.activation(
@@ -203,13 +213,15 @@ def tile_list_fresh_news_sections_kernel(
             cols = slice(first, first + width)
             nc.vector.quantize_mx(out=z_codes[h, b][:, cols].bitcast(FP8X4), scales=z_sc[h, b][:, cols], in_=z_bf[step][:])
 
-        wd_bf = [held("wd_bf%d" % b, [P, N, PACK], BF16) for b in range(2)]
         wd_codes = [held("wd_codes%d" % b, [P, N], U32) for b in range(2)]
         wd_sc = [held("wd_sc%d" % b, [P, N], U8) for b in range(2)]
+        wd_bf = {}
 
-        nc.scalar.copy(out=wd_bf[0][:], in_=wd_raw[0][:].rearrange("p t n -> p n t"))
-        interleave(wd_bf[1][:], wd_raw[1][:])
-        for b in range(2):
+        def cast_wd(b):
+            wd_bf[b] = held("wd_bf%d" % b, [P, N, PACK], BF16)
+            interleave(wd_bf[b][:], wd_raw[b][:])
+
+        def quantise_wd(b):
             nc.vector.quantize_mx(
                 out=wd_codes[b][:].bitcast(FP8X4), scales=wd_sc[b][:], in_=wd_bf[b][:].rearrange("p n t -> p (n t)")
             )
@@ -270,12 +282,15 @@ def tile_list_fresh_news_sections_kernel(
                 queue.dma_start(out[P * n : P * (n + 1), HALF + first : HALF + first + P], scores[:])
 
         behind_step = {
-            3: [lambda: first_half(0)],
-            5: [lambda: first_half(1)],
-            6: [store_first_half],
+            0: [lambda: cast_wd(1), lambda: quantise_wd(0)],
+            1: [lambda: quantise_wd(1)],
+            2: [lambda: first_half(0)],
+            4: [lambda: first_half(1)],
+            5: [store_first_half],
             7: [third_quarter],
             8: [lambda: last_eighth(0, 0), lambda: last_eighth(1, 0), lambda: last_eighth(0, 1)],
         }
+        cast_wd(0)
         for s, step in enumerate(STEPS):
             match(step)
             if s > 0:

@@ -1,6 +1,7 @@
 from contextlib import ExitStack
 
 import concourse.mybir as mybir
+from concourse.masks import make_identity
 
 K, T, S, T2, S2, N = 1024, 2048, 1024, 4096, 1024, 256
 FLOPS = 2 * K * S * S2 + 2 * 2 * S * N * S2
@@ -22,7 +23,7 @@ PACK = 4
 HALF = 512
 QUARTER = 256
 QUADRANTS = 4
-MATCH_BANKS = 6
+MATCH_BANKS = 5
 SC_FIRST = 96
 PLANE_ROW = (12, 0)
 STEPS = (
@@ -30,7 +31,8 @@ STEPS = (
     + [(1, 0, 0, QUARTER), (1, 1, 0, QUARTER), (1, 0, QUARTER, QUARTER)]
     + [(1, 1, QUARTER, P), (1, 1, QUARTER + P, P)]
 )
-SCALAR_STEPS = [STEPS[s] for s in (2, 5)]
+SCALAR_STEPS = []
+GPSIMD_SHARE = 4
 
 
 def tile_list_fresh_news_sections_kernel(
@@ -42,6 +44,8 @@ def tile_list_fresh_news_sections_kernel(
         ring = ctx.enter_context(tc.tile_pool(name="ring", bufs=4))
         results = ctx.enter_context(tc.tile_pool(name="results", bufs=8))
         psum_match = ctx.enter_context(tc.psum_pool(name="psum_match", bufs=MATCH_BANKS))
+        psum_fresh = ctx.enter_context(tc.psum_pool(name="psum_fresh", bufs=1))
+        pair = ctx.enter_context(tc.tile_pool(name="pair", bufs=2))
         psum_sum = ctx.enter_context(tc.psum_pool(name="psum_sum", bufs=2))
 
         def held(name, shape, dtype):
@@ -74,9 +78,15 @@ def tile_list_fresh_news_sections_kernel(
         nc.sync.dma_start(art_table_sc[SC_FIRST:P, :], tab_scales.rearrange("a q t -> (a q) t").bitcast(I32))
         nc.sync.dma_start(rdr_list[:], offs2)
         nc.sync.dma_start(rdr_table_sc[SC_FIRST:P, :], tab2_scales.rearrange("a q t -> (a q) t").bitcast(I32))
-        nc.sync.dma_start(
-            fresh_sb[:].rearrange("p (b t) -> p b t", b=2), fresh.rearrange("(b p t) -> p b t", b=2, t=PACK)
-        )
+        fresh_rows = held("fresh_rows", [P, HALF], F32)
+        identity = held("identity", [P, P], F32)
+        nc.gpsimd.memset(fresh_rows[:], 0.0)
+        make_identity(nc, identity[:])
+        nc.sync.dma_start(fresh_rows[0:2, :], fresh.rearrange("(b i) -> b i", b=2))
+        fresh_ps = psum_fresh.tile([P, P, PACK], F32, name="fresh_ps")
+        for t in range(PACK):
+            nc.tensor.transpose(fresh_ps[:, :, t], fresh_rows[:, t:HALF:PACK], identity[:])
+        nc.scalar.copy(out=fresh_sb[:].rearrange("p (b t) -> p b t", b=2), in_=fresh_ps[:, 0:2, :])
         nc.scalar.activation(out=warm[:, 1:2], in_=warm[:, 0:1], func=TANH)
         nc.sync.dma_start(rdr_table[0][:], table_words(tab2_words, 0))
         for a in range(2):
@@ -186,7 +196,7 @@ def tile_list_fresh_news_sections_kernel(
                 nc.scalar.activation(
                     out=bounded[:, u, :].rearrange("p (x y) -> p x y", y=products.shape[2]), in_=products, func=TANH
                 )
-            z_bf[step] = ring.tile([P, width * PACK], BF16, name="z_bf", align_bytes=64)
+            z_bf[step] = pair.tile([P, width * PACK], BF16, name="z_bf", align_bytes=64)
             if on_scalar:
                 z_rows = ring.tile([P, PACK, width], BF16, name="z_rows")
                 for t in range(PACK):
@@ -198,15 +208,19 @@ def tile_list_fresh_news_sections_kernel(
                     )
                 interleave(z_bf[step][:].rearrange("p (j t) -> p j t", t=PACK), z_rows[:])
             else:
-                nc.vector.tensor_tensor(
-                    z_bf[step][:].rearrange("p (j u e) -> p j u e", u=PACK // side, e=side),
-                    bounded[:].rearrange("p u (j e) -> p j u e", e=side),
-                    fresh_sb[:, PACK * b : PACK * (b + 1)]
-                    .rearrange("p (u e) -> p u e", e=side)
-                    .unsqueeze(1)
-                    .to_broadcast([P, width, PACK // side, side]),
-                    MULT,
-                )
+                split = width - width // GPSIMD_SHARE
+                for engine, cols, factors in (
+                    (nc.vector, slice(0, split), fresh_ps[:, b, :]),
+                    (nc.gpsimd, slice(split, width), fresh_sb[:, PACK * b : PACK * (b + 1)]),
+                ):
+                    engine.tensor_tensor(
+                        z_bf[step][:].rearrange("p (j u e) -> p j u e", u=PACK // side, e=side)[:, cols],
+                        bounded[:].rearrange("p u (j e) -> p j u e", e=side)[:, cols],
+                        factors.rearrange("p (u e) -> p u e", e=side)
+                        .unsqueeze(1)
+                        .to_broadcast([P, cols.stop - cols.start, PACK // side, side]),
+                        MULT,
+                    )
 
         def quantise_z(step):
             h, b, first, width = step

@@ -23,16 +23,24 @@ PACK = 4
 HALF = 512
 QUARTER = 256
 QUADRANTS = 4
-MATCH_BANKS = 5
+MATCH_BANKS = 7
 SC_FIRST = 96
 PLANE_ROW = (12, 0)
-STEPS = (
-    [(0, b, first, QUARTER) for b in range(2) for first in (0, QUARTER)]
-    + [(1, 0, 0, QUARTER), (1, 1, 0, QUARTER), (1, 0, QUARTER, QUARTER)]
-    + [(1, 1, QUARTER, P), (1, 1, QUARTER + P, P)]
-)
-SCALAR_STEPS = []
-GPSIMD_SHARE = 4
+STEPS = [
+    (0, 0, 0, QUARTER, 64),
+    (0, 0, QUARTER, QUARTER, 64),
+    (0, 1, 0, QUARTER, 64),
+    (0, 1, QUARTER, QUARTER, 64),
+    (1, 0, 0, QUARTER, 64),
+    (1, 1, 0, QUARTER, 64),
+    (1, 0, QUARTER, QUARTER, 144),
+    (1, 1, QUARTER, P, 32),
+    (1, 1, QUARTER + P, P, 32),
+]
+
+
+SCALAR_STEPS = (7, 8)
+HELD_STEP = 5
 
 
 def tile_list_fresh_news_sections_kernel(
@@ -41,12 +49,11 @@ def tile_list_fresh_news_sections_kernel(
     nc = tc.nc
     with ExitStack() as ctx:
         keep = ctx.enter_context(tc.tile_pool(name="keep", bufs=1))
-        ring = ctx.enter_context(tc.tile_pool(name="ring", bufs=4))
         results = ctx.enter_context(tc.tile_pool(name="results", bufs=8))
         psum_match = ctx.enter_context(tc.psum_pool(name="psum_match", bufs=MATCH_BANKS))
         psum_fresh = ctx.enter_context(tc.psum_pool(name="psum_fresh", bufs=1))
+        ring = ctx.enter_context(tc.tile_pool(name="ring", bufs=4))
         pair = ctx.enter_context(tc.tile_pool(name="pair", bufs=2))
-        psum_sum = ctx.enter_context(tc.psum_pool(name="psum_sum", bufs=2))
 
         def held(name, shape, dtype):
             return keep.tile(shape, dtype, name=name, align_bytes=256)
@@ -58,7 +65,7 @@ def tile_list_fresh_news_sections_kernel(
         w4_sc = held("w4_sc", [P, 2, N // 4], I32)
         w4_codes = held("w4_codes", [P, 2, 2 * N], U8)
         wd_raw = [held("wd_raw%d" % b, [P, PACK, N], F32) for b in range(2)]
-        gate_sb = [held("gate_sb%d" % h, [P, 2, HALF], F32) for h in range(2)]
+        gate_sb = [keep.tile([P, 2, HALF], F32, name="gate_sb", tag="gate%d" % h, align_bytes=256) for h in range(2)]
         art_table_sc = held("art_table_sc", [P, T // 4], I32)
         rdr_table_sc = held("rdr_table_sc", [P, T2 // 4], I32)
         plane1 = held("plane1", [P, (S + S2) // 4], I32)
@@ -75,7 +82,7 @@ def tile_list_fresh_news_sections_kernel(
             return table[a].rearrange("p t i -> p (t i)").bitcast(I32)
 
         nc.sync.dma_start(art_list[:], offs)
-        nc.sync.dma_start(art_table_sc[SC_FIRST:P, :], tab_scales.rearrange("a q t -> (a q) t").bitcast(I32))
+        nc.scalar.dma_start(art_table_sc[SC_FIRST:P, :], tab_scales.rearrange("a q t -> (a q) t").bitcast(I32))
         nc.sync.dma_start(rdr_list[:], offs2)
         nc.sync.dma_start(rdr_table_sc[SC_FIRST:P, :], tab2_scales.rearrange("a q t -> (a q) t").bitcast(I32))
         fresh_rows = held("fresh_rows", [P, HALF], F32)
@@ -96,19 +103,22 @@ def tile_list_fresh_news_sections_kernel(
         art_sc_listed = held("art_sc_listed", [P, S], U8)
         rdr_sc_listed = held("rdr_sc_listed", [P, S2], U8)
         plane0 = held("plane0", [P, (S + S2) // 4], I32)
-        art = [[held("art%d%d" % (a, b), [P, HALF], U32) for b in range(2)] for a in range(2)]
-        rdr = [[held("rdr%d%d" % (a, h), [P, HALF], U32) for h in range(2)] for a in range(2)]
+        art_all = [held("art%d" % a, [P, S], U32) for a in range(2)]
+        art = [[art_all[a][:, HALF * b : HALF * (b + 1)] for b in range(2)] for a in range(2)]
+        rdr0 = held("rdr0", [P, S2], U32)
+        rdr1 = [held("rdr1%d" % h, [P, HALF], U32) for h in range(2)]
+        rdr = [[rdr0[:, HALF * h : HALF * (h + 1)] for h in range(2)], [rdr1[h][:] for h in range(2)]]
 
         def list_half(offsets, half):
             return offsets[:, 32 * half : 32 * (half + 1)]
 
         def gather_rdr(a, h):
-            nc.vector.tensor_copy(rdr[a][h][:], rdr_table[a][:].bitcast(U32).indirect(list_half(rdr_list, h)))
+            nc.vector.tensor_copy(rdr[a][h], rdr_table[a][:].bitcast(U32).indirect(list_half(rdr_list, h)))
 
-        def gather_art(a, b):
+        def gather_art(a):
             nc.vector.tensor_copy(
-                art[a][b][:].rearrange("p (t m) -> p m t", t=PACK),
-                art_table[a][:].bitcast(U32).indirect(list_half(art_list, b)),
+                art_all[a][:].rearrange("p (b t m) -> p b m t", b=2, t=PACK),
+                art_table[a][:].bitcast(U32).indirect(art_list[:]),
             )
 
         nc.vector.tensor_copy(art_sc_listed[:], art_table_sc[:].bitcast(U8).indirect(art_list[:]))
@@ -126,12 +136,9 @@ def tile_list_fresh_news_sections_kernel(
             nc.sync.dma_start(plane1[r:P:32, :], plane0[SC_FIRST + 16 + r : P : 4, :])
         planes = [plane0[:].bitcast(U8), plane1[:].bitcast(U8)]
 
-        gather_rdr(0, 0)
-        gather_art(0, 0)
-        gather_art(0, 1)
-        gather_rdr(0, 1)
-        gather_art(1, 0)
-        gather_art(1, 1)
+        nc.vector.tensor_copy(rdr0[:], rdr_table[0][:].bitcast(U32).indirect(rdr_list[:]))
+        gather_art(0)
+        gather_art(1)
 
         for b in range(2):
             nc.sync.dma_start(wd_raw[b][:], wd[HALF * b : HALF * (b + 1), :].rearrange("(p t) n -> p t n", t=PACK))
@@ -147,173 +154,199 @@ def tile_list_fresh_news_sections_kernel(
         gather_rdr(1, 0)
         gather_rdr(1, 1)
 
-        def match_pass(bank, step, t, a):
-            h, b, first, width = step
-            nc.tensor.matmul_mx(
-                out=bank[:, t % (HALF // width), :],
-                lhsT=art[a][b][:, P * t : P * (t + 1)].bitcast(FP8X4),
-                lhsT_scale=planes[a][PLANE_ROW[a] :, HALF * b + P * t : HALF * b + P * (t + 1)],
-                rhs=rdr[a][h][:, first : first + width].bitcast(FP8X4),
-                rhs_scale=planes[a][PLANE_ROW[a] :, S + HALF * h + first : S + HALF * h + first + width],
-                start=(a == 0 and t % (HALF // width) == 0),
-                stop=(a == 1 and (t + 1) % (HALF // width) == 0),
-            )
+        def step_banks(s):
+            width = STEPS[s][3]
+            readers = min(width, QUARTER)
+            side = HALF // readers
+            return [(s, c, u) for c in range(width // readers) for u in range(PACK // side)], readers, side
 
         banks = {}
 
-        def open_bank(step, u, pool, tag):
-            side = HALF // step[3]
-            banks[step, u] = pool.tile([P, side, step[3]], F32, name=tag)
-            for t in range(side * u, side * (u + 1)):
-                match_pass(banks[step, u], step, t, 0)
+        def match_passes(key, a):
+            s, c, u = key
+            h, b, first = STEPS[s][:3]
+            readers, side = step_banks(s)[1:]
+            col = first + readers * c
+            for e in range(side):
+                t = side * u + e
+                nc.tensor.matmul_mx(
+                    out=banks[key][:, e, :],
+                    lhsT=art[a][b][:, P * t : P * (t + 1)].bitcast(FP8X4),
+                    lhsT_scale=planes[a][PLANE_ROW[a] :, HALF * b + P * t : HALF * b + P * (t + 1)],
+                    rhs=rdr[a][h][:, col : col + readers].bitcast(FP8X4),
+                    rhs_scale=planes[a][PLANE_ROW[a] :, S + HALF * h + col : S + HALF * h + col + readers],
+                    start=(a == 0 and e == 0),
+                    stop=(a == 1 and e == side - 1),
+                )
 
-        for u in range(2):
-            open_bank(STEPS[0], u, psum_sum, "sum_bank")
-        for step, u in [(step, u) for step in STEPS[1:4] for u in range(2)][:MATCH_BANKS]:
-            open_bank(step, u, psum_match, "match_bank")
+        def open_bank(key, pool, tag):
+            readers, side = step_banks(key[0])[1:]
+            banks[key] = pool.tile([P, side, readers], F32, name=tag)
+            match_passes(key, 0)
+
+        every_bank = [key for s in range(len(STEPS)) for key in step_banks(s)[0]]
+        for key in every_bank[:MATCH_BANKS]:
+            open_bank(key, psum_match, "match_bank")
+        for key in every_bank:
+            if key not in banks:
+                open_bank(key, psum_match, "match_bank")
+            match_passes(key, 1)
 
         z_codes = {(h, b): held("z_codes%d%d" % (h, b), [P, HALF], U32) for h in range(2) for b in range(2)}
         z_sc = {(h, b): held("z_sc%d%d" % (h, b), [P, HALF], U8) for h in range(2) for b in range(2)}
         z_bf = {}
+        late_codes = {}
 
         def interleave(columns, rows):
             nc.vector.tensor_copy(
                 out=columns.rearrange("p (g i) t -> p g t i", i=4), in_=rows.rearrange("p t (g i) -> p g t i", i=4)
             )
 
-        def match(step):
-            b, width = step[1], step[3]
-            side = HALF // width
-            on_scalar = step in SCALAR_STEPS
-            bounded = ring.tile([P, PACK // side, HALF], F32, name="bounded")
-            for u in range(PACK // side):
-                if (step, u) not in banks:
-                    open_bank(step, u, psum_match, "match_bank")
-                for t in range(side * u, side * (u + 1)):
-                    match_pass(banks[step, u], step, t, 1)
-                order = "p e j -> p e j" if on_scalar else "p e j -> p j e"
-                products = banks[step, u][:].rearrange(order)
-                nc.scalar.activation(
-                    out=bounded[:, u, :].rearrange("p (x y) -> p x y", y=products.shape[2]), in_=products, func=TANH
-                )
-            z_bf[step] = pair.tile([P, width * PACK], BF16, name="z_bf", align_bytes=64)
-            if on_scalar:
+        def match(s):
+            b, width, share = STEPS[s][1], STEPS[s][3], STEPS[s][4]
+            keys, readers, side = step_banks(s)
+            bounded = ring.tile([P, PACK // side, width, side], F32, name="bounded")
+            for key in keys:
+                c, u = key[1:]
+                if s in SCALAR_STEPS:
+                    nc.scalar.activation(
+                        out=bounded[:, u].rearrange("p j e -> p (j e)"),
+                        in_=banks[key][:].rearrange("p e j -> p (e j)"),
+                        func=TANH,
+                    )
+                else:
+                    nc.scalar.activation(
+                        out=bounded[:, u, readers * c : readers * (c + 1), :],
+                        in_=banks[key][:].rearrange("p e j -> p j e"),
+                        func=TANH,
+                    )
+            z_bf[s] = pair.tile([P, width * PACK], BF16, name="z_bf", align_bytes=64)
+            if s in SCALAR_STEPS:
                 z_rows = ring.tile([P, PACK, width], BF16, name="z_rows")
+                rows = bounded[:].rearrange("p u j e -> p (u j e)")
                 for t in range(PACK):
                     nc.scalar.activation(
                         out=z_rows[:, t, :],
-                        in_=bounded[:, t // side, width * (t % side) : width * (t % side + 1)],
+                        in_=rows[:, width * t : width * (t + 1)],
                         func=COPY,
                         scale=fresh_sb[:, PACK * b + t : PACK * b + t + 1],
                     )
-                interleave(z_bf[step][:].rearrange("p (j t) -> p j t", t=PACK), z_rows[:])
-            else:
-                split = width - width // GPSIMD_SHARE
-                for engine, cols, factors in (
-                    (nc.vector, slice(0, split), fresh_ps[:, b, :]),
-                    (nc.gpsimd, slice(split, width), fresh_sb[:, PACK * b : PACK * (b + 1)]),
-                ):
-                    engine.tensor_tensor(
-                        z_bf[step][:].rearrange("p (j u e) -> p j u e", u=PACK // side, e=side)[:, cols],
-                        bounded[:].rearrange("p u (j e) -> p j u e", e=side)[:, cols],
-                        factors.rearrange("p (u e) -> p u e", e=side)
-                        .unsqueeze(1)
-                        .to_broadcast([P, cols.stop - cols.start, PACK // side, side]),
-                        MULT,
-                    )
+                interleave(z_bf[s][:].rearrange("p (j t) -> p j t", t=PACK), z_rows[:])
+                return
+            for engine, cols, factors in (
+                (nc.vector, slice(0, width - share), fresh_ps[:, b, :]),
+                (nc.gpsimd, slice(width - share, width), fresh_sb[:, PACK * b : PACK * (b + 1)]),
+            ):
+                engine.tensor_tensor(
+                    z_bf[s][:].rearrange("p (j u e) -> p j u e", u=PACK // side, e=side)[:, cols],
+                    bounded[:].rearrange("p u j e -> p j u e")[:, cols],
+                    factors.rearrange("p (u e) -> p u e", e=side)
+                    .unsqueeze(1)
+                    .to_broadcast([P, cols.stop - cols.start, PACK // side, side]),
+                    MULT,
+                )
 
-        def quantise_z(step):
-            h, b, first, width = step
+        def quantise_z(s):
+            h, b, first, width = STEPS[s][:4]
             cols = slice(first, first + width)
-            nc.vector.quantize_mx(out=z_codes[h, b][:, cols].bitcast(FP8X4), scales=z_sc[h, b][:, cols], in_=z_bf[step][:])
+            if s == HELD_STEP:
+                late_codes[s] = keep.tile([P, width], U32, name="z_late", tag="gate0", align_bytes=256)[:]
+            codes = late_codes.get(s, z_codes[h, b][:, cols])
+            nc.vector.quantize_mx(out=codes.bitcast(FP8X4), scales=z_sc[h, b][:, cols], in_=z_bf[s][:])
 
         wd_codes = [held("wd_codes%d" % b, [P, N], U32) for b in range(2)]
         wd_sc = [held("wd_sc%d" % b, [P, N], U8) for b in range(2)]
-        wd_bf = {}
+        wd_bf = [held("wd_bf%d" % b, [P, N, PACK], BF16) for b in range(2)]
 
         def cast_wd(b):
-            wd_bf[b] = held("wd_bf%d" % b, [P, N, PACK], BF16)
-            interleave(wd_bf[b][:], wd_raw[b][:])
+            if b == 0:
+                nc.scalar.copy(out=wd_bf[0][:, P:N, :], in_=wd_raw[0][:, :, P:N].rearrange("p t n -> p n t"))
+                interleave(wd_bf[0][:, 0:P, :], wd_raw[0][:, :, 0:P])
+            else:
+                interleave(wd_bf[b][:], wd_raw[b][:])
 
         def quantise_wd(b):
             nc.vector.quantize_mx(
                 out=wd_codes[b][:].bitcast(FP8X4), scales=wd_sc[b][:], in_=wd_bf[b][:].rearrange("p n t -> p (n t)")
             )
 
-        def section_passes(acc, h, b, n, cols):
+        def section_passes(acc, n, b, codes, scales, start, stop):
             rows = slice(P * n, P * (n + 1))
-            for codes, scales, last in (
-                (w4_codes[:, b, 2 * P * n : 2 * P * (n + 1)].bitcast(FP4X4), w4_sc[:, b, :].bitcast(U8)[:, rows], False),
-                (wd_codes[b][:, rows].bitcast(FP8X4), wd_sc[b][:, rows], True),
-            ):
+            width = codes.shape[1]
+            narrow = width if width == HALF else P
+            for first in range(0, width, narrow):
+                cols = slice(first, first + narrow)
                 nc.tensor.matmul_mx(
-                    out=acc,
-                    lhsT=codes,
-                    lhsT_scale=scales,
-                    rhs=z_codes[h, b][:, cols].bitcast(FP8X4),
-                    rhs_scale=z_sc[h, b][:, cols],
-                    start=(b == 0 and not last),
-                    stop=(b == 1 and last),
+                    out=acc[:, cols],
+                    lhsT=w4_codes[:, b, 2 * P * n : 2 * P * (n + 1)].bitcast(FP4X4),
+                    lhsT_scale=w4_sc[:, b, :].bitcast(U8)[:, rows],
+                    rhs=codes[:, cols].bitcast(FP8X4),
+                    rhs_scale=scales[:, cols],
+                    start=(start and first == 0),
+                    stop=False,
                 )
+            nc.tensor.matmul_mx(
+                out=acc,
+                lhsT=wd_codes[b][:, rows].bitcast(FP8X4),
+                lhsT_scale=wd_sc[b][:, rows],
+                rhs=codes.bitcast(FP8X4),
+                rhs_scale=scales,
+                start=False,
+                stop=stop,
+            )
 
         sums = {}
 
         def first_half(b):
             for n in range(2):
                 if b == 0:
-                    sums["half", n] = psum_sum.tile([P, HALF], F32, name="sum_bank")
-                section_passes(sums["half", n][:], 0, b, n, slice(0, HALF))
+                    sums[n] = psum_match.tile([P, HALF], F32, name="match_bank")
+                section_passes(sums[n][:], n, b, z_codes[0, b][:], z_sc[0, b][:], b == 0, b == 1)
 
         def store_first_half():
             for n in range(2):
                 scores = results.tile([P, HALF], F32, name="scores")
-                nc.vector.tensor_tensor(scores[:], sums["half", n][:], gate_sb[0][:, n, :], MULT)
+                nc.vector.tensor_tensor(scores[:], sums[n][:], gate_sb[0][:, n, :], MULT)
                 nc.sync.dma_start(out[P * n : P * (n + 1), 0:HALF], scores[:])
 
-        def third_quarter():
-            for n in range(2):
-                sums["third", n] = psum_sum.tile([P, QUARTER], F32, name="sum_bank")
-                for c in range(2):
-                    for b in range(2):
-                        section_passes(sums["third", n][:, P * c : P * (c + 1)], 1, b, n, slice(P * c, P * (c + 1)))
+        pieces = {}
 
-        def store_third_quarter(n):
-            scores = results.tile([P, QUARTER], F32, name="scores")
-            nc.vector.tensor_tensor(scores[:], sums["third", n][:], gate_sb[1][:, n, 0:QUARTER], MULT)
-            nc.sync.dma_start(out[P * n : P * (n + 1), HALF : HALF + QUARTER], scores[:])
-
-        def last_eighth(c, b):
+        def piece_passes(s, b):
+            first, width = STEPS[s][2:4]
+            cols = slice(first, first + width)
+            codes = late_codes[s] if (s == HELD_STEP and b == 1) else z_codes[1, b][:, cols]
             for n in range(2):
                 if b == 0:
-                    sums["last", c, n] = psum_match.tile([P, P], F32, name="match_bank")
-                section_passes(sums["last", c, n][:], 1, b, n, slice(QUARTER + P * c, QUARTER + P * (c + 1)))
+                    pieces[s, n] = psum_match.tile([P, width], F32, name="match_bank")
+                section_passes(pieces[s, n][:], n, b, codes, z_sc[1, b][:, cols], b == 0, b == 1)
 
-        def store_last_eighth(c):
-            first = QUARTER + P * c
-            for n, queue in enumerate((nc.sync, nc.scalar)):
-                scores = results.tile([P, P], F32, name="scores")
-                nc.vector.tensor_tensor(scores[:], sums["last", c, n][:], gate_sb[1][:, n, first : first + P], MULT)
-                queue.dma_start(out[P * n : P * (n + 1), HALF + first : HALF + first + P], scores[:])
+        def store_piece(s, n, queue):
+            first, width = STEPS[s][2:4]
+            scores = results.tile([P, width], F32, name="scores")
+            nc.vector.tensor_tensor(scores[:], pieces[s, n][:], gate_sb[1][:, n, first : first + width], MULT)
+            queue.dma_start(out[P * n : P * (n + 1), HALF + first : HALF + first + width], scores[:])
 
         behind_step = {
             0: [lambda: cast_wd(1), lambda: quantise_wd(0)],
             1: [lambda: quantise_wd(1)],
             2: [lambda: first_half(0)],
             4: [lambda: first_half(1)],
-            5: [store_first_half],
-            7: [third_quarter],
-            8: [lambda: last_eighth(0, 0), lambda: last_eighth(1, 0), lambda: last_eighth(0, 1)],
+            7: [lambda: piece_passes(5, 0), lambda: piece_passes(5, 1)],
+            8: [lambda: piece_passes(7, 0), lambda: piece_passes(8, 0), lambda: piece_passes(7, 1)],
         }
         cast_wd(0)
-        for s, step in enumerate(STEPS):
-            match(step)
+        for s in range(len(STEPS)):
+            if s == 6:
+                store_first_half()
+            match(s)
             if s > 0:
-                quantise_z(STEPS[s - 1])
+                quantise_z(s - 1)
             for work in behind_step.get(s, []):
                 work()
-        store_third_quarter(0)
-        quantise_z(STEPS[-1])
-        last_eighth(1, 1)
-        store_third_quarter(1)
-        for c in range(2):
-            store_last_eighth(c)
+        store_piece(5, 0, nc.sync)
+        quantise_z(8)
+        piece_passes(8, 1)
+        store_piece(5, 1, nc.scalar)
+        for s in (7, 8):
+            store_piece(s, 0, nc.sync)
+            store_piece(s, 1, nc.scalar)

@@ -41,6 +41,7 @@ STEPS = [
 
 SCALAR_STEPS = (7, 8)
 HELD_STEP = 5
+SHARED_STEPS = 7
 
 
 def tile_list_fresh_news_sections_kernel(
@@ -52,8 +53,7 @@ def tile_list_fresh_news_sections_kernel(
         results = ctx.enter_context(tc.tile_pool(name="results", bufs=8))
         psum_match = ctx.enter_context(tc.psum_pool(name="psum_match", bufs=MATCH_BANKS))
         psum_fresh = ctx.enter_context(tc.psum_pool(name="psum_fresh", bufs=1))
-        ring = ctx.enter_context(tc.tile_pool(name="ring", bufs=4))
-        pair = ctx.enter_context(tc.tile_pool(name="pair", bufs=2))
+        ring = ctx.enter_context(tc.tile_pool(name="ring", bufs=2))
 
         def held(name, shape, dtype):
             return keep.tile(shape, dtype, name=name, align_bytes=256)
@@ -64,7 +64,7 @@ def tile_list_fresh_news_sections_kernel(
         rdr_table = [held("rdr_table%d" % a, [P, T2], I32) for a in range(2)]
         w4_sc = held("w4_sc", [P, 2, N // 4], I32)
         w4_codes = held("w4_codes", [P, 2, 2 * N], U8)
-        wd_raw = [held("wd_raw%d" % b, [P, PACK, N], F32) for b in range(2)]
+        wd_raw = keep.tile([P, 2, PACK, N], F32, name="wd_raw", tag="wd_raw", align_bytes=64)
         gate_sb = [keep.tile([P, 2, HALF], F32, name="gate_sb", tag="gate%d" % h, align_bytes=256) for h in range(2)]
         art_table_sc = held("art_table_sc", [P, T // 4], I32)
         rdr_table_sc = held("rdr_table_sc", [P, T2 // 4], I32)
@@ -140,8 +140,9 @@ def tile_list_fresh_news_sections_kernel(
         gather_art(0)
         gather_art(1)
 
-        for b in range(2):
-            nc.sync.dma_start(wd_raw[b][:], wd[HALF * b : HALF * (b + 1), :].rearrange("(p t) n -> p t n", t=PACK))
+        nc.sync.dma_start(
+            wd_raw[:].rearrange("p b t n -> p b (t n)"), wd.rearrange("(b p t) n -> p b (t n)", b=2, t=PACK)
+        )
         nc.sync.dma_start(w4_codes[:].bitcast(I32), w4_words.rearrange("b p c -> p b c").bitcast(I32))
         for q in range(QUADRANTS):
             nc.sync.dma_start(
@@ -196,6 +197,7 @@ def tile_list_fresh_news_sections_kernel(
         z_sc = {(h, b): held("z_sc%d%d" % (h, b), [P, HALF], U8) for h in range(2) for b in range(2)}
         z_bf = {}
         late_codes = {}
+        stage = {}
 
         def interleave(columns, rows):
             nc.vector.tensor_copy(
@@ -205,7 +207,11 @@ def tile_list_fresh_news_sections_kernel(
         def match(s):
             b, width, share = STEPS[s][1], STEPS[s][3], STEPS[s][4]
             keys, readers, side = step_banks(s)
-            bounded = ring.tile([P, PACK // side, width, side], F32, name="bounded")
+            room = (STEPS[s + 1][3] - STEPS[s + 1][4]) * PACK // 2 if s < SHARED_STEPS - 1 else 0
+            if s == 0:
+                room = share * side
+            stage[s] = (held("stage%d" % s, [P, room + width * PACK], F32), room)
+            bounded = stage[s][0][:, room:].rearrange("p (u j e) -> p u j e", u=PACK // side, e=side)
             for key in keys:
                 c, u = key[1:]
                 if s in SCALAR_STEPS:
@@ -220,10 +226,15 @@ def tile_list_fresh_news_sections_kernel(
                         in_=banks[key][:].rearrange("p e j -> p j e"),
                         func=TANH,
                     )
-            z_bf[s] = pair.tile([P, width * PACK], BF16, name="z_bf", align_bytes=64)
+            if s == 0:
+                z_bf[s] = keep.tile([P, width * PACK], BF16, name="z_bf", tag="wd_raw", align_bytes=64)[:]
+            elif s < SHARED_STEPS:
+                z_bf[s] = stage[s - 1][0][:, 0 : width * PACK // 2].bitcast(BF16)
+            else:
+                z_bf[s] = z_bf[s - 2][:, 0 : width * PACK]
             if s in SCALAR_STEPS:
                 z_rows = ring.tile([P, PACK, width], BF16, name="z_rows")
-                rows = bounded[:].rearrange("p u j e -> p (u j e)")
+                rows = bounded.rearrange("p u j e -> p (u j e)")
                 for t in range(PACK):
                     nc.scalar.activation(
                         out=z_rows[:, t, :],
@@ -231,15 +242,15 @@ def tile_list_fresh_news_sections_kernel(
                         func=COPY,
                         scale=fresh_sb[:, PACK * b + t : PACK * b + t + 1],
                     )
-                interleave(z_bf[s][:].rearrange("p (j t) -> p j t", t=PACK), z_rows[:])
+                interleave(z_bf[s].rearrange("p (j t) -> p j t", t=PACK), z_rows[:])
                 return
             for engine, cols, factors in (
                 (nc.vector, slice(0, width - share), fresh_ps[:, b, :]),
                 (nc.gpsimd, slice(width - share, width), fresh_sb[:, PACK * b : PACK * (b + 1)]),
             ):
                 engine.tensor_tensor(
-                    z_bf[s][:].rearrange("p (j u e) -> p j u e", u=PACK // side, e=side)[:, cols],
-                    bounded[:].rearrange("p u j e -> p j u e")[:, cols],
+                    z_bf[s].rearrange("p (j u e) -> p j u e", u=PACK // side, e=side)[:, cols],
+                    bounded.rearrange("p u j e -> p j u e")[:, cols],
                     factors.rearrange("p (u e) -> p u e", e=side)
                     .unsqueeze(1)
                     .to_broadcast([P, cols.stop - cols.start, PACK // side, side]),
@@ -252,18 +263,14 @@ def tile_list_fresh_news_sections_kernel(
             if s == HELD_STEP:
                 late_codes[s] = keep.tile([P, width], U32, name="z_late", tag="gate0", align_bytes=256)[:]
             codes = late_codes.get(s, z_codes[h, b][:, cols])
-            nc.vector.quantize_mx(out=codes.bitcast(FP8X4), scales=z_sc[h, b][:, cols], in_=z_bf[s][:])
+            nc.vector.quantize_mx(out=codes.bitcast(FP8X4), scales=z_sc[h, b][:, cols], in_=z_bf[s])
 
         wd_codes = [held("wd_codes%d" % b, [P, N], U32) for b in range(2)]
         wd_sc = [held("wd_sc%d" % b, [P, N], U8) for b in range(2)]
-        wd_bf = [held("wd_bf%d" % b, [P, N, PACK], BF16) for b in range(2)]
+        wd_bf = [keep.tile([P, N, PACK], BF16, name="wd_bf", tag="wd_bf%d" % b, align_bytes=64) for b in range(2)]
 
         def cast_wd(b):
-            if b == 0:
-                nc.scalar.copy(out=wd_bf[0][:, P:N, :], in_=wd_raw[0][:, :, P:N].rearrange("p t n -> p n t"))
-                interleave(wd_bf[0][:, 0:P, :], wd_raw[0][:, :, 0:P])
-            else:
-                interleave(wd_bf[b][:], wd_raw[b][:])
+            interleave(wd_bf[b][:], wd_raw[:, b])
 
         def quantise_wd(b):
             nc.vector.quantize_mx(
@@ -327,14 +334,15 @@ def tile_list_fresh_news_sections_kernel(
             queue.dma_start(out[P * n : P * (n + 1), HALF + first : HALF + first + width], scores[:])
 
         behind_step = {
-            0: [lambda: cast_wd(1), lambda: quantise_wd(0)],
-            1: [lambda: quantise_wd(1)],
+            0: [lambda: quantise_wd(1)],
             2: [lambda: first_half(0)],
             4: [lambda: first_half(1)],
             7: [lambda: piece_passes(5, 0), lambda: piece_passes(5, 1)],
             8: [lambda: piece_passes(7, 0), lambda: piece_passes(8, 0), lambda: piece_passes(7, 1)],
         }
-        cast_wd(0)
+        for b in range(2):
+            cast_wd(b)
+        quantise_wd(0)
         for s in range(len(STEPS)):
             if s == 6:
                 store_first_half()

@@ -16,6 +16,7 @@ FP8X4 = mybir.dt.float8_e4m3fn_x4
 FP4X4 = mybir.dt.float4_e2m1fn_x4
 MULT = mybir.AluOpType.mult
 TANH = mybir.ActivationFunctionType.Tanh
+IDENTITY = mybir.ActivationFunctionType.Identity
 COPY = mybir.ActivationFunctionType.Copy
 
 P = 128
@@ -70,9 +71,7 @@ def tile_list_fresh_news_sections_kernel(
         rdr_table_sc = held("rdr_table_sc", [P, T2 // 4], I32)
         plane1 = held("plane1", [P, (S + S2) // 4], I32)
         fresh_sb = held("fresh_sb", [P, 2 * PACK], F32)
-        warm = held("warm", [P, 2], F32)
 
-        nc.vector.memset(warm[:, 0:1], 0.0)
         nc.vector.memset(art_table_sc[0:SC_FIRST, :], 0)
         nc.vector.memset(rdr_table_sc[0:SC_FIRST, :], 0)
         nc.vector.memset(plane1[:], 0)
@@ -93,8 +92,7 @@ def tile_list_fresh_news_sections_kernel(
         fresh_ps = psum_fresh.tile([P, P, PACK], F32, name="fresh_ps")
         for t in range(PACK):
             nc.tensor.transpose(fresh_ps[:, :, t], fresh_rows[:, t:HALF:PACK], identity[:])
-        nc.scalar.copy(out=fresh_sb[:].rearrange("p (b t) -> p b t", b=2), in_=fresh_ps[:, 0:2, :])
-        nc.scalar.activation(out=warm[:, 1:2], in_=warm[:, 0:1], func=TANH)
+        nc.scalar.activation(out=fresh_sb[:].rearrange("p (b t) -> p b t", b=2), in_=fresh_ps[:, 0:2, :], func=IDENTITY)
         nc.sync.dma_start(rdr_table[0][:], table_words(tab2_words, 0))
         for a in range(2):
             nc.sync.dma_start(art_table[a][:], table_words(tab_words, a))

@@ -24,25 +24,12 @@ PACK = 4
 HALF = 512
 QUARTER = 256
 QUADRANTS = 4
-MATCH_BANKS = 7
+BANKS = 7
 SC_FIRST = 96
 PLANE_ROW = (12, 0)
-STEPS = [
-    (0, 0, 0, QUARTER, 64),
-    (0, 0, QUARTER, QUARTER, 64),
-    (0, 1, 0, QUARTER, 64),
-    (0, 1, QUARTER, QUARTER, 64),
-    (1, 0, 0, QUARTER, 64),
-    (1, 1, 0, QUARTER, 64),
-    (1, 0, QUARTER, QUARTER, 144),
-    (1, 1, QUARTER, P, 32),
-    (1, 1, QUARTER + P, P, 32),
-]
-
-
-SCALAR_STEPS = (7, 8)
-HELD_STEP = 5
-SHARED_STEPS = 7
+UNIT = QUARTER * PACK
+SLIDE = 32
+SHARE = (160, 160, 160, 164)
 
 
 def tile_list_fresh_news_sections_kernel(
@@ -51,31 +38,32 @@ def tile_list_fresh_news_sections_kernel(
     nc = tc.nc
     with ExitStack() as ctx:
         keep = ctx.enter_context(tc.tile_pool(name="keep", bufs=1))
-        results = ctx.enter_context(tc.tile_pool(name="results", bufs=8))
-        psum_match = ctx.enter_context(tc.psum_pool(name="psum_match", bufs=MATCH_BANKS))
-        psum_fresh = ctx.enter_context(tc.psum_pool(name="psum_fresh", bufs=1))
-        ring = ctx.enter_context(tc.tile_pool(name="ring", bufs=2))
+        psum = ctx.enter_context(tc.psum_pool(name="psum", bufs=1))
 
-        def held(name, shape, dtype):
-            return keep.tile(shape, dtype, name=name, align_bytes=256)
+        def held(name, shape, dtype, tag=None):
+            return keep.tile(shape, dtype, name=name, tag=tag or name, align_bytes=256)
 
         art_list = keep.tile([P, S // 16], U16, name="art_list")
         rdr_list = keep.tile([P, S2 // 16], U16, name="rdr_list")
         art_table = [held("art_table%d" % a, [P, T], I32) for a in range(2)]
         rdr_table = [held("rdr_table%d" % a, [P, T2], I32) for a in range(2)]
-        w4_sc = held("w4_sc", [P, 2, N // 4], I32)
-        w4_codes = held("w4_codes", [P, 2, 2 * N], U8)
-        wd_raw = keep.tile([P, 2, PACK, N], F32, name="wd_raw", tag="wd_raw", align_bytes=64)
-        gate_sb = [keep.tile([P, 2, HALF], F32, name="gate_sb", tag="gate%d" % h, align_bytes=256) for h in range(2)]
         art_table_sc = held("art_table_sc", [P, T // 4], I32)
         rdr_table_sc = held("rdr_table_sc", [P, T2 // 4], I32)
-        plane1 = held("plane1", [P, (S + S2) // 4], I32)
-        fresh_sb = held("fresh_sb", [P, 2 * PACK], F32)
+        planes = [held("plane%d" % a, [P, (S + S2) // 4], I32) for a in range(2)]
+        w4_sc = held("w4_sc", [P, 2, N // 4], I32)
+        w4_codes = held("w4_codes", [P, 2, 2 * N], U8)
+        wd_raw = held("wd_raw", [P, 2, PACK, N], F32)
+        gate_sb = [held("gate%d" % q, [P, 2, QUARTER], F32) for q in range(4)]
+        fresh_rows = held("fresh_rows", [P, HALF], F32)
+        fresh_sb = held("fresh_sb", [P, 2, PACK], F32)
+        identity = held("identity", [P, P], F32)
 
         nc.vector.memset(art_table_sc[0:SC_FIRST, :], 0)
-        nc.vector.memset(rdr_table_sc[0:SC_FIRST, :], 0)
-        nc.vector.memset(plane1[:], 0)
+        nc.vector.memset(fresh_rows[0 : P - 2, :], 0.0)
         nc.vector.memset(w4_sc[:], 0)
+        nc.gpsimd.memset(rdr_table_sc[0:SC_FIRST, :], 0)
+        make_identity(nc, identity[:])
+        nc.gpsimd.memset(planes[1][:], 0)
 
         def table_words(table, a):
             return table[a].rearrange("p t i -> p (t i)").bitcast(I32)
@@ -84,15 +72,11 @@ def tile_list_fresh_news_sections_kernel(
         nc.scalar.dma_start(art_table_sc[SC_FIRST:P, :], tab_scales.rearrange("a q t -> (a q) t").bitcast(I32))
         nc.sync.dma_start(rdr_list[:], offs2)
         nc.sync.dma_start(rdr_table_sc[SC_FIRST:P, :], tab2_scales.rearrange("a q t -> (a q) t").bitcast(I32))
-        fresh_rows = held("fresh_rows", [P, HALF], F32)
-        identity = held("identity", [P, P], F32)
-        nc.gpsimd.memset(fresh_rows[:], 0.0)
-        make_identity(nc, identity[:])
-        nc.sync.dma_start(fresh_rows[0:2, :], fresh.rearrange("(b i) -> b i", b=2))
-        fresh_ps = psum_fresh.tile([P, P, PACK], F32, name="fresh_ps")
+        nc.sync.dma_start(fresh_rows[P - 2 : P, :], fresh.rearrange("(b i) -> b i", b=2))
+        fresh_ps = psum.tile([P, P, PACK], F32, name="fresh_ps")
         for t in range(PACK):
             nc.tensor.transpose(fresh_ps[:, :, t], fresh_rows[:, t:HALF:PACK], identity[:])
-        nc.scalar.activation(out=fresh_sb[:].rearrange("p (b t) -> p b t", b=2), in_=fresh_ps[:, 0:2, :], func=IDENTITY)
+        nc.scalar.activation(out=fresh_sb[:], in_=fresh_ps[:, P - 2 : P, :], func=IDENTITY)
         nc.sync.dma_start(rdr_table[0][:], table_words(tab2_words, 0))
         for a in range(2):
             nc.sync.dma_start(art_table[a][:], table_words(tab_words, a))
@@ -100,43 +84,30 @@ def tile_list_fresh_news_sections_kernel(
 
         art_sc_listed = held("art_sc_listed", [P, S], U8)
         rdr_sc_listed = held("rdr_sc_listed", [P, S2], U8)
-        plane0 = held("plane0", [P, (S + S2) // 4], I32)
-        art_all = [held("art%d" % a, [P, S], U32) for a in range(2)]
-        art = [[art_all[a][:, HALF * b : HALF * (b + 1)] for b in range(2)] for a in range(2)]
+        art = [held("art%d" % a, [P, S], U32) for a in range(2)]
         rdr0 = held("rdr0", [P, S2], U32)
         rdr1 = [held("rdr1%d" % h, [P, HALF], U32) for h in range(2)]
-        rdr = [[rdr0[:, HALF * h : HALF * (h + 1)] for h in range(2)], [rdr1[h][:] for h in range(2)]]
-
-        def list_half(offsets, half):
-            return offsets[:, 32 * half : 32 * (half + 1)]
-
-        def gather_rdr(a, h):
-            nc.vector.tensor_copy(rdr[a][h], rdr_table[a][:].bitcast(U32).indirect(list_half(rdr_list, h)))
-
-        def gather_art(a):
-            nc.vector.tensor_copy(
-                art_all[a][:].rearrange("p (b t m) -> p b m t", b=2, t=PACK),
-                art_table[a][:].bitcast(U32).indirect(art_list[:]),
-            )
 
         nc.vector.tensor_copy(art_sc_listed[:], art_table_sc[:].bitcast(U8).indirect(art_list[:]))
         nc.vector.tensor_copy(rdr_sc_listed[:], rdr_table_sc[:].bitcast(U8).indirect(rdr_list[:]))
         nc.vector.tensor_copy(
-            plane0[:].bitcast(U8)[:, 0:S].rearrange("p (b t m) -> p b t m", b=2, t=PACK),
+            planes[0][:].bitcast(U8)[:, 0:S].rearrange("p (b t m) -> p b t m", b=2, t=PACK),
             art_sc_listed[:].rearrange("p (b m t) -> p b t m", b=2, t=PACK),
         )
-        nc.vector.tensor_copy(plane0[:, S // 4 :], rdr_sc_listed[:].bitcast(I32))
+        nc.vector.tensor_copy(planes[0][:, S // 4 :], rdr_sc_listed[:].bitcast(I32))
         for q in range(QUADRANTS - 1):
             row = 32 * q + PLANE_ROW[0]
-            nc.sync.dma_start(plane0[row : row + 4, :], plane0[SC_FIRST + 4 * q : SC_FIRST + 4 * q + 4, :])
+            nc.sync.dma_start(planes[0][row : row + 4, :], planes[0][SC_FIRST + 4 * q : SC_FIRST + 4 * q + 4, :])
         nc.sync.dma_start(rdr_table[1][:, T:T2], table_words(tab2_words, 1)[:, T:T2])
         for r in range(4):
-            nc.sync.dma_start(plane1[r:P:32, :], plane0[SC_FIRST + 16 + r : P : 4, :])
-        planes = [plane0[:].bitcast(U8), plane1[:].bitcast(U8)]
+            nc.sync.dma_start(planes[1][r:P:32, :], planes[0][SC_FIRST + 16 + r : P : 4, :])
 
         nc.vector.tensor_copy(rdr0[:], rdr_table[0][:].bitcast(U32).indirect(rdr_list[:]))
-        gather_art(0)
-        gather_art(1)
+        for a in range(2):
+            nc.vector.tensor_copy(
+                art[a][:].rearrange("p (b t m) -> p b m t", b=2, t=PACK),
+                art_table[a][:].bitcast(U32).indirect(art_list[:]),
+            )
 
         nc.sync.dma_start(
             wd_raw[:].rearrange("p b t n -> p b (t n)"), wd.rearrange("(b p t) n -> p b (t n)", b=2, t=PACK)
@@ -147,212 +118,174 @@ def tile_list_fresh_news_sections_kernel(
                 w4_sc[32 * q : 32 * q + 4, :, :],
                 w4_scales[:, 4 * q : 4 * q + 4, :].rearrange("b r c -> r b c").bitcast(I32),
             )
+        for q in range(4):
+            nc.sync.dma_start(
+                gate_sb[q][:], gate[:, QUARTER * q : QUARTER * (q + 1)].rearrange("(n p) j -> p n j", p=P)
+            )
+
         for h in range(2):
-            nc.sync.dma_start(gate_sb[h][:], gate[:, HALF * h : HALF * (h + 1)].rearrange("(n p) j -> p n j", p=P))
+            nc.vector.tensor_copy(
+                rdr1[h][:], rdr_table[1][:].bitcast(U32).indirect(rdr_list[:, 32 * h : 32 * (h + 1)])
+            )
 
-        gather_rdr(1, 0)
-        gather_rdr(1, 1)
+        turn = []
 
-        def step_banks(s):
-            width = STEPS[s][3]
-            readers = min(width, QUARTER)
-            side = HALF // readers
-            return [(s, c, u) for c in range(width // readers) for u in range(PACK // side)], readers, side
+        def next_bank(shape):
+            turn.append(0)
+            return psum.tile(shape, F32, name="bank", tag="bank%d" % ((len(turn) - 1) % BANKS))
 
-        banks = {}
-
-        def match_passes(key, a):
-            s, c, u = key
-            h, b, first = STEPS[s][:3]
-            readers, side = step_banks(s)[1:]
-            col = first + readers * c
-            for e in range(side):
-                t = side * u + e
+        def match_pass(bank, a, b, slots, first, width):
+            words = rdr0[:, first : first + width] if a == 0 else rdr1[first // HALF][:, first % HALF : first % HALF + width]
+            plane = planes[a][:].bitcast(U8)
+            for e, t in enumerate(slots):
+                col = HALF * b + P * t
                 nc.tensor.matmul_mx(
-                    out=banks[key][:, e, :],
-                    lhsT=art[a][b][:, P * t : P * (t + 1)].bitcast(FP8X4),
-                    lhsT_scale=planes[a][PLANE_ROW[a] :, HALF * b + P * t : HALF * b + P * (t + 1)],
-                    rhs=rdr[a][h][:, col : col + readers].bitcast(FP8X4),
-                    rhs_scale=planes[a][PLANE_ROW[a] :, S + HALF * h + col : S + HALF * h + col + readers],
+                    out=bank[:, e, :],
+                    lhsT=art[a][:, col : col + P].bitcast(FP8X4),
+                    lhsT_scale=plane[PLANE_ROW[a] :, col : col + P],
+                    rhs=words.bitcast(FP8X4),
+                    rhs_scale=plane[PLANE_ROW[a] :, S + first : S + first + width],
                     start=(a == 0 and e == 0),
-                    stop=(a == 1 and e == side - 1),
+                    stop=(a == 1 and e == len(slots) - 1),
                 )
 
-        def open_bank(key, pool, tag):
-            readers, side = step_banks(key[0])[1:]
-            banks[key] = pool.tile([P, side, readers], F32, name=tag)
-            match_passes(key, 0)
+        matches = {}
 
-        every_bank = [key for s in range(len(STEPS)) for key in step_banks(s)[0]]
-        for key in every_bank[:MATCH_BANKS]:
-            open_bank(key, psum_match, "match_bank")
-        for key in every_bank:
-            if key not in banks:
-                open_bank(key, psum_match, "match_bank")
-            match_passes(key, 1)
+        def pair_args(key):
+            q, b, u = key
+            return b, (2 * u, 2 * u + 1), QUARTER * q, QUARTER
 
-        z_codes = {(h, b): held("z_codes%d%d" % (h, b), [P, HALF], U32) for h in range(2) for b in range(2)}
-        z_sc = {(h, b): held("z_sc%d%d" % (h, b), [P, HALF], U8) for h in range(2) for b in range(2)}
-        z_bf = {}
-        late_codes = {}
-        stage = {}
+        def open_pair(key):
+            matches[key] = next_bank([P, 2, QUARTER])
+            match_pass(matches[key], 0, *pair_args(key))
+
+        def close_pair(key):
+            if key not in matches:
+                open_pair(key)
+            match_pass(matches[key], 1, *pair_args(key))
+
+        pairs = [(q, b, u) for q in range(4) for b in range(2) for u in range(2)]
+        for key in pairs[:BANKS]:
+            open_pair(key)
+        for key in pairs[:14]:
+            close_pair(key)
+        narrow = []
+        for c in range(2):
+            narrow.append(next_bank([P, PACK, P]))
+            for a in range(2):
+                match_pass(narrow[c], a, 1, range(PACK), 3 * QUARTER + P * c, P)
+
+        bounded = {}
+
+        def squash(q, b):
+            bounded[q, b] = held("bounded%d%d" % (q, b), [P, UNIT], F32)
+            for u in range(2):
+                nc.scalar.activation(
+                    out=bounded[q, b][:].rearrange("p (u j e) -> p u j e", u=2, e=2)[:, u], in_=matches[q, b, u][:].rearrange("p e j -> p j e"), func=TANH
+                )
+
+        values = held("values", [P, 2 * UNIT + 3 * SLIDE], BF16)
+
+        def region(q, i):
+            first = (3 - q) * SLIDE + i * UNIT
+            return values[:, first : first + UNIT]
+
+        def weigh(engine, q, b, dst, cols):
+            factors = fresh_ps[:, P - 2 + b, :] if engine is nc.vector else fresh_sb[:, b, :]
+            engine.tensor_tensor(
+                dst.rearrange("p (j u e) -> p j u e", u=2, e=2)[:, cols],
+                bounded[q, b][:].rearrange("p (u j e) -> p j u e", u=2, e=2)[:, cols],
+                factors.rearrange("p (u e) -> p u e", e=2).unsqueeze(1).to_broadcast([P, cols.stop - cols.start, 2, 2]),
+                MULT,
+            )
 
         def interleave(columns, rows):
             nc.vector.tensor_copy(
                 out=columns.rearrange("p (g i) t -> p g t i", i=4), in_=rows.rearrange("p t (g i) -> p g t i", i=4)
             )
 
-        def match(s):
-            b, width, share = STEPS[s][1], STEPS[s][3], STEPS[s][4]
-            keys, readers, side = step_banks(s)
-            room = (STEPS[s + 1][3] - STEPS[s + 1][4]) * PACK // 2 if s < SHARED_STEPS - 1 else 0
-            if s == 0:
-                room = share * side
-            stage[s] = (held("stage%d" % s, [P, room + width * PACK], F32), room)
-            bounded = stage[s][0][:, room:].rearrange("p (u j e) -> p u j e", u=PACK // side, e=side)
-            for key in keys:
-                c, u = key[1:]
-                if s in SCALAR_STEPS:
-                    nc.scalar.activation(
-                        out=bounded[:, u].rearrange("p j e -> p (j e)"),
-                        in_=banks[key][:].rearrange("p e j -> p (e j)"),
-                        func=TANH,
-                    )
-                else:
-                    nc.scalar.activation(
-                        out=bounded[:, u, readers * c : readers * (c + 1), :],
-                        in_=banks[key][:].rearrange("p e j -> p j e"),
-                        func=TANH,
-                    )
-            if s == 0:
-                z_bf[s] = keep.tile([P, width * PACK], BF16, name="z_bf", tag="wd_raw", align_bytes=64)[:]
-            elif s < SHARED_STEPS:
-                z_bf[s] = stage[s - 1][0][:, 0 : width * PACK // 2].bitcast(BF16)
-            else:
-                z_bf[s] = z_bf[s - 2][:, 0 : width * PACK]
-            if s in SCALAR_STEPS:
-                z_rows = ring.tile([P, PACK, width], BF16, name="z_rows")
-                rows = bounded.rearrange("p u j e -> p (u j e)")
-                for t in range(PACK):
-                    nc.scalar.activation(
-                        out=z_rows[:, t, :],
-                        in_=rows[:, width * t : width * (t + 1)],
-                        func=COPY,
-                        scale=fresh_sb[:, PACK * b + t : PACK * b + t + 1],
-                    )
-                interleave(z_bf[s].rearrange("p (j t) -> p j t", t=PACK), z_rows[:])
-                return
-            for engine, cols, factors in (
-                (nc.vector, slice(0, width - share), fresh_ps[:, b, :]),
-                (nc.gpsimd, slice(width - share, width), fresh_sb[:, PACK * b : PACK * (b + 1)]),
-            ):
-                engine.tensor_tensor(
-                    z_bf[s].rearrange("p (j u e) -> p j u e", u=PACK // side, e=side)[:, cols],
-                    bounded.rearrange("p u j e -> p j u e")[:, cols],
-                    factors.rearrange("p (u e) -> p u e", e=side)
-                    .unsqueeze(1)
-                    .to_broadcast([P, cols.stop - cols.start, PACK // side, side]),
-                    MULT,
-                )
-
-        def quantise_z(s):
-            h, b, first, width = STEPS[s][:4]
-            cols = slice(first, first + width)
-            if s == HELD_STEP:
-                late_codes[s] = keep.tile([P, width], U32, name="z_late", tag="gate0", align_bytes=256)[:]
-            codes = late_codes.get(s, z_codes[h, b][:, cols])
-            nc.vector.quantize_mx(out=codes.bitcast(FP8X4), scales=z_sc[h, b][:, cols], in_=z_bf[s])
+        def quantise(codes, scales, src):
+            nc.vector.quantize_mx(out=codes.bitcast(FP8X4), scales=scales, in_=src)
 
         wd_codes = [held("wd_codes%d" % b, [P, N], U32) for b in range(2)]
         wd_sc = [held("wd_sc%d" % b, [P, N], U8) for b in range(2)]
-        wd_bf = [keep.tile([P, N, PACK], BF16, name="wd_bf", tag="wd_bf%d" % b, align_bytes=64) for b in range(2)]
+        for b in range(2):
+            interleave(region(0, b).rearrange("p (n t) -> p n t", t=PACK), wd_raw[:, b])
+        for b in range(2):
+            quantise(wd_codes[b][:], wd_sc[b][:], region(0, b))
 
-        def cast_wd(b):
-            interleave(wd_bf[b][:], wd_raw[:, b])
-
-        def quantise_wd(b):
-            nc.vector.quantize_mx(
-                out=wd_codes[b][:].bitcast(FP8X4), scales=wd_sc[b][:], in_=wd_bf[b][:].rearrange("p n t -> p (n t)")
-            )
-
-        def section_passes(acc, n, b, codes, scales, start, stop):
-            rows = slice(P * n, P * (n + 1))
-            width = codes.shape[1]
-            narrow = width if width == HALF else P
-            for first in range(0, width, narrow):
-                cols = slice(first, first + narrow)
+        def section_passes(bank, b, codes, scales):
+            for n in range(2):
+                rows = slice(P * n, P * (n + 1))
                 nc.tensor.matmul_mx(
-                    out=acc[:, cols],
+                    out=bank[:, n, :],
                     lhsT=w4_codes[:, b, 2 * P * n : 2 * P * (n + 1)].bitcast(FP4X4),
                     lhsT_scale=w4_sc[:, b, :].bitcast(U8)[:, rows],
-                    rhs=codes[:, cols].bitcast(FP8X4),
-                    rhs_scale=scales[:, cols],
-                    start=(start and first == 0),
+                    rhs=codes.bitcast(FP8X4),
+                    rhs_scale=scales,
+                    start=(b == 0 and n == 0),
                     stop=False,
                 )
-            nc.tensor.matmul_mx(
-                out=acc,
-                lhsT=wd_codes[b][:, rows].bitcast(FP8X4),
-                lhsT_scale=wd_sc[b][:, rows],
-                rhs=codes.bitcast(FP8X4),
-                rhs_scale=scales,
-                start=False,
-                stop=stop,
-            )
+                nc.tensor.matmul_mx(
+                    out=bank[:, n, :],
+                    lhsT=wd_codes[b][:, rows].bitcast(FP8X4),
+                    lhsT_scale=wd_sc[b][:, rows],
+                    rhs=codes.bitcast(FP8X4),
+                    rhs_scale=scales,
+                    start=False,
+                    stop=(b == 1 and n == 1),
+                )
 
+        def store(bank, q, cols, queue, scores=None):
+            width = cols.stop - cols.start
+            if scores is None:
+                scores = held("scores%d_%d" % (q, cols.start), [P, 2, width], F32)[:]
+            nc.vector.tensor_tensor(scores, bank[:], gate_sb[q][:, :, cols], MULT)
+            first = QUARTER * q + cols.start
+            queue.dma_start(out[:, first : first + width].rearrange("(n p) j -> p n j", p=P), scores)
+
+        whole = slice(0, QUARTER)
+        halves = [slice(P * c, P * (c + 1)) for c in range(2)]
         sums = {}
+        for q in range(4):
+            squash(q, 0)
+            weigh(nc.gpsimd, q, 0, region(q, 0), slice(0, SHARE[q]))
+            weigh(nc.vector, q, 0, region(q, 0), slice(SHARE[q], QUARTER))
+            codes = held("z_codes%d" % q, [P, 2, QUARTER], U32)
+            scales = [held("z_sc%d%d" % (q, b), [P, QUARTER], U8) for b in range(2)]
+            if q < 3:
+                squash(q, 1)
+                weigh(nc.vector, q, 1, region(q, 1), whole)
+                for b in range(2):
+                    quantise(codes[:, b, :], scales[b][:], region(q, b))
+                sums[q] = next_bank([P, 2, QUARTER])
+                for b in range(2):
+                    section_passes(sums[q], b, codes[:, b, :], scales[b][:])
 
-        def first_half(b):
-            for n in range(2):
-                if b == 0:
-                    sums[n] = psum_match.tile([P, HALF], F32, name="match_bank")
-                section_passes(sums[n][:], n, b, z_codes[0, b][:], z_sc[0, b][:], b == 0, b == 1)
-
-        def store_first_half():
-            for n in range(2):
-                scores = results.tile([P, HALF], F32, name="scores")
-                nc.vector.tensor_tensor(scores[:], sums[n][:], gate_sb[0][:, n, :], MULT)
-                nc.sync.dma_start(out[P * n : P * (n + 1), 0:HALF], scores[:])
-
-        pieces = {}
-
-        def piece_passes(s, b):
-            first, width = STEPS[s][2:4]
-            cols = slice(first, first + width)
-            codes = late_codes[s] if (s == HELD_STEP and b == 1) else z_codes[1, b][:, cols]
-            for n in range(2):
-                if b == 0:
-                    pieces[s, n] = psum_match.tile([P, width], F32, name="match_bank")
-                section_passes(pieces[s, n][:], n, b, codes, z_sc[1, b][:, cols], b == 0, b == 1)
-
-        def store_piece(s, n, queue):
-            first, width = STEPS[s][2:4]
-            scores = results.tile([P, width], F32, name="scores")
-            nc.vector.tensor_tensor(scores[:], pieces[s, n][:], gate_sb[1][:, n, first : first + width], MULT)
-            queue.dma_start(out[P * n : P * (n + 1), HALF + first : HALF + first + width], scores[:])
-
-        behind_step = {
-            0: [lambda: quantise_wd(1)],
-            2: [lambda: first_half(0)],
-            4: [lambda: first_half(1)],
-            7: [lambda: piece_passes(5, 0), lambda: piece_passes(5, 1)],
-            8: [lambda: piece_passes(7, 0), lambda: piece_passes(8, 0), lambda: piece_passes(7, 1)],
-        }
-        for b in range(2):
-            cast_wd(b)
-        quantise_wd(0)
-        for s in range(len(STEPS)):
-            if s == 6:
-                store_first_half()
-            match(s)
-            if s > 0:
-                quantise_z(s - 1)
-            for work in behind_step.get(s, []):
-                work()
-        store_piece(5, 0, nc.sync)
-        quantise_z(8)
-        piece_passes(8, 1)
-        store_piece(5, 1, nc.scalar)
-        for s in (7, 8):
-            store_piece(s, 0, nc.sync)
-            store_piece(s, 1, nc.scalar)
+        woven = held("woven", [P, P, PACK], F32)
+        nc.scalar.activation(out=woven[:], in_=narrow[0][:].rearrange("p t j -> p j t"), func=TANH)
+        rows32 = held("rows32", [P, PACK, P], F32)
+        nc.scalar.activation(out=rows32[:], in_=narrow[1][:], func=TANH)
+        rows16 = held("rows16", [P, PACK, P], BF16)
+        for t in range(PACK):
+            nc.scalar.activation(out=rows16[:, t, :], in_=rows32[:, t, :], func=COPY, scale=fresh_sb[:, 1, t : t + 1])
+        late = [region(3, 1)[:, 0:HALF], bounded[3, 0][:, 0:QUARTER].bitcast(BF16)]
+        store(sums[0], 0, whole, nc.sync)
+        nc.vector.tensor_tensor(
+            late[0].rearrange("p (j t) -> p j t", t=PACK),
+            woven[:],
+            fresh_ps[:, P - 1, :].unsqueeze(1).to_broadcast([P, P, PACK]),
+            MULT,
+        )
+        interleave(late[1].rearrange("p (j t) -> p j t", t=PACK), rows16[:])
+        quantise(codes[:, 0, :], scales[0][:], region(3, 0))
+        last = [next_bank([P, 2, P]) for c in range(2)]
+        for c in range(2):
+            section_passes(last[c], 0, codes[:, 0, halves[c]], scales[0][:, halves[c]])
+        for c in range(2):
+            quantise(codes[:, 1, halves[c]], scales[1][:, halves[c]], late[c])
+            section_passes(last[c], 1, codes[:, 1, halves[c]], scales[1][:, halves[c]])
+        store(sums[1], 1, whole, nc.sync, bounded[3, 0][:, QUARTER : QUARTER + HALF].rearrange("p (n j) -> p n j", n=2))
+        store(sums[2], 2, whole, nc.scalar)
+        store(last[0], 3, halves[0], nc.sync)
+        store(last[1], 3, halves[1], nc.scalar)

@@ -29,7 +29,8 @@ SC_FIRST = 96
 PLANE_ROW = (12, 0)
 UNIT = QUARTER * PACK
 SLIDE = 32
-SHARE = (160, 160, 160, 164)
+SHARE = (136, 136, 136, 136)
+LATE = 320
 
 
 def tile_list_fresh_news_sections_kernel(
@@ -55,7 +56,8 @@ def tile_list_fresh_news_sections_kernel(
         wd_raw = held("wd_raw", [P, 2, PACK, N], F32)
         gate_sb = [held("gate%d" % q, [P, 2, QUARTER], F32) for q in range(4)]
         fresh_rows = held("fresh_rows", [P, HALF], F32)
-        fresh_sb = held("fresh_sb", [P, 2, PACK], F32)
+        fresh_sb = held("fresh_sb", [P, PACK], F32)
+        fresh_wide = held("fresh_wide", [P, PACK * max(SHARE)], F32)
         identity = held("identity", [P, P], F32)
 
         nc.vector.memset(art_table_sc[0:SC_FIRST, :], 0)
@@ -76,7 +78,12 @@ def tile_list_fresh_news_sections_kernel(
         fresh_ps = psum.tile([P, P, PACK], F32, name="fresh_ps")
         for t in range(PACK):
             nc.tensor.transpose(fresh_ps[:, :, t], fresh_rows[:, t:HALF:PACK], identity[:])
-        nc.scalar.activation(out=fresh_sb[:], in_=fresh_ps[:, P - 2 : P, :], func=IDENTITY)
+        nc.scalar.activation(out=fresh_sb[:], in_=fresh_ps[:, P - 1, :], func=IDENTITY)
+        nc.scalar.activation(
+            out=fresh_wide[:].rearrange("p (j t) -> p j t", t=PACK),
+            in_=fresh_ps[:, P - 2, :].unsqueeze(1).to_broadcast([P, max(SHARE), PACK]),
+            func=IDENTITY,
+        )
         nc.sync.dma_start(rdr_table[0][:], table_words(tab2_words, 0))
         for a in range(2):
             nc.sync.dma_start(art_table[a][:], table_words(tab_words, a))
@@ -149,39 +156,37 @@ def tile_list_fresh_news_sections_kernel(
                     stop=(a == 1 and e == len(slots) - 1),
                 )
 
+        def narrow(q, b):
+            return b == 0 or q == 3
+
+        def bank_args(q, b, part):
+            if narrow(q, b):
+                return b, range(PACK), QUARTER * q + P * part, P
+            return b, (2 * part, 2 * part + 1), QUARTER * q, QUARTER
+
         matches = {}
 
-        def pair_args(key):
-            q, b, u = key
-            return b, (2 * u, 2 * u + 1), QUARTER * q, QUARTER
+        def open_bank(key):
+            matches[key] = next_bank([P, PACK, P] if narrow(*key[:2]) else [P, 2, QUARTER])
+            match_pass(matches[key], 0, *bank_args(*key))
 
-        def open_pair(key):
-            matches[key] = next_bank([P, 2, QUARTER])
-            match_pass(matches[key], 0, *pair_args(key))
-
-        def close_pair(key):
+        keys = [(q, b, part) for q in range(4) for b in range(2) for part in range(2)]
+        for key in keys[:BANKS]:
+            open_bank(key)
+        for key in keys:
             if key not in matches:
-                open_pair(key)
-            match_pass(matches[key], 1, *pair_args(key))
-
-        pairs = [(q, b, u) for q in range(4) for b in range(2) for u in range(2)]
-        for key in pairs[:BANKS]:
-            open_pair(key)
-        for key in pairs[:14]:
-            close_pair(key)
-        narrow = []
-        for c in range(2):
-            narrow.append(next_bank([P, PACK, P]))
-            for a in range(2):
-                match_pass(narrow[c], a, 1, range(PACK), 3 * QUARTER + P * c, P)
+                open_bank(key)
+            match_pass(matches[key], 1, *bank_args(*key))
 
         bounded = {}
 
         def squash(q, b):
             bounded[q, b] = held("bounded%d%d" % (q, b), [P, UNIT], F32)
-            for u in range(2):
+            for part in range(2):
                 nc.scalar.activation(
-                    out=bounded[q, b][:].rearrange("p (u j e) -> p u j e", u=2, e=2)[:, u], in_=matches[q, b, u][:].rearrange("p e j -> p j e"), func=TANH
+                    out=bounded[q, b][:, HALF * part : HALF * (part + 1)].rearrange("p (j e) -> p j e", e=PACK if b == 0 else 2),
+                    in_=matches[q, b, part][:].rearrange("p e j -> p j e"),
+                    func=TANH,
                 )
 
         values = held("values", [P, 2 * UNIT + 3 * SLIDE], BF16)
@@ -190,12 +195,21 @@ def tile_list_fresh_news_sections_kernel(
             first = (3 - q) * SLIDE + i * UNIT
             return values[:, first : first + UNIT]
 
-        def weigh(engine, q, b, dst, cols):
-            factors = fresh_ps[:, P - 2 + b, :] if engine is nc.vector else fresh_sb[:, b, :]
-            engine.tensor_tensor(
-                dst.rearrange("p (j u e) -> p j u e", u=2, e=2)[:, cols],
-                bounded[q, b][:].rearrange("p (u j e) -> p j u e", u=2, e=2)[:, cols],
-                factors.rearrange("p (u e) -> p u e", e=2).unsqueeze(1).to_broadcast([P, cols.stop - cols.start, 2, 2]),
+        def weigh_shared(q):
+            cut = PACK * SHARE[q]
+            nc.gpsimd.tensor_tensor(region(q, 0)[:, 0:cut], bounded[q, 0][:, 0:cut], fresh_wide[:, 0:cut], MULT)
+            nc.vector.tensor_tensor(
+                region(q, 0)[:, cut:].rearrange("p (j t) -> p j t", t=PACK),
+                bounded[q, 0][:, cut:].rearrange("p (j t) -> p j t", t=PACK),
+                fresh_ps[:, P - 2, :].unsqueeze(1).to_broadcast([P, QUARTER - SHARE[q], PACK]),
+                MULT,
+            )
+
+        def weigh_pairs(q):
+            nc.vector.tensor_tensor(
+                region(q, 1).rearrange("p (j u e) -> p j u e", u=2, e=2),
+                bounded[q, 1][:].rearrange("p (u j e) -> p j u e", u=2, e=2),
+                fresh_ps[:, P - 1, :].rearrange("p (u e) -> p u e", e=2).unsqueeze(1).to_broadcast([P, QUARTER, 2, 2]),
                 MULT,
             )
 
@@ -214,78 +228,71 @@ def tile_list_fresh_news_sections_kernel(
         for b in range(2):
             quantise(wd_codes[b][:], wd_sc[b][:], region(0, b))
 
-        def section_passes(bank, b, codes, scales):
-            for n in range(2):
-                rows = slice(P * n, P * (n + 1))
-                nc.tensor.matmul_mx(
-                    out=bank[:, n, :],
-                    lhsT=w4_codes[:, b, 2 * P * n : 2 * P * (n + 1)].bitcast(FP4X4),
-                    lhsT_scale=w4_sc[:, b, :].bitcast(U8)[:, rows],
-                    rhs=codes.bitcast(FP8X4),
-                    rhs_scale=scales,
-                    start=(b == 0 and n == 0),
-                    stop=False,
-                )
-                nc.tensor.matmul_mx(
-                    out=bank[:, n, :],
-                    lhsT=wd_codes[b][:, rows].bitcast(FP8X4),
-                    lhsT_scale=wd_sc[b][:, rows],
-                    rhs=codes.bitcast(FP8X4),
-                    rhs_scale=scales,
-                    start=False,
-                    stop=(b == 1 and n == 1),
-                )
+        def section_passes(acc, n, b, codes, scales, start, stop):
+            rows = slice(P * n, P * (n + 1))
+            nc.tensor.matmul_mx(
+                out=acc,
+                lhsT=w4_codes[:, b, 2 * P * n : 2 * P * (n + 1)].bitcast(FP4X4),
+                lhsT_scale=w4_sc[:, b, :].bitcast(U8)[:, rows],
+                rhs=codes.bitcast(FP8X4),
+                rhs_scale=scales,
+                start=start,
+                stop=False,
+            )
+            nc.tensor.matmul_mx(
+                out=acc,
+                lhsT=wd_codes[b][:, rows].bitcast(FP8X4),
+                lhsT_scale=wd_sc[b][:, rows],
+                rhs=codes.bitcast(FP8X4),
+                rhs_scale=scales,
+                start=False,
+                stop=stop,
+            )
 
-        def store(bank, q, cols, queue, scores=None):
-            width = cols.stop - cols.start
-            if scores is None:
-                scores = held("scores%d_%d" % (q, cols.start), [P, 2, width], F32)[:]
-            nc.vector.tensor_tensor(scores, bank[:], gate_sb[q][:, :, cols], MULT)
-            first = QUARTER * q + cols.start
-            queue.dma_start(out[:, first : first + width].rearrange("(n p) j -> p n j", p=P), scores)
+        def store(q, queue, scores):
+            nc.vector.tensor_tensor(scores, sums[q][:], gate_sb[q][:], MULT)
+            queue.dma_start(out[:, QUARTER * q : QUARTER * (q + 1)].rearrange("(n p) j -> p n j", p=P), scores)
 
-        whole = slice(0, QUARTER)
-        halves = [slice(P * c, P * (c + 1)) for c in range(2)]
         sums = {}
         for q in range(4):
             squash(q, 0)
-            weigh(nc.gpsimd, q, 0, region(q, 0), slice(0, SHARE[q]))
-            weigh(nc.vector, q, 0, region(q, 0), slice(SHARE[q], QUARTER))
+            weigh_shared(q)
             codes = held("z_codes%d" % q, [P, 2, QUARTER], U32)
             scales = [held("z_sc%d%d" % (q, b), [P, QUARTER], U8) for b in range(2)]
             if q < 3:
                 squash(q, 1)
-                weigh(nc.vector, q, 1, region(q, 1), whole)
+                weigh_pairs(q)
                 for b in range(2):
                     quantise(codes[:, b, :], scales[b][:], region(q, b))
                 sums[q] = next_bank([P, 2, QUARTER])
                 for b in range(2):
-                    section_passes(sums[q], b, codes[:, b, :], scales[b][:])
+                    for n in range(2):
+                        section_passes(sums[q][:, n, :], n, b, codes[:, b, :], scales[b][:], b + n == 0, b + n == 2)
 
-        woven = held("woven", [P, P, PACK], F32)
-        nc.scalar.activation(out=woven[:], in_=narrow[0][:].rearrange("p t j -> p j t"), func=TANH)
         rows32 = held("rows32", [P, PACK, P], F32)
-        nc.scalar.activation(out=rows32[:], in_=narrow[1][:], func=TANH)
+        nc.scalar.activation(out=rows32[:], in_=matches[3, 1, 0][:], func=TANH)
+        woven = held("woven", [P, P, PACK], F32)
+        nc.scalar.activation(out=woven[:], in_=matches[3, 1, 1][:].rearrange("p t j -> p j t"), func=TANH)
         rows16 = held("rows16", [P, PACK, P], BF16)
         for t in range(PACK):
-            nc.scalar.activation(out=rows16[:, t, :], in_=rows32[:, t, :], func=COPY, scale=fresh_sb[:, 1, t : t + 1])
-        late = [region(3, 1)[:, 0:HALF], bounded[3, 0][:, 0:QUARTER].bitcast(BF16)]
-        store(sums[0], 0, whole, nc.sync)
+            nc.scalar.activation(out=rows16[:, t, :], in_=rows32[:, t, :], func=COPY, scale=fresh_sb[:, t : t + 1])
+        late = bounded[3, 0][:, LATE : LATE + HALF].bitcast(BF16)
+        store(0, nc.sync, held("scores0", [P, 2, QUARTER], F32)[:])
         nc.vector.tensor_tensor(
-            late[0].rearrange("p (j t) -> p j t", t=PACK),
+            late[:, HALF:].rearrange("p (j t) -> p j t", t=PACK),
             woven[:],
             fresh_ps[:, P - 1, :].unsqueeze(1).to_broadcast([P, P, PACK]),
             MULT,
         )
-        interleave(late[1].rearrange("p (j t) -> p j t", t=PACK), rows16[:])
-        quantise(codes[:, 0, :], scales[0][:], region(3, 0))
-        last = [next_bank([P, 2, P]) for c in range(2)]
-        for c in range(2):
-            section_passes(last[c], 0, codes[:, 0, halves[c]], scales[0][:, halves[c]])
-        for c in range(2):
-            quantise(codes[:, 1, halves[c]], scales[1][:, halves[c]], late[c])
-            section_passes(last[c], 1, codes[:, 1, halves[c]], scales[1][:, halves[c]])
-        store(sums[1], 1, whole, nc.sync, bounded[3, 0][:, QUARTER : QUARTER + HALF].rearrange("p (n j) -> p n j", n=2))
-        store(sums[2], 2, whole, nc.scalar)
-        store(last[0], 3, halves[0], nc.sync)
-        store(last[1], 3, halves[1], nc.scalar)
+        interleave(late[:, 0:HALF].rearrange("p (j t) -> p j t", t=PACK), rows16[:])
+        last = [next_bank([P, QUARTER]) for n in range(2)]
+        for b in range(2):
+            quantise(codes[:, b, :], scales[b][:], late if b else region(3, 0))
+            for n in range(2):
+                section_passes(last[n][:], n, b, codes[:, b, :], scales[b][:], b == 0, b == 1)
+        store(1, nc.sync, fresh_wide[:, 0:HALF].rearrange("p (n j) -> p n j", n=2))
+        store(2, nc.scalar, held("scores2", [P, 2, QUARTER], F32)[:])
+        for n, queue in enumerate((nc.sync, nc.scalar)):
+            scores = held("scores3%d" % n, [P, QUARTER], F32)
+            nc.vector.tensor_tensor(scores[:], last[n][:], gate_sb[3][:, n, :], MULT)
+            queue.dma_start(out[P * n : P * (n + 1), 3 * QUARTER :], scores[:])

@@ -29,8 +29,7 @@ SC_FIRST = 96
 PLANE_ROW = (12, 0)
 UNIT = QUARTER * PACK
 SLIDE = 32
-SHARE = (136, 136, 136, 136)
-LATE = 320
+SHARE = (136, 136, 136, 144)
 
 
 def tile_list_fresh_news_sections_kernel(
@@ -276,7 +275,13 @@ def tile_list_fresh_news_sections_kernel(
         rows16 = held("rows16", [P, PACK, P], BF16)
         for t in range(PACK):
             nc.scalar.activation(out=rows16[:, t, :], in_=rows32[:, t, :], func=COPY, scale=fresh_sb[:, t : t + 1])
-        late = bounded[3, 0][:, LATE : LATE + HALF].bitcast(BF16)
+        late = held("late", [P, UNIT], BF16)[:]
+        nc.scalar.copy(
+            out=late[:, 0:HALF].rearrange("p (g i t) -> p g t i", i=4, t=PACK),
+            in_=rows16[:].rearrange("p t (g i) -> p g t i", i=4),
+        )
+        spilled = held("spilled", [P, QUARTER], F32)
+        nc.scalar.copy(out=spilled[:], in_=sums[1][:, 1, :])
         store(0, nc.sync, held("scores0", [P, 2, QUARTER], F32)[:])
         nc.vector.tensor_tensor(
             late[:, HALF:].rearrange("p (j t) -> p j t", t=PACK),
@@ -284,15 +289,19 @@ def tile_list_fresh_news_sections_kernel(
             fresh_ps[:, P - 1, :].unsqueeze(1).to_broadcast([P, P, PACK]),
             MULT,
         )
-        interleave(late[:, 0:HALF].rearrange("p (j t) -> p j t", t=PACK), rows16[:])
         last = [next_bank([P, QUARTER]) for n in range(2)]
         for b in range(2):
             quantise(codes[:, b, :], scales[b][:], late if b else region(3, 0))
             for n in range(2):
                 section_passes(last[n][:], n, b, codes[:, b, :], scales[b][:], b == 0, b == 1)
-        store(1, nc.sync, fresh_wide[:, 0:HALF].rearrange("p (n j) -> p n j", n=2))
-        store(2, nc.scalar, held("scores2", [P, 2, QUARTER], F32)[:])
-        for n, queue in enumerate((nc.sync, nc.scalar)):
+        scores = region(3, 0)[:, 0:HALF].bitcast(F32)
+        nc.gpsimd.tensor_tensor(scores, spilled[:], gate_sb[1][:, 1, :], MULT)
+        nc.scalar.dma_start(out[P:, QUARTER:HALF], scores)
+        scores = fresh_wide[:, 0:QUARTER]
+        nc.vector.tensor_tensor(scores, sums[1][:, 0, :], gate_sb[1][:, 0, :], MULT)
+        nc.sync.dma_start(out[0:P, QUARTER:HALF], scores)
+        store(2, nc.sync, held("scores2", [P, 2, QUARTER], F32)[:])
+        for n, queue in enumerate((nc.scalar, nc.sync)):
             scores = held("scores3%d" % n, [P, QUARTER], F32)
             nc.vector.tensor_tensor(scores[:], last[n][:], gate_sb[3][:, n, :], MULT)
             queue.dma_start(out[P * n : P * (n + 1), 3 * QUARTER :], scores[:])

@@ -30,6 +30,7 @@ PLANE_ROW = (12, 0)
 UNIT = QUARTER * PACK
 SLIDE = 32
 SHARE = (136, 136, 136, 144)
+EARLY = 1536
 
 
 def tile_list_fresh_news_sections_kernel(
@@ -86,7 +87,7 @@ def tile_list_fresh_news_sections_kernel(
         nc.sync.dma_start(rdr_table[0][:], table_words(tab2_words, 0))
         for a in range(2):
             nc.sync.dma_start(art_table[a][:], table_words(tab_words, a))
-        nc.sync.dma_start(rdr_table[1][:, 0:T], table_words(tab2_words, 1)[:, 0:T])
+        nc.sync.dma_start(rdr_table[1][:, 0:EARLY], table_words(tab2_words, 1)[:, 0:EARLY])
 
         art_sc_listed = held("art_sc_listed", [P, S], U8)
         rdr_sc_listed = held("rdr_sc_listed", [P, S2], U8)
@@ -104,7 +105,7 @@ def tile_list_fresh_news_sections_kernel(
         for q in range(QUADRANTS - 1):
             row = 32 * q + PLANE_ROW[0]
             nc.sync.dma_start(planes[0][row : row + 4, :], planes[0][SC_FIRST + 4 * q : SC_FIRST + 4 * q + 4, :])
-        nc.sync.dma_start(rdr_table[1][:, T:T2], table_words(tab2_words, 1)[:, T:T2])
+        nc.sync.dma_start(rdr_table[1][:, EARLY:], table_words(tab2_words, 1)[:, EARLY:])
         for r in range(4):
             nc.sync.dma_start(planes[1][r:P:32, :], planes[0][SC_FIRST + 16 + r : P : 4, :])
 
@@ -156,7 +157,7 @@ def tile_list_fresh_news_sections_kernel(
                 )
 
         def narrow(q, b):
-            return b == 0 or q == 3
+            return b == 1 and q == 3
 
         def bank_args(q, b, part):
             if narrow(q, b):
@@ -183,7 +184,7 @@ def tile_list_fresh_news_sections_kernel(
             bounded[q, b] = held("bounded%d%d" % (q, b), [P, UNIT], F32)
             for part in range(2):
                 nc.scalar.activation(
-                    out=bounded[q, b][:, HALF * part : HALF * (part + 1)].rearrange("p (j e) -> p j e", e=PACK if b == 0 else 2),
+                    out=bounded[q, b][:, HALF * part : HALF * (part + 1)].rearrange("p (j e) -> p j e", e=2),
                     in_=matches[q, b, part][:].rearrange("p e j -> p j e"),
                     func=TANH,
                 )
@@ -194,23 +195,24 @@ def tile_list_fresh_news_sections_kernel(
             first = (3 - q) * SLIDE + i * UNIT
             return values[:, first : first + UNIT]
 
-        def weigh_shared(q):
-            cut = PACK * SHARE[q]
-            nc.gpsimd.tensor_tensor(region(q, 0)[:, 0:cut], bounded[q, 0][:, 0:cut], fresh_wide[:, 0:cut], MULT)
-            nc.vector.tensor_tensor(
-                region(q, 0)[:, cut:].rearrange("p (j t) -> p j t", t=PACK),
-                bounded[q, 0][:, cut:].rearrange("p (j t) -> p j t", t=PACK),
-                fresh_ps[:, P - 2, :].unsqueeze(1).to_broadcast([P, QUARTER - SHARE[q], PACK]),
+        def weigh(engine, q, b, cols, factors):
+            engine.tensor_tensor(
+                region(q, b).rearrange("p (j u e) -> p j u e", u=2, e=2)[:, cols],
+                bounded[q, b][:].rearrange("p (u j e) -> p j u e", u=2, e=2)[:, cols],
+                factors,
                 MULT,
             )
 
+        def spread(b, count):
+            return fresh_ps[:, P - 2 + b, :].rearrange("p (u e) -> p u e", e=2).unsqueeze(1).to_broadcast([P, count, 2, 2])
+
+        def weigh_shared(q):
+            wide = fresh_wide[:].rearrange("p (j u e) -> p j u e", u=2, e=2)[:, 0 : SHARE[q]]
+            weigh(nc.gpsimd, q, 0, slice(0, SHARE[q]), wide)
+            weigh(nc.vector, q, 0, slice(SHARE[q], QUARTER), spread(0, QUARTER - SHARE[q]))
+
         def weigh_pairs(q):
-            nc.vector.tensor_tensor(
-                region(q, 1).rearrange("p (j u e) -> p j u e", u=2, e=2),
-                bounded[q, 1][:].rearrange("p (u j e) -> p j u e", u=2, e=2),
-                fresh_ps[:, P - 1, :].rearrange("p (u e) -> p u e", e=2).unsqueeze(1).to_broadcast([P, QUARTER, 2, 2]),
-                MULT,
-            )
+            weigh(nc.vector, q, 1, slice(0, QUARTER), spread(1, QUARTER))
 
         def interleave(columns, rows):
             nc.vector.tensor_copy(

@@ -30,7 +30,6 @@ PLANE_ROW = (12, 0)
 UNIT = QUARTER * PACK
 SLIDE = 32
 SHARE = (136, 136, 136, 144)
-EARLY = 1536
 
 
 def tile_list_fresh_news_sections_kernel(
@@ -41,12 +40,12 @@ def tile_list_fresh_news_sections_kernel(
         keep = ctx.enter_context(tc.tile_pool(name="keep", bufs=1))
         psum = ctx.enter_context(tc.psum_pool(name="psum", bufs=1))
 
-        def held(name, shape, dtype, tag=None):
-            return keep.tile(shape, dtype, name=name, tag=tag or name, align_bytes=256)
+        def held(name, shape, dtype):
+            return keep.tile(shape, dtype, name=name, tag=name, align_bytes=256)
 
         art_list = keep.tile([P, S // 16], U16, name="art_list")
         rdr_list = keep.tile([P, S2 // 16], U16, name="rdr_list")
-        art_table = [held("art_table%d" % a, [P, T], I32) for a in range(2)]
+        art_table = held("art_table", [P, 2 * T], I32)
         rdr_table = [held("rdr_table%d" % a, [P, T2], I32) for a in range(2)]
         art_table_sc = held("art_table_sc", [P, T // 4], I32)
         rdr_table_sc = held("rdr_table_sc", [P, T2 // 4], I32)
@@ -68,12 +67,12 @@ def tile_list_fresh_news_sections_kernel(
         nc.gpsimd.memset(planes[1][:], 0)
 
         def table_words(table, a):
-            return table[a].rearrange("p t i -> p (t i)").bitcast(I32)
+            return table[a].rearrange("p w t -> p (w t)").bitcast(I32)
 
         nc.sync.dma_start(art_list[:], offs)
-        nc.scalar.dma_start(art_table_sc[SC_FIRST:P, :], tab_scales.rearrange("a q t -> (a q) t").bitcast(I32))
+        nc.scalar.dma_start(art_table_sc[SC_FIRST:P, :], tab_scales.rearrange("a s w -> (a s) w").bitcast(I32))
         nc.sync.dma_start(rdr_list[:], offs2)
-        nc.sync.dma_start(rdr_table_sc[SC_FIRST:P, :], tab2_scales.rearrange("a q t -> (a q) t").bitcast(I32))
+        nc.sync.dma_start(rdr_table_sc[SC_FIRST:P, :], tab2_scales.rearrange("a s w -> (a s) w").bitcast(I32))
         nc.sync.dma_start(fresh_rows[P - 2 : P, :], fresh.rearrange("(b i) -> b i", b=2))
         fresh_ps = psum.tile([P, P, PACK], F32, name="fresh_ps")
         for t in range(PACK):
@@ -84,16 +83,21 @@ def tile_list_fresh_news_sections_kernel(
             in_=fresh_ps[:, P - 2, :].unsqueeze(1).to_broadcast([P, max(SHARE), PACK]),
             func=IDENTITY,
         )
+        nc.sync.dma_start(
+            art_table[:].rearrange("p (a w) -> p a w", a=2), tab_words.rearrange("a p w t -> p a (w t)").bitcast(I32)
+        )
         nc.sync.dma_start(rdr_table[0][:], table_words(tab2_words, 0))
-        for a in range(2):
-            nc.sync.dma_start(art_table[a][:], table_words(tab_words, a))
-        nc.sync.dma_start(rdr_table[1][:, 0:EARLY], table_words(tab2_words, 1)[:, 0:EARLY])
 
         art_sc_listed = held("art_sc_listed", [P, S], U8)
         rdr_sc_listed = held("rdr_sc_listed", [P, S2], U8)
         art = [held("art%d" % a, [P, S], U32) for a in range(2)]
-        rdr0 = held("rdr0", [P, S2], U32)
-        rdr1 = [held("rdr1%d" % h, [P, HALF], U32) for h in range(2)]
+        rdr = [[held("rdr%d%d" % (a, h), [P, HALF], U32) for h in range(2)] for a in range(2)]
+
+        def gather_readers(a):
+            for h in range(2):
+                nc.vector.tensor_copy(
+                    rdr[a][h][:], rdr_table[a][:].bitcast(U32).indirect(rdr_list[:, 32 * h : 32 * (h + 1)])
+                )
 
         nc.vector.tensor_copy(art_sc_listed[:], art_table_sc[:].bitcast(U8).indirect(art_list[:]))
         nc.vector.tensor_copy(rdr_sc_listed[:], rdr_table_sc[:].bitcast(U8).indirect(rdr_list[:]))
@@ -102,47 +106,44 @@ def tile_list_fresh_news_sections_kernel(
             art_sc_listed[:].rearrange("p (b m t) -> p b t m", b=2, t=PACK),
         )
         nc.vector.tensor_copy(planes[0][:, S // 4 :], rdr_sc_listed[:].bitcast(I32))
-        for q in range(QUADRANTS - 1):
-            row = 32 * q + PLANE_ROW[0]
-            nc.sync.dma_start(planes[0][row : row + 4, :], planes[0][SC_FIRST + 4 * q : SC_FIRST + 4 * q + 4, :])
-        nc.sync.dma_start(rdr_table[1][:, EARLY:], table_words(tab2_words, 1)[:, EARLY:])
+        for c in range(QUADRANTS - 1):
+            row = 32 * c + PLANE_ROW[0]
+            nc.sync.dma_start(planes[0][row : row + 4, :], planes[0][SC_FIRST + 4 * c : SC_FIRST + 4 * c + 4, :])
+        nc.sync.dma_start(rdr_table[1][:], table_words(tab2_words, 1))
         for r in range(4):
             nc.sync.dma_start(planes[1][r:P:32, :], planes[0][SC_FIRST + 16 + r : P : 4, :])
 
-        nc.vector.tensor_copy(rdr0[:], rdr_table[0][:].bitcast(U32).indirect(rdr_list[:]))
         for a in range(2):
             nc.vector.tensor_copy(
                 art[a][:].rearrange("p (b t m) -> p b m t", b=2, t=PACK),
-                art_table[a][:].bitcast(U32).indirect(art_list[:]),
+                art_table[:, T * a : T * (a + 1)].bitcast(U32).indirect(art_list[:]),
             )
+        gather_readers(0)
 
         nc.sync.dma_start(
             wd_raw[:].rearrange("p b t n -> p b (t n)"), wd.rearrange("(b p t) n -> p b (t n)", b=2, t=PACK)
         )
-        nc.sync.dma_start(w4_codes[:].bitcast(I32), w4_words.rearrange("b p c -> p b c").bitcast(I32))
-        for q in range(QUADRANTS):
+        nc.sync.dma_start(w4_codes[:].bitcast(I32), w4_words.rearrange("b p w -> p b w").bitcast(I32))
+        for c in range(QUADRANTS):
             nc.sync.dma_start(
-                w4_sc[32 * q : 32 * q + 4, :, :],
-                w4_scales[:, 4 * q : 4 * q + 4, :].rearrange("b r c -> r b c").bitcast(I32),
+                w4_sc[32 * c : 32 * c + 4, :, :],
+                w4_scales[:, 4 * c : 4 * c + 4, :].rearrange("b r n -> r b n").bitcast(I32),
             )
         for q in range(4):
             nc.sync.dma_start(
                 gate_sb[q][:], gate[:, QUARTER * q : QUARTER * (q + 1)].rearrange("(n p) j -> p n j", p=P)
             )
 
-        for h in range(2):
-            nc.vector.tensor_copy(
-                rdr1[h][:], rdr_table[1][:].bitcast(U32).indirect(rdr_list[:, 32 * h : 32 * (h + 1)])
-            )
+        gather_readers(1)
 
-        turn = []
+        taken = []
 
         def next_bank(shape):
-            turn.append(0)
-            return psum.tile(shape, F32, name="bank", tag="bank%d" % ((len(turn) - 1) % BANKS))
+            taken.append(psum.tile(shape, F32, name="bank", tag="bank%d" % (len(taken) % BANKS)))
+            return taken[-1]
 
         def match_pass(bank, a, b, slots, first, width):
-            words = rdr0[:, first : first + width] if a == 0 else rdr1[first // HALF][:, first % HALF : first % HALF + width]
+            words = rdr[a][first // HALF][:, first % HALF : first % HALF + width]
             plane = planes[a][:].bitcast(U8)
             for e, t in enumerate(slots):
                 col = HALF * b + P * t
@@ -191,9 +192,9 @@ def tile_list_fresh_news_sections_kernel(
 
         values = held("values", [P, 2 * UNIT + 3 * SLIDE], BF16)
 
-        def region(q, i):
-            first = (3 - q) * SLIDE + i * UNIT
-            return values[:, first : first + UNIT]
+        def region(q, b):
+            base = (3 - q) * SLIDE + b * UNIT
+            return values[:, base : base + UNIT]
 
         def weigh(engine, q, b, cols, factors):
             engine.tensor_tensor(
@@ -204,20 +205,13 @@ def tile_list_fresh_news_sections_kernel(
             )
 
         def spread(b, count):
-            return fresh_ps[:, P - 2 + b, :].rearrange("p (u e) -> p u e", e=2).unsqueeze(1).to_broadcast([P, count, 2, 2])
+            factors = fresh_ps[:, P - 2 + b, :].rearrange("p (u e) -> p u e", e=2)
+            return factors.unsqueeze(1).to_broadcast([P, count, 2, 2])
 
         def weigh_shared(q):
             wide = fresh_wide[:].rearrange("p (j u e) -> p j u e", u=2, e=2)[:, 0 : SHARE[q]]
             weigh(nc.gpsimd, q, 0, slice(0, SHARE[q]), wide)
             weigh(nc.vector, q, 0, slice(SHARE[q], QUARTER), spread(0, QUARTER - SHARE[q]))
-
-        def weigh_pairs(q):
-            weigh(nc.vector, q, 1, slice(0, QUARTER), spread(1, QUARTER))
-
-        def interleave(columns, rows):
-            nc.vector.tensor_copy(
-                out=columns.rearrange("p (g i) t -> p g t i", i=4), in_=rows.rearrange("p t (g i) -> p g t i", i=4)
-            )
 
         def quantise(codes, scales, src):
             nc.vector.quantize_mx(out=codes.bitcast(FP8X4), scales=scales, in_=src)
@@ -225,16 +219,19 @@ def tile_list_fresh_news_sections_kernel(
         wd_codes = [held("wd_codes%d" % b, [P, N], U32) for b in range(2)]
         wd_sc = [held("wd_sc%d" % b, [P, N], U8) for b in range(2)]
         for b in range(2):
-            interleave(region(0, b).rearrange("p (n t) -> p n t", t=PACK), wd_raw[:, b])
+            nc.vector.tensor_copy(
+                out=region(0, b).rearrange("p (g x t) -> p g t x", x=4, t=PACK),
+                in_=wd_raw[:, b].rearrange("p t (g x) -> p g t x", x=4),
+            )
         for b in range(2):
             quantise(wd_codes[b][:], wd_sc[b][:], region(0, b))
 
         def section_passes(acc, n, b, codes, scales, start, stop):
-            rows = slice(P * n, P * (n + 1))
+            sections = slice(P * n, P * (n + 1))
             nc.tensor.matmul_mx(
                 out=acc,
                 lhsT=w4_codes[:, b, 2 * P * n : 2 * P * (n + 1)].bitcast(FP4X4),
-                lhsT_scale=w4_sc[:, b, :].bitcast(U8)[:, rows],
+                lhsT_scale=w4_sc[:, b, :].bitcast(U8)[:, sections],
                 rhs=codes.bitcast(FP8X4),
                 rhs_scale=scales,
                 start=start,
@@ -242,17 +239,18 @@ def tile_list_fresh_news_sections_kernel(
             )
             nc.tensor.matmul_mx(
                 out=acc,
-                lhsT=wd_codes[b][:, rows].bitcast(FP8X4),
-                lhsT_scale=wd_sc[b][:, rows],
+                lhsT=wd_codes[b][:, sections].bitcast(FP8X4),
+                lhsT_scale=wd_sc[b][:, sections],
                 rhs=codes.bitcast(FP8X4),
                 rhs_scale=scales,
                 start=False,
                 stop=stop,
             )
 
-        def store(q, queue, scores):
-            nc.vector.tensor_tensor(scores, sums[q][:], gate_sb[q][:], MULT)
-            queue.dma_start(out[:, QUARTER * q : QUARTER * (q + 1)].rearrange("(n p) j -> p n j", p=P), scores)
+        def store_quarter(q):
+            scores = held("scores%d" % q, [P, 2, QUARTER], F32)
+            nc.vector.tensor_tensor(scores[:], sums[q][:], gate_sb[q][:], MULT)
+            nc.sync.dma_start(out[:, QUARTER * q : QUARTER * (q + 1)].rearrange("(n p) j -> p n j", p=P), scores[:])
 
         sums = {}
         for q in range(4):
@@ -262,7 +260,7 @@ def tile_list_fresh_news_sections_kernel(
             scales = [held("z_sc%d%d" % (q, b), [P, QUARTER], U8) for b in range(2)]
             if q < 3:
                 squash(q, 1)
-                weigh_pairs(q)
+                weigh(nc.vector, q, 1, slice(0, QUARTER), spread(1, QUARTER))
                 for b in range(2):
                     quantise(codes[:, b, :], scales[b][:], region(q, b))
                 sums[q] = next_bank([P, 2, QUARTER])
@@ -279,12 +277,12 @@ def tile_list_fresh_news_sections_kernel(
             nc.scalar.activation(out=rows16[:, t, :], in_=rows32[:, t, :], func=COPY, scale=fresh_sb[:, t : t + 1])
         late = held("late", [P, UNIT], BF16)[:]
         nc.scalar.copy(
-            out=late[:, 0:HALF].rearrange("p (g i t) -> p g t i", i=4, t=PACK),
-            in_=rows16[:].rearrange("p t (g i) -> p g t i", i=4),
+            out=late[:, 0:HALF].rearrange("p (g x t) -> p g t x", x=4, t=PACK),
+            in_=rows16[:].rearrange("p t (g x) -> p g t x", x=4),
         )
         spilled = held("spilled", [P, QUARTER], F32)
         nc.scalar.copy(out=spilled[:], in_=sums[1][:, 1, :])
-        store(0, nc.sync, held("scores0", [P, 2, QUARTER], F32)[:])
+        store_quarter(0)
         nc.vector.tensor_tensor(
             late[:, HALF:].rearrange("p (j t) -> p j t", t=PACK),
             woven[:],
@@ -296,13 +294,13 @@ def tile_list_fresh_news_sections_kernel(
             quantise(codes[:, b, :], scales[b][:], late if b else region(3, 0))
             for n in range(2):
                 section_passes(last[n][:], n, b, codes[:, b, :], scales[b][:], b == 0, b == 1)
-        scores = region(3, 0)[:, 0:HALF].bitcast(F32)
-        nc.gpsimd.tensor_tensor(scores, spilled[:], gate_sb[1][:, 1, :], MULT)
-        nc.scalar.dma_start(out[P:, QUARTER:HALF], scores)
-        scores = fresh_wide[:, 0:QUARTER]
-        nc.vector.tensor_tensor(scores, sums[1][:, 0, :], gate_sb[1][:, 0, :], MULT)
-        nc.sync.dma_start(out[0:P, QUARTER:HALF], scores)
-        store(2, nc.sync, held("scores2", [P, 2, QUARTER], F32)[:])
+        lower = region(3, 0)[:, 0:HALF].bitcast(F32)
+        nc.gpsimd.tensor_tensor(lower, spilled[:], gate_sb[1][:, 1, :], MULT)
+        nc.scalar.dma_start(out[P:, QUARTER:HALF], lower)
+        upper = fresh_wide[:, 0:QUARTER]
+        nc.vector.tensor_tensor(upper, sums[1][:, 0, :], gate_sb[1][:, 0, :], MULT)
+        nc.sync.dma_start(out[0:P, QUARTER:HALF], upper)
+        store_quarter(2)
         for n, queue in enumerate((nc.scalar, nc.sync)):
             scores = held("scores3%d" % n, [P, QUARTER], F32)
             nc.vector.tensor_tensor(scores[:], last[n][:], gate_sb[3][:, n, :], MULT)

@@ -15,6 +15,7 @@ U8 = mybir.dt.uint8
 FP8X4 = mybir.dt.float8_e4m3fn_x4
 FP4X4 = mybir.dt.float4_e2m1fn_x4
 MULT = mybir.AluOpType.mult
+ADD = mybir.AluOpType.add
 TANH = mybir.ActivationFunctionType.Tanh
 IDENTITY = mybir.ActivationFunctionType.Identity
 COPY = mybir.ActivationFunctionType.Copy
@@ -27,9 +28,10 @@ QUADRANTS = 4
 BANKS = 7
 SC_FIRST = 96
 PLANE_ROW = (12, 0)
+UNITS = 8
 UNIT = QUARTER * PACK
-SLIDE = 32
-SHARE = (136, 136, 136, 144)
+SHARE = {2: 88, 4: 136, 6: 112}
+OWN = 224
 
 
 def tile_list_fresh_news_sections_kernel(
@@ -38,25 +40,26 @@ def tile_list_fresh_news_sections_kernel(
     nc = tc.nc
     with ExitStack() as ctx:
         keep = ctx.enter_context(tc.tile_pool(name="keep", bufs=1))
+        placed = ctx.enter_context(tc.tile_pool(name="placed", bufs=1))
         psum = ctx.enter_context(tc.psum_pool(name="psum", bufs=1))
 
-        def held(name, shape, dtype):
-            return keep.tile(shape, dtype, name=name, tag=name, align_bytes=256)
+        def held(name, shape, dtype, over=None):
+            return keep.tile(shape, dtype, name=name, tag=over or name, align_bytes=256)
 
         art_list = keep.tile([P, S // 16], U16, name="art_list")
         rdr_list = keep.tile([P, S2 // 16], U16, name="rdr_list")
-        art_table = held("art_table", [P, 2 * T], I32)
+        art_table = [held("art_table%d" % a, [P, T], I32) for a in range(2)]
         rdr_table = [held("rdr_table%d" % a, [P, T2], I32) for a in range(2)]
         art_table_sc = held("art_table_sc", [P, T // 4], I32)
         rdr_table_sc = held("rdr_table_sc", [P, T2 // 4], I32)
         planes = [held("plane%d" % a, [P, (S + S2) // 4], I32) for a in range(2)]
         w4_sc = held("w4_sc", [P, 2, N // 4], I32)
         w4_codes = held("w4_codes", [P, 2, 2 * N], U8)
-        wd_raw = held("wd_raw", [P, 2, PACK, N], F32)
+        wd_raw = placed.tile([P, 2, PACK, N], F32, name="wd_raw", align_bytes=256, offset=0)
         gate_sb = [held("gate%d" % q, [P, 2, QUARTER], F32) for q in range(4)]
         fresh_rows = held("fresh_rows", [P, HALF], F32)
         fresh_sb = held("fresh_sb", [P, PACK], F32)
-        fresh_wide = held("fresh_wide", [P, PACK * max(SHARE)], F32)
+        fresh_wide = held("fresh_wide", [P, PACK * max(SHARE.values())], F32)
         identity = held("identity", [P, P], F32)
 
         nc.vector.memset(art_table_sc[0:SC_FIRST, :], 0)
@@ -80,24 +83,27 @@ def tile_list_fresh_news_sections_kernel(
         nc.scalar.activation(out=fresh_sb[:], in_=fresh_ps[:, P - 1, :], func=IDENTITY)
         nc.scalar.activation(
             out=fresh_wide[:].rearrange("p (j t) -> p j t", t=PACK),
-            in_=fresh_ps[:, P - 2, :].unsqueeze(1).to_broadcast([P, max(SHARE), PACK]),
+            in_=fresh_ps[:, P - 2, :].unsqueeze(1).to_broadcast([P, max(SHARE.values()), PACK]),
             func=IDENTITY,
         )
-        nc.sync.dma_start(
-            art_table[:].rearrange("p (a w) -> p a w", a=2), tab_words.rearrange("a p w t -> p a (w t)").bitcast(I32)
-        )
+        nc.sync.dma_start(art_table[0][:], table_words(tab_words, 0))
         nc.sync.dma_start(rdr_table[0][:], table_words(tab2_words, 0))
+        nc.sync.dma_start(art_table[1][:], table_words(tab_words, 1))
 
         art_sc_listed = held("art_sc_listed", [P, S], U8)
         rdr_sc_listed = held("rdr_sc_listed", [P, S2], U8)
         art = [held("art%d" % a, [P, S], U32) for a in range(2)]
-        rdr = [[held("rdr%d%d" % (a, h), [P, HALF], U32) for h in range(2)] for a in range(2)]
+        pieces = (((0, HALF), (HALF, HALF)), ((0, QUARTER), (QUARTER, QUARTER), (HALF, HALF)))
+        rdr = {}
 
         def gather_readers(a):
-            for h in range(2):
+            for first, count in pieces[a]:
+                words = held("rdr%d_%d" % (a, first), [P, count], U32)
                 nc.vector.tensor_copy(
-                    rdr[a][h][:], rdr_table[a][:].bitcast(U32).indirect(rdr_list[:, 32 * h : 32 * (h + 1)])
+                    words[:], rdr_table[a][:].bitcast(U32).indirect(rdr_list[:, first // 16 : (first + count) // 16])
                 )
+                for q in range(first // QUARTER, (first + count) // QUARTER):
+                    rdr[a, q] = words[:, QUARTER * q - first : QUARTER * (q + 1) - first]
 
         nc.vector.tensor_copy(art_sc_listed[:], art_table_sc[:].bitcast(U8).indirect(art_list[:]))
         nc.vector.tensor_copy(rdr_sc_listed[:], rdr_table_sc[:].bitcast(U8).indirect(rdr_list[:]))
@@ -113,12 +119,15 @@ def tile_list_fresh_news_sections_kernel(
         for r in range(4):
             nc.sync.dma_start(planes[1][r:P:32, :], planes[0][SC_FIRST + 16 + r : P : 4, :])
 
-        for a in range(2):
+        def gather_articles(a):
             nc.vector.tensor_copy(
                 art[a][:].rearrange("p (b t m) -> p b m t", b=2, t=PACK),
-                art_table[:, T * a : T * (a + 1)].bitcast(U32).indirect(art_list[:]),
+                art_table[a][:].bitcast(U32).indirect(art_list[:]),
             )
+
+        gather_articles(0)
         gather_readers(0)
+        gather_articles(1)
 
         nc.sync.dma_start(
             wd_raw[:].rearrange("p b t n -> p b (t n)"), wd.rearrange("(b p t) n -> p b (t n)", b=2, t=PACK)
@@ -142,89 +151,86 @@ def tile_list_fresh_news_sections_kernel(
             taken.append(psum.tile(shape, F32, name="bank", tag="bank%d" % (len(taken) % BANKS)))
             return taken[-1]
 
-        def match_pass(bank, a, b, slots, first, width):
-            words = rdr[a][first // HALF][:, first % HALF : first % HALF + width]
-            plane = planes[a][:].bitcast(U8)
-            for e, t in enumerate(slots):
-                col = HALF * b + P * t
-                nc.tensor.matmul_mx(
-                    out=bank[:, e, :],
-                    lhsT=art[a][:, col : col + P].bitcast(FP8X4),
-                    lhsT_scale=plane[PLANE_ROW[a] :, col : col + P],
-                    rhs=words.bitcast(FP8X4),
-                    rhs_scale=plane[PLANE_ROW[a] :, S + first : S + first + width],
-                    start=(a == 0 and e == 0),
-                    stop=(a == 1 and e == len(slots) - 1),
-                )
-
-        def narrow(q, b):
-            return b == 1 and q == 3
-
-        def bank_args(q, b, part):
-            if narrow(q, b):
-                return b, range(PACK), QUARTER * q + P * part, P
-            return b, (2 * part, 2 * part + 1), QUARTER * q, QUARTER
-
         matches = {}
 
-        def open_bank(key):
-            matches[key] = next_bank([P, PACK, P] if narrow(*key[:2]) else [P, 2, QUARTER])
-            match_pass(matches[key], 0, *bank_args(*key))
+        def match_pass(a, u, part):
+            q, b = divmod(u, 2)
+            if a == 0:
+                matches[u, part] = next_bank([P, 2, QUARTER])
+            plane = planes[a][:].bitcast(U8)
+            for e in range(2):
+                col = HALF * b + P * (2 * part + e)
+                nc.tensor.matmul_mx(
+                    out=matches[u, part][:, e, :],
+                    lhsT=art[a][:, col : col + P].bitcast(FP8X4),
+                    lhsT_scale=plane[PLANE_ROW[a] :, col : col + P],
+                    rhs=rdr[a, q].bitcast(FP8X4),
+                    rhs_scale=plane[PLANE_ROW[a] :, S + QUARTER * q : S + QUARTER * (q + 1)],
+                    start=(a == 0 and e == 0),
+                    stop=(a == 1 and e == 1),
+                )
 
-        keys = [(q, b, part) for q in range(4) for b in range(2) for part in range(2)]
+        keys = [(u, part) for u in range(UNITS) for part in range(2)]
         for key in keys[:BANKS]:
-            open_bank(key)
+            match_pass(0, *key)
         for key in keys:
             if key not in matches:
-                open_bank(key)
-            match_pass(matches[key], 1, *bank_args(*key))
+                match_pass(0, *key)
+            match_pass(1, *key)
 
         bounded = {}
 
-        def squash(q, b):
-            bounded[q, b] = held("bounded%d%d" % (q, b), [P, UNIT], F32)
+        def squash(u):
+            bounded[u] = held("bounded%d" % u, [P, UNIT], F32)
             for part in range(2):
                 nc.scalar.activation(
-                    out=bounded[q, b][:, HALF * part : HALF * (part + 1)].rearrange("p (j e) -> p j e", e=2),
-                    in_=matches[q, b, part][:].rearrange("p e j -> p j e"),
+                    out=bounded[u][:, HALF * part : HALF * (part + 1)].rearrange("p (j e) -> p j e", e=2),
+                    in_=matches[u, part][:].rearrange("p e j -> p j e"),
                     func=TANH,
                 )
 
-        values = held("values", [P, 2 * UNIT + 3 * SLIDE], BF16)
+        wd_round = held("wd_round", [P, 2 * UNIT], BF16, over="rdr_table1")
+        nc.gpsimd.tensor_scalar(
+            wd_round[:].rearrange("p (b n t) -> p b n t", b=2, t=PACK),
+            wd_raw[:].rearrange("p b t n -> p b n t"),
+            1.0,
+            0.0,
+            MULT,
+            ADD,
+        )
 
-        def region(q, b):
-            base = (3 - q) * SLIDE + b * UNIT
-            return values[:, base : base + UNIT]
+        values = held("values", [P, 3 * UNIT], BF16)
+        late = held("late", [P, UNIT], BF16)
+        shared = 2 * UNIT - PACK * SHARE[2]
+        places = [values[:, UNIT : 2 * UNIT], values[:, 0:UNIT], values[:, shared : shared + UNIT], wd_round[:, 0:UNIT]]
 
-        def weigh(engine, q, b, cols, factors):
+        def region(u):
+            if u == UNITS - 1:
+                return late[:]
+            return places[u if u < 4 else 2 + u % 2]
+
+        def weigh(engine, u, cols, factors):
             engine.tensor_tensor(
-                region(q, b).rearrange("p (j u e) -> p j u e", u=2, e=2)[:, cols],
-                bounded[q, b][:].rearrange("p (u j e) -> p j u e", u=2, e=2)[:, cols],
+                region(u).rearrange("p (j h e) -> p j h e", h=2, e=2)[:, cols],
+                bounded[u][:].rearrange("p (h j e) -> p j h e", h=2, e=2)[:, cols],
                 factors,
                 MULT,
             )
 
-        def spread(b, count):
-            factors = fresh_ps[:, P - 2 + b, :].rearrange("p (u e) -> p u e", e=2)
-            return factors.unsqueeze(1).to_broadcast([P, count, 2, 2])
+        def weigh_vector(u):
+            share = SHARE.get(u, 0)
+            factors = fresh_ps[:, P - 2 + u % 2, :].rearrange("p (h e) -> p h e", e=2)
+            weigh(nc.vector, u, slice(share, QUARTER), factors.unsqueeze(1).to_broadcast([P, QUARTER - share, 2, 2]))
 
-        def weigh_shared(q):
-            wide = fresh_wide[:].rearrange("p (j u e) -> p j u e", u=2, e=2)[:, 0 : SHARE[q]]
-            weigh(nc.gpsimd, q, 0, slice(0, SHARE[q]), wide)
-            weigh(nc.vector, q, 0, slice(SHARE[q], QUARTER), spread(0, QUARTER - SHARE[q]))
+        def weigh_gpsimd(u):
+            wide = fresh_wide[:].rearrange("p (j h e) -> p j h e", h=2, e=2)[:, 0 : SHARE[u]]
+            weigh(nc.gpsimd, u, slice(0, SHARE[u]), wide)
 
         def quantise(codes, scales, src):
             nc.vector.quantize_mx(out=codes.bitcast(FP8X4), scales=scales, in_=src)
 
-        wd_codes = [held("wd_codes%d" % b, [P, N], U32) for b in range(2)]
-        wd_sc = [held("wd_sc%d" % b, [P, N], U8) for b in range(2)]
-        for b in range(2):
-            nc.vector.tensor_copy(
-                out=region(0, b).rearrange("p (g x t) -> p g t x", x=4, t=PACK),
-                in_=wd_raw[:, b].rearrange("p t (g x) -> p g t x", x=4),
-            )
-        for b in range(2):
-            quantise(wd_codes[b][:], wd_sc[b][:], region(0, b))
+        wd_codes = held("wd_codes", [P, 2 * N], U32)
+        wd_sc = held("wd_sc", [P, 2 * N], U8)
 
         def section_passes(acc, n, b, codes, scales, start, stop):
             sections = slice(P * n, P * (n + 1))
@@ -239,69 +245,95 @@ def tile_list_fresh_news_sections_kernel(
             )
             nc.tensor.matmul_mx(
                 out=acc,
-                lhsT=wd_codes[b][:, sections].bitcast(FP8X4),
-                lhsT_scale=wd_sc[b][:, sections],
+                lhsT=wd_codes[:, N * b : N * (b + 1)][:, sections].bitcast(FP8X4),
+                lhsT_scale=wd_sc[:, N * b : N * (b + 1)][:, sections],
                 rhs=codes.bitcast(FP8X4),
                 rhs_scale=scales,
                 start=False,
                 stop=stop,
             )
 
+        sums = {}
+
+        quantised = {}
+
+        def quantise_unit(u, scales=None):
+            codes = held("z_codes%d" % u, [P, QUARTER], U32)[:]
+            if scales is None:
+                scales = held("z_sc%d" % u, [P, QUARTER], U8)[:]
+            quantise(codes, scales, region(u))
+            quantised[u] = (codes, scales)
+
+        def contract(u):
+            q, b = divmod(u, 2)
+            if b == 0 and q < 3:
+                bank = next_bank([P, 2, QUARTER])
+                sums[q] = [bank[:, 0, :], bank[:, 1, :], bank[:]]
+            elif b == 0:
+                sums[q] = [next_bank([P, QUARTER])[:] for n in range(2)]
+            for n in range(2):
+                first, last = (b + n == 0, b + n == 2) if q < 3 else (b == 0, b == 1)
+                section_passes(sums[q][n], n, b, *quantised[u], first, last)
+
         def store_quarter(q):
             scores = held("scores%d" % q, [P, 2, QUARTER], F32)
-            nc.vector.tensor_tensor(scores[:], sums[q][:], gate_sb[q][:], MULT)
+            nc.vector.tensor_tensor(scores[:], sums[q][2], gate_sb[q][:], MULT)
             nc.sync.dma_start(out[:, QUARTER * q : QUARTER * (q + 1)].rearrange("(n p) j -> p n j", p=P), scores[:])
 
-        sums = {}
-        for q in range(4):
-            squash(q, 0)
-            weigh_shared(q)
-            codes = held("z_codes%d" % q, [P, 2, QUARTER], U32)
-            scales = [held("z_sc%d%d" % (q, b), [P, QUARTER], U8) for b in range(2)]
-            if q < 3:
-                squash(q, 1)
-                weigh(nc.vector, q, 1, slice(0, QUARTER), spread(1, QUARTER))
-                for b in range(2):
-                    quantise(codes[:, b, :], scales[b][:], region(q, b))
-                sums[q] = next_bank([P, 2, QUARTER])
-                for b in range(2):
-                    for n in range(2):
-                        section_passes(sums[q][:, n, :], n, b, codes[:, b, :], scales[b][:], b + n == 0, b + n == 2)
+        for u in range(3):
+            squash(u)
+            weigh_vector(u)
+        quantise(wd_codes[:], wd_sc[:], wd_round[:])
+        for u in range(2):
+            scales = placed.tile([P, QUARTER], U8, name="z_sc%d" % u, align_bytes=256, offset=QUARTER * u)
+            quantise_unit(u, scales[:])
+            contract(u)
+        for u in (2, 4):
+            if u == 4:
+                squash(u)
+            weigh_gpsimd(u)
+            if u == 4:
+                weigh_vector(u)
+            squash(u + 1)
+            weigh_vector(u + 1)
+            for v in (u, u + 1):
+                quantise_unit(v)
+                contract(v)
 
-        rows32 = held("rows32", [P, PACK, P], F32)
-        nc.scalar.activation(out=rows32[:], in_=matches[3, 1, 0][:], func=TANH)
-        woven = held("woven", [P, P, PACK], F32)
-        nc.scalar.activation(out=woven[:], in_=matches[3, 1, 1][:].rearrange("p t j -> p j t"), func=TANH)
-        rows16 = held("rows16", [P, PACK, P], BF16)
+        last = UNITS - 1
+        squash(last - 1)
+        weigh_gpsimd(last - 1)
+        weigh_vector(last - 1)
+        rows32 = held("rows32", [P, PACK, QUARTER], F32)
+        for part in range(2):
+            nc.scalar.activation(out=rows32[:, 2 * part : 2 * part + 2, :], in_=matches[last, part][:], func=TANH)
+        rows16 = held("rows16", [P, PACK, OWN], BF16)
         for t in range(PACK):
-            nc.scalar.activation(out=rows16[:, t, :], in_=rows32[:, t, :], func=COPY, scale=fresh_sb[:, t : t + 1])
-        late = held("late", [P, UNIT], BF16)[:]
+            nc.scalar.activation(out=rows16[:, t, :], in_=rows32[:, t, 0:OWN], func=COPY, scale=fresh_sb[:, t : t + 1])
         nc.scalar.copy(
-            out=late[:, 0:HALF].rearrange("p (g x t) -> p g t x", x=4, t=PACK),
+            out=late[:, 0 : PACK * OWN].rearrange("p (g x t) -> p g t x", x=4, t=PACK),
             in_=rows16[:].rearrange("p t (g x) -> p g t x", x=4),
         )
         spilled = held("spilled", [P, QUARTER], F32)
-        nc.scalar.copy(out=spilled[:], in_=sums[1][:, 1, :])
+        nc.scalar.copy(out=spilled[:], in_=sums[1][1])
         store_quarter(0)
         nc.vector.tensor_tensor(
-            late[:, HALF:].rearrange("p (j t) -> p j t", t=PACK),
-            woven[:],
-            fresh_ps[:, P - 1, :].unsqueeze(1).to_broadcast([P, P, PACK]),
+            late[:, PACK * OWN :].rearrange("p (j t) -> p j t", t=PACK),
+            rows32[:, :, OWN:].rearrange("p t j -> p j t"),
+            fresh_ps[:, P - 1, :].unsqueeze(1).to_broadcast([P, QUARTER - OWN, PACK]),
             MULT,
         )
-        last = [next_bank([P, QUARTER]) for n in range(2)]
-        for b in range(2):
-            quantise(codes[:, b, :], scales[b][:], late if b else region(3, 0))
-            for n in range(2):
-                section_passes(last[n][:], n, b, codes[:, b, :], scales[b][:], b == 0, b == 1)
-        lower = region(3, 0)[:, 0:HALF].bitcast(F32)
+        for u in (last - 1, last):
+            quantise_unit(u)
+            contract(u)
+        lower = region(last - 1)[:, 0:HALF].bitcast(F32)
         nc.gpsimd.tensor_tensor(lower, spilled[:], gate_sb[1][:, 1, :], MULT)
         nc.scalar.dma_start(out[P:, QUARTER:HALF], lower)
         upper = fresh_wide[:, 0:QUARTER]
-        nc.vector.tensor_tensor(upper, sums[1][:, 0, :], gate_sb[1][:, 0, :], MULT)
+        nc.vector.tensor_tensor(upper, sums[1][0], gate_sb[1][:, 0, :], MULT)
         nc.sync.dma_start(out[0:P, QUARTER:HALF], upper)
         store_quarter(2)
         for n, queue in enumerate((nc.scalar, nc.sync)):
             scores = held("scores3%d" % n, [P, QUARTER], F32)
-            nc.vector.tensor_tensor(scores[:], last[n][:], gate_sb[3][:, n, :], MULT)
+            nc.vector.tensor_tensor(scores[:], sums[3][n], gate_sb[3][:, n, :], MULT)
             queue.dma_start(out[P * n : P * (n + 1), 3 * QUARTER :], scores[:])

@@ -15,7 +15,6 @@ U8 = mybir.dt.uint8
 FP8X4 = mybir.dt.float8_e4m3fn_x4
 FP4X4 = mybir.dt.float4_e2m1fn_x4
 MULT = mybir.AluOpType.mult
-ADD = mybir.AluOpType.add
 TANH = mybir.ActivationFunctionType.Tanh
 IDENTITY = mybir.ActivationFunctionType.Identity
 COPY = mybir.ActivationFunctionType.Copy
@@ -30,8 +29,9 @@ SC_FIRST = 96
 PLANE_ROW = (12, 0)
 UNITS = 8
 UNIT = QUARTER * PACK
-SHARE = {2: 88, 4: 136, 6: 112}
-OWN = 224
+SLIDE = 32
+SHARE = {0: 136, 2: 136, 4: 136, 6: 124}
+OWN = 192
 
 
 def tile_list_fresh_news_sections_kernel(
@@ -40,11 +40,10 @@ def tile_list_fresh_news_sections_kernel(
     nc = tc.nc
     with ExitStack() as ctx:
         keep = ctx.enter_context(tc.tile_pool(name="keep", bufs=1))
-        placed = ctx.enter_context(tc.tile_pool(name="placed", bufs=1))
         psum = ctx.enter_context(tc.psum_pool(name="psum", bufs=1))
 
-        def held(name, shape, dtype, over=None):
-            return keep.tile(shape, dtype, name=name, tag=over or name, align_bytes=256)
+        def held(name, shape, dtype):
+            return keep.tile(shape, dtype, name=name, tag=name, align_bytes=256)
 
         art_list = keep.tile([P, S // 16], U16, name="art_list")
         rdr_list = keep.tile([P, S2 // 16], U16, name="rdr_list")
@@ -55,7 +54,7 @@ def tile_list_fresh_news_sections_kernel(
         planes = [held("plane%d" % a, [P, (S + S2) // 4], I32) for a in range(2)]
         w4_sc = held("w4_sc", [P, 2, N // 4], I32)
         w4_codes = held("w4_codes", [P, 2, 2 * N], U8)
-        wd_raw = placed.tile([P, 2, PACK, N], F32, name="wd_raw", align_bytes=256, offset=0)
+        wd_raw = held("wd_raw", [P, 2, PACK, N], F32)
         gate_sb = [held("gate%d" % q, [P, 2, QUARTER], F32) for q in range(4)]
         fresh_rows = held("fresh_rows", [P, HALF], F32)
         fresh_sb = held("fresh_sb", [P, PACK], F32)
@@ -189,25 +188,14 @@ def tile_list_fresh_news_sections_kernel(
                     func=TANH,
                 )
 
-        wd_round = held("wd_round", [P, 2 * UNIT], BF16, over="rdr_table1")
-        nc.gpsimd.tensor_scalar(
-            wd_round[:].rearrange("p (b n t) -> p b n t", b=2, t=PACK),
-            wd_raw[:].rearrange("p b t n -> p b n t"),
-            1.0,
-            0.0,
-            MULT,
-            ADD,
-        )
-
-        values = held("values", [P, 3 * UNIT], BF16)
+        values = held("values", [P, 2 * UNIT + 3 * SLIDE], BF16)
         late = held("late", [P, UNIT], BF16)
-        shared = 2 * UNIT - PACK * SHARE[2]
-        places = [values[:, UNIT : 2 * UNIT], values[:, 0:UNIT], values[:, shared : shared + UNIT], wd_round[:, 0:UNIT]]
 
         def region(u):
             if u == UNITS - 1:
                 return late[:]
-            return places[u if u < 4 else 2 + u % 2]
+            base = (3 - u // 2) * SLIDE + u % 2 * UNIT
+            return values[:, base : base + UNIT]
 
         def weigh(engine, u, cols, factors):
             engine.tensor_tensor(
@@ -231,6 +219,13 @@ def tile_list_fresh_news_sections_kernel(
 
         wd_codes = held("wd_codes", [P, 2 * N], U32)
         wd_sc = held("wd_sc", [P, 2 * N], U8)
+        for b in range(2):
+            nc.vector.tensor_copy(
+                out=region(b).rearrange("p (g x t) -> p g t x", x=4, t=PACK),
+                in_=wd_raw[:, b].rearrange("p t (g x) -> p g t x", x=4),
+            )
+        for b in range(2):
+            quantise(wd_codes[:, N * b : N * (b + 1)], wd_sc[:, N * b : N * (b + 1)], region(b))
 
         def section_passes(acc, n, b, codes, scales, start, stop):
             sections = slice(P * n, P * (n + 1))
@@ -257,10 +252,9 @@ def tile_list_fresh_news_sections_kernel(
 
         quantised = {}
 
-        def quantise_unit(u, scales=None):
+        def quantise_unit(u):
             codes = held("z_codes%d" % u, [P, QUARTER], U32)[:]
-            if scales is None:
-                scales = held("z_sc%d" % u, [P, QUARTER], U8)[:]
+            scales = held("z_sc%d" % u, [P, QUARTER], U8)[:]
             quantise(codes, scales, region(u))
             quantised[u] = (codes, scales)
 
@@ -280,20 +274,10 @@ def tile_list_fresh_news_sections_kernel(
             nc.vector.tensor_tensor(scores[:], sums[q][2], gate_sb[q][:], MULT)
             nc.sync.dma_start(out[:, QUARTER * q : QUARTER * (q + 1)].rearrange("(n p) j -> p n j", p=P), scores[:])
 
-        for u in range(3):
+        for u in range(0, UNITS - 2, 2):
             squash(u)
-            weigh_vector(u)
-        quantise(wd_codes[:], wd_sc[:], wd_round[:])
-        for u in range(2):
-            scales = placed.tile([P, QUARTER], U8, name="z_sc%d" % u, align_bytes=256, offset=QUARTER * u)
-            quantise_unit(u, scales[:])
-            contract(u)
-        for u in (2, 4):
-            if u == 4:
-                squash(u)
             weigh_gpsimd(u)
-            if u == 4:
-                weigh_vector(u)
+            weigh_vector(u)
             squash(u + 1)
             weigh_vector(u + 1)
             for v in (u, u + 1):

@@ -30,8 +30,8 @@ PLANE_ROW = (12, 0)
 UNITS = 8
 UNIT = QUARTER * PACK
 SLIDE = 32
-SHARE = {0: 136, 2: 136, 4: 136, 6: 124}
-OWN = 192
+SHARE = {0: 136, 2: 136, 4: 136, 6: 132}
+OWN = 160
 
 
 def tile_list_fresh_news_sections_kernel(
@@ -55,7 +55,7 @@ def tile_list_fresh_news_sections_kernel(
         w4_sc = held("w4_sc", [P, 2, N // 4], I32)
         w4_codes = held("w4_codes", [P, 2, 2 * N], U8)
         wd_raw = held("wd_raw", [P, 2, PACK, N], F32)
-        gate_sb = [held("gate%d" % q, [P, 2, QUARTER], F32) for q in range(4)]
+        gate_half = [held("gate%d" % h, [P, 2, HALF], F32) for h in range(2)]
         fresh_rows = held("fresh_rows", [P, HALF], F32)
         fresh_sb = held("fresh_sb", [P, PACK], F32)
         fresh_wide = held("fresh_wide", [P, PACK * max(SHARE.values())], F32)
@@ -63,10 +63,10 @@ def tile_list_fresh_news_sections_kernel(
 
         nc.vector.memset(art_table_sc[0:SC_FIRST, :], 0)
         nc.vector.memset(fresh_rows[0 : P - 2, :], 0.0)
+        nc.vector.memset(rdr_table_sc[0:SC_FIRST, :], 0)
+        nc.vector.memset(planes[1][:], 0)
         nc.vector.memset(w4_sc[:], 0)
-        nc.gpsimd.memset(rdr_table_sc[0:SC_FIRST, :], 0)
         make_identity(nc, identity[:])
-        nc.gpsimd.memset(planes[1][:], 0)
 
         def table_words(table, a):
             return table[a].rearrange("p w t -> p (w t)").bitcast(I32)
@@ -137,10 +137,11 @@ def tile_list_fresh_news_sections_kernel(
                 w4_sc[32 * c : 32 * c + 4, :, :],
                 w4_scales[:, 4 * c : 4 * c + 4, :].rearrange("b r n -> r b n").bitcast(I32),
             )
-        for q in range(4):
+        for h in range(2):
             nc.sync.dma_start(
-                gate_sb[q][:], gate[:, QUARTER * q : QUARTER * (q + 1)].rearrange("(n p) j -> p n j", p=P)
+                gate_half[h][:], gate[:, HALF * h : HALF * (h + 1)].rearrange("(n p) j -> p n j", p=P)
             )
+        gate_sb = [gate_half[q // 2][:, :, QUARTER * (q % 2) : QUARTER * (q % 2 + 1)] for q in range(4)]
 
         gather_readers(1)
 
@@ -269,11 +270,6 @@ def tile_list_fresh_news_sections_kernel(
                 first, last = (b + n == 0, b + n == 2) if q < 3 else (b == 0, b == 1)
                 section_passes(sums[q][n], n, b, *quantised[u], first, last)
 
-        def store_quarter(q):
-            scores = held("scores%d" % q, [P, 2, QUARTER], F32)
-            nc.vector.tensor_tensor(scores[:], sums[q][2], gate_sb[q][:], MULT)
-            nc.sync.dma_start(out[:, QUARTER * q : QUARTER * (q + 1)].rearrange("(n p) j -> p n j", p=P), scores[:])
-
         for u in range(0, UNITS - 2, 2):
             squash(u)
             weigh_gpsimd(u)
@@ -300,7 +296,9 @@ def tile_list_fresh_news_sections_kernel(
         )
         spilled = held("spilled", [P, QUARTER], F32)
         nc.scalar.copy(out=spilled[:], in_=sums[1][1])
-        store_quarter(0)
+        scores = held("scores0", [P, 2, QUARTER], F32)
+        nc.vector.tensor_tensor(scores[:], sums[0][2], gate_sb[0], MULT)
+        nc.sync.dma_start(out[:, 0:QUARTER].rearrange("(n p) j -> p n j", p=P), scores[:])
         nc.vector.tensor_tensor(
             late[:, PACK * OWN :].rearrange("p (j t) -> p j t", t=PACK),
             rows32[:, :, OWN:].rearrange("p t j -> p j t"),
@@ -316,8 +314,7 @@ def tile_list_fresh_news_sections_kernel(
         upper = fresh_wide[:, 0:QUARTER]
         nc.vector.tensor_tensor(upper, sums[1][0], gate_sb[1][:, 0, :], MULT)
         nc.sync.dma_start(out[0:P, QUARTER:HALF], upper)
-        store_quarter(2)
-        for n, queue in enumerate((nc.scalar, nc.sync)):
-            scores = held("scores3%d" % n, [P, QUARTER], F32)
-            nc.vector.tensor_tensor(scores[:], sums[3][n], gate_sb[3][:, n, :], MULT)
-            queue.dma_start(out[P * n : P * (n + 1), 3 * QUARTER :], scores[:])
+        for q, n, queue in ((2, 0, nc.scalar), (2, 1, nc.sync), (3, 0, nc.scalar), (3, 1, nc.sync)):
+            scores = held("scores%d%d" % (q, n), [P, QUARTER], F32)
+            nc.vector.tensor_tensor(scores[:], sums[q][n], gate_sb[q][:, n, :], MULT)
+            queue.dma_start(out[P * n : P * (n + 1), QUARTER * q : QUARTER * (q + 1)], scores[:])

@@ -15,6 +15,7 @@ U8 = mybir.dt.uint8
 FP8X4 = mybir.dt.float8_e4m3fn_x4
 FP4X4 = mybir.dt.float4_e2m1fn_x4
 MULT = mybir.AluOpType.mult
+ADD = mybir.AluOpType.add
 TANH = mybir.ActivationFunctionType.Tanh
 IDENTITY = mybir.ActivationFunctionType.Identity
 COPY = mybir.ActivationFunctionType.Copy
@@ -30,7 +31,7 @@ PLANE_ROW = (12, 0)
 UNITS = 8
 UNIT = QUARTER * PACK
 SLIDE = 32
-SHARE = {0: 136, 2: 136, 4: 136, 6: 132}
+SHARE = {2: 136, 4: 136, 6: 132}
 OWN = 160
 
 
@@ -40,6 +41,7 @@ def tile_list_fresh_news_sections_kernel(
     nc = tc.nc
     with ExitStack() as ctx:
         keep = ctx.enter_context(tc.tile_pool(name="keep", bufs=1))
+        reuse = ctx.enter_context(tc.tile_pool(name="reuse", bufs=1))
         psum = ctx.enter_context(tc.psum_pool(name="psum", bufs=1))
 
         def held(name, shape, dtype):
@@ -54,7 +56,9 @@ def tile_list_fresh_news_sections_kernel(
         planes = [held("plane%d" % a, [P, (S + S2) // 4], I32) for a in range(2)]
         w4_sc = held("w4_sc", [P, 2, N // 4], I32)
         w4_codes = held("w4_codes", [P, 2, 2 * N], U8)
-        wd_raw = held("wd_raw", [P, 2, PACK, N], F32)
+        wd_raw = [
+            reuse.tile([P, PACK, N], F32, name="wd_raw%d" % b, offset=4 * UNIT * b, align_bytes=256) for b in range(2)
+        ]
         gate_half = [held("gate%d" % h, [P, 2, HALF], F32) for h in range(2)]
         fresh_rows = held("fresh_rows", [P, HALF], F32)
         fresh_sb = held("fresh_sb", [P, PACK], F32)
@@ -128,9 +132,11 @@ def tile_list_fresh_news_sections_kernel(
         gather_readers(0)
         gather_articles(1)
 
-        nc.sync.dma_start(
-            wd_raw[:].rearrange("p b t n -> p b (t n)"), wd.rearrange("(b p t) n -> p b (t n)", b=2, t=PACK)
-        )
+        for b in range(2):
+            nc.sync.dma_start(
+                wd_raw[b][:].rearrange("p t n -> p (t n)"),
+                wd[HALF * b : HALF * (b + 1), :].rearrange("(p t) n -> p (t n)", t=PACK),
+            )
         nc.sync.dma_start(w4_codes[:].bitcast(I32), w4_words.rearrange("b p w -> p b w").bitcast(I32))
         for c in range(QUADRANTS):
             nc.sync.dma_start(
@@ -155,19 +161,22 @@ def tile_list_fresh_news_sections_kernel(
 
         def match_pass(a, u, part):
             q, b = divmod(u, 2)
+            count, width = (PACK, P) if q == 0 else (2, QUARTER)
+            first_t, first_j = (0, P * part) if q == 0 else (2 * part, 0)
             if a == 0:
-                matches[u, part] = next_bank([P, 2, QUARTER])
+                matches[u, part] = next_bank([P, count, width])
             plane = planes[a][:].bitcast(U8)
-            for e in range(2):
-                col = HALF * b + P * (2 * part + e)
+            readers = S + QUARTER * q + first_j
+            for e in range(count):
+                col = HALF * b + P * (first_t + e)
                 nc.tensor.matmul_mx(
                     out=matches[u, part][:, e, :],
                     lhsT=art[a][:, col : col + P].bitcast(FP8X4),
                     lhsT_scale=plane[PLANE_ROW[a] :, col : col + P],
-                    rhs=rdr[a, q].bitcast(FP8X4),
-                    rhs_scale=plane[PLANE_ROW[a] :, S + QUARTER * q : S + QUARTER * (q + 1)],
+                    rhs=rdr[a, q][:, first_j : first_j + width].bitcast(FP8X4),
+                    rhs_scale=plane[PLANE_ROW[a] :, readers : readers + width],
                     start=(a == 0 and e == 0),
-                    stop=(a == 1 and e == 1),
+                    stop=(a == 1 and e == count - 1),
                 )
 
         keys = [(u, part) for u in range(UNITS) for part in range(2)]
@@ -184,7 +193,7 @@ def tile_list_fresh_news_sections_kernel(
             bounded[u] = held("bounded%d" % u, [P, UNIT], F32)
             for part in range(2):
                 nc.scalar.activation(
-                    out=bounded[u][:, HALF * part : HALF * (part + 1)].rearrange("p (j e) -> p j e", e=2),
+                    out=bounded[u][:, HALF * part : HALF * (part + 1)].rearrange("p (j e) -> p j e", e=PACK if u < 2 else 2),
                     in_=matches[u, part][:].rearrange("p e j -> p j e"),
                     func=TANH,
                 )
@@ -220,13 +229,16 @@ def tile_list_fresh_news_sections_kernel(
 
         wd_codes = held("wd_codes", [P, 2 * N], U32)
         wd_sc = held("wd_sc", [P, 2 * N], U8)
+        wd_rounded = held("wd_rounded", [P, 2 * UNIT], BF16)
         for b in range(2):
-            nc.vector.tensor_copy(
-                out=region(b).rearrange("p (g x t) -> p g t x", x=4, t=PACK),
-                in_=wd_raw[:, b].rearrange("p t (g x) -> p g t x", x=4),
+            nc.gpsimd.tensor_scalar(
+                wd_rounded[:, UNIT * b : UNIT * (b + 1)].rearrange("p (n t) -> p n t", t=PACK),
+                wd_raw[b][:].rearrange("p t n -> p n t"),
+                1.0,
+                0.0,
+                MULT,
+                ADD,
             )
-        for b in range(2):
-            quantise(wd_codes[:, N * b : N * (b + 1)], wd_sc[:, N * b : N * (b + 1)], region(b))
 
         def section_passes(acc, n, b, codes, scales, start, stop):
             sections = slice(P * n, P * (n + 1))
@@ -254,7 +266,12 @@ def tile_list_fresh_news_sections_kernel(
         quantised = {}
 
         def quantise_unit(u):
-            codes = held("z_codes%d" % u, [P, QUARTER], U32)[:]
+            if u < 2:
+                codes = reuse.tile(
+                    [P, QUARTER], U32, name="z_codes%d" % u, offset=4 * UNIT + 4 * QUARTER * u, align_bytes=256
+                )[:]
+            else:
+                codes = held("z_codes%d" % u, [P, QUARTER], U32)[:]
             scales = held("z_sc%d" % u, [P, QUARTER], U8)[:]
             quantise(codes, scales, region(u))
             quantised[u] = (codes, scales)
@@ -270,7 +287,21 @@ def tile_list_fresh_news_sections_kernel(
                 first, last = (b + n == 0, b + n == 2) if q < 3 else (b == 0, b == 1)
                 section_passes(sums[q][n], n, b, *quantised[u], first, last)
 
-        for u in range(0, UNITS - 2, 2):
+        for u in range(2):
+            squash(u)
+            for part in range(2):
+                cols = slice(HALF * part, HALF * (part + 1))
+                nc.vector.tensor_tensor(
+                    region(u)[:, cols].rearrange("p (j t) -> p j t", t=PACK),
+                    bounded[u][:, cols].rearrange("p (j t) -> p j t", t=PACK),
+                    fresh_ps[:, P - 2 + u, :].unsqueeze(1).to_broadcast([P, P, PACK]),
+                    MULT,
+                )
+        quantise(wd_codes[:], wd_sc[:], wd_rounded[:])
+        for u in range(2):
+            quantise_unit(u)
+            contract(u)
+        for u in range(2, UNITS - 2, 2):
             squash(u)
             weigh_gpsimd(u)
             weigh_vector(u)

@@ -27,6 +27,7 @@ QUARTER = 256
 QUADRANTS = 4
 BANKS = 7
 SC_FIRST = 96
+RDR_FIRST = 32
 PLANE_ROW = (12, 0)
 UNITS = 8
 UNIT = QUARTER * PACK
@@ -66,10 +67,12 @@ def tile_list_fresh_news_sections_kernel(
         identity = held("identity", [P, P], F32)
 
         nc.vector.memset(art_table_sc[0:SC_FIRST, :], 0)
-        nc.vector.memset(fresh_rows[0 : P - 2, :], 0.0)
-        nc.vector.memset(rdr_table_sc[0:SC_FIRST, :], 0)
-        nc.vector.memset(planes[1][:], 0)
-        nc.vector.memset(w4_sc[:], 0)
+        nc.gpsimd.memset(rdr_table_sc[64:P, :], 0)
+        nc.gpsimd.memset(rdr_table_sc[0:RDR_FIRST, :], 0)
+        nc.gpsimd.memset(planes[0][0:SC_FIRST, S // 4 :], 0)
+        nc.gpsimd.memset(planes[1][:], 0)
+        nc.gpsimd.memset(fresh_rows[0 : P - 2, :], 0.0)
+        nc.gpsimd.memset(w4_sc[:], 0)
         make_identity(nc, identity[:])
 
         def table_words(table, a):
@@ -78,7 +81,7 @@ def tile_list_fresh_news_sections_kernel(
         nc.sync.dma_start(art_list[:], offs)
         nc.scalar.dma_start(art_table_sc[SC_FIRST:P, :], tab_scales.rearrange("a s w -> (a s) w").bitcast(I32))
         nc.sync.dma_start(rdr_list[:], offs2)
-        nc.sync.dma_start(rdr_table_sc[SC_FIRST:P, :], tab2_scales.rearrange("a s w -> (a s) w").bitcast(I32))
+        nc.sync.dma_start(rdr_table_sc[RDR_FIRST : RDR_FIRST + 32, :], tab2_scales.rearrange("a s w -> (a s) w").bitcast(I32))
         nc.sync.dma_start(fresh_rows[P - 2 : P, :], fresh.rearrange("(b i) -> b i", b=2))
         fresh_ps = psum.tile([P, P, PACK], F32, name="fresh_ps")
         for t in range(PACK):
@@ -114,7 +117,9 @@ def tile_list_fresh_news_sections_kernel(
             planes[0][:].bitcast(U8)[:, 0:S].rearrange("p (b t m) -> p b t m", b=2, t=PACK),
             art_sc_listed[:].rearrange("p (b m t) -> p b t m", b=2, t=PACK),
         )
-        nc.vector.tensor_copy(planes[0][:, S // 4 :], rdr_sc_listed[:].bitcast(I32))
+        nc.vector.tensor_copy(
+            planes[0][SC_FIRST:P, S // 4 :], rdr_sc_listed[:].bitcast(I32)[RDR_FIRST : RDR_FIRST + 32, :]
+        )
         for c in range(QUADRANTS - 1):
             row = 32 * c + PLANE_ROW[0]
             nc.sync.dma_start(planes[0][row : row + 4, :], planes[0][SC_FIRST + 4 * c : SC_FIRST + 4 * c + 4, :])

@@ -237,8 +237,8 @@ def tile_list_fresh_news_sections_kernel(
         wd_rounded = held("wd_rounded", [P, 2 * UNIT], BF16)
         for b in range(2):
             nc.gpsimd.tensor_scalar(
-                wd_rounded[:, UNIT * b : UNIT * (b + 1)].rearrange("p (n t) -> p n t", t=PACK),
-                wd_raw[b][:].rearrange("p t n -> p n t"),
+                wd_rounded[:, UNIT * b : UNIT * (b + 1)].rearrange("p (g x t) -> p g t x", x=2, t=PACK),
+                wd_raw[b][:].rearrange("p t (g x) -> p g t x", x=2),
                 1.0,
                 0.0,
                 MULT,

@@ -82,7 +82,7 @@ def tile_list_fresh_news_sections_kernel(
         nc.scalar.dma_start(art_table_sc[SC_FIRST:P, :], tab_scales.rearrange("a s w -> (a s) w").bitcast(I32))
         nc.sync.dma_start(rdr_list[:], offs2)
         nc.sync.dma_start(rdr_table_sc[RDR_FIRST : RDR_FIRST + 32, :], tab2_scales.rearrange("a s w -> (a s) w").bitcast(I32))
-        nc.sync.dma_start(fresh_rows[P - 2 : P, :], fresh.rearrange("(b i) -> b i", b=2))
+        nc.scalar.dma_start(fresh_rows[P - 2 : P, :], fresh.rearrange("(b i) -> b i", b=2))
         fresh_ps = psum.tile([P, P, PACK], F32, name="fresh_ps")
         for t in range(PACK):
             nc.tensor.transpose(fresh_ps[:, :, t], fresh_rows[:, t:HALF:PACK], identity[:])
@@ -99,7 +99,7 @@ def tile_list_fresh_news_sections_kernel(
         art_sc_listed = held("art_sc_listed", [P, S], U8)
         rdr_sc_listed = held("rdr_sc_listed", [P, S2], U8)
         art = [held("art%d" % a, [P, S], U32) for a in range(2)]
-        pieces = (((0, HALF), (HALF, HALF)), ((0, QUARTER), (QUARTER, QUARTER), (HALF, HALF)))
+        pieces = (((0, HALF), (HALF, HALF)), ((0, QUARTER), (QUARTER, S2 - QUARTER)))
         rdr = {}
 
         def gather_readers(a):
@@ -111,12 +111,21 @@ def tile_list_fresh_news_sections_kernel(
                 for q in range(first // QUARTER, (first + count) // QUARTER):
                     rdr[a, q] = words[:, QUARTER * q - first : QUARTER * (q + 1) - first]
 
-        nc.vector.tensor_copy(art_sc_listed[:], art_table_sc[:].bitcast(U8).indirect(art_list[:]))
+        for b in range(2):
+            nc.vector.tensor_copy(
+                art_sc_listed[:, HALF * b : HALF * (b + 1)],
+                art_table_sc[:].bitcast(U8).indirect(art_list[:, 32 * b : 32 * (b + 1)]),
+            )
+
+        def sort_scales(b):
+            nc.vector.tensor_copy(
+                planes[0][:].bitcast(U8)[:, HALF * b : HALF * (b + 1)].rearrange("p (t m) -> p t m", t=PACK),
+                art_sc_listed[:, HALF * b : HALF * (b + 1)].rearrange("p (m t) -> p t m", t=PACK),
+            )
+
+        sort_scales(0)
         nc.vector.tensor_copy(rdr_sc_listed[:], rdr_table_sc[:].bitcast(U8).indirect(rdr_list[:]))
-        nc.vector.tensor_copy(
-            planes[0][:].bitcast(U8)[:, 0:S].rearrange("p (b t m) -> p b t m", b=2, t=PACK),
-            art_sc_listed[:].rearrange("p (b m t) -> p b t m", b=2, t=PACK),
-        )
+        sort_scales(1)
         nc.vector.tensor_copy(
             planes[0][SC_FIRST:P, S // 4 :], rdr_sc_listed[:].bitcast(I32)[RDR_FIRST : RDR_FIRST + 32, :]
         )

@@ -32,8 +32,8 @@ PLANE_ROW = (12, 0)
 UNITS = 8
 UNIT = QUARTER * PACK
 SLIDE = 32
-SHARE = {2: 136, 4: 136, 6: 132}
-OWN = 160
+SHARE = {2: 140, 4: 140, 6: 128}
+OWN = 184
 
 
 def tile_list_fresh_news_sections_kernel(

@@ -32,7 +32,7 @@ PLANE_ROW = (12, 0)
 UNITS = 8
 UNIT = QUARTER * PACK
 SLIDE = 32
-SHARE = {2: 140, 4: 140, 6: 128}
+SHARE = {2: 136, 4: 136, 6: 148}
 OWN = 184
 
 
@@ -43,6 +43,7 @@ def tile_list_fresh_news_sections_kernel(
     with ExitStack() as ctx:
         keep = ctx.enter_context(tc.tile_pool(name="keep", bufs=1))
         reuse = ctx.enter_context(tc.tile_pool(name="reuse", bufs=1))
+        sliding = ctx.enter_context(tc.tile_pool(name="sliding", bufs=1))
         psum = ctx.enter_context(tc.psum_pool(name="psum", bufs=1))
 
         def held(name, shape, dtype):
@@ -60,7 +61,7 @@ def tile_list_fresh_news_sections_kernel(
         wd_raw = [
             reuse.tile([P, PACK, N], F32, name="wd_raw%d" % b, offset=4 * UNIT * b, align_bytes=256) for b in range(2)
         ]
-        gate_half = [held("gate%d" % h, [P, 2, HALF], F32) for h in range(2)]
+        gate_all = held("gate", [P, 2, S2], F32)
         fresh_rows = held("fresh_rows", [P, HALF], F32)
         fresh_sb = held("fresh_sb", [P, PACK], F32)
         fresh_wide = held("fresh_wide", [P, PACK * max(SHARE.values())], F32)
@@ -157,11 +158,8 @@ def tile_list_fresh_news_sections_kernel(
                 w4_sc[32 * c : 32 * c + 4, :, :],
                 w4_scales[:, 4 * c : 4 * c + 4, :].rearrange("b r n -> r b n").bitcast(I32),
             )
-        for h in range(2):
-            nc.sync.dma_start(
-                gate_half[h][:], gate[:, HALF * h : HALF * (h + 1)].rearrange("(n p) j -> p n j", p=P)
-            )
-        gate_sb = [gate_half[q // 2][:, :, QUARTER * (q % 2) : QUARTER * (q % 2 + 1)] for q in range(4)]
+        nc.sync.dma_start(gate_all[:], gate.rearrange("(n p) j -> p n j", p=P))
+        gate_sb = [gate_all[:, :, QUARTER * q : QUARTER * (q + 1)] for q in range(4)]
 
         gather_readers(1)
 
@@ -204,7 +202,7 @@ def tile_list_fresh_news_sections_kernel(
         bounded = {}
 
         def squash(u):
-            bounded[u] = held("bounded%d" % u, [P, UNIT], F32)
+            bounded[u] = held("bounded%d" % u, [P, UNIT + (HALF if u == 6 else 0)], F32)
             for part in range(2):
                 nc.scalar.activation(
                     out=bounded[u][:, HALF * part : HALF * (part + 1)].rearrange("p (j e) -> p j e", e=PACK if u < 2 else 2),
@@ -212,19 +210,21 @@ def tile_list_fresh_news_sections_kernel(
                     func=TANH,
                 )
 
-        values = held("values", [P, 2 * UNIT + 3 * SLIDE], BF16)
-        late = held("late", [P, UNIT], BF16)
+        def in_row(name, u, first, shape, dtype):
+            place = first + ((3 - u // 2) * SLIDE + u % 2 * UNIT if u < UNITS - 1 else 2 * UNIT + 3 * SLIDE)
+            return sliding.tile(shape, dtype, name=name, offset=2 * place, align_bytes=64)
+
+        values = {}
 
         def region(u):
-            if u == UNITS - 1:
-                return late[:]
-            base = (3 - u // 2) * SLIDE + u % 2 * UNIT
-            return values[:, base : base + UNIT]
+            if u not in values:
+                values[u] = in_row("values%d" % u, u, 0, [P, UNIT], BF16)
+            return values[u][:]
 
         def weigh(engine, u, cols, factors):
             engine.tensor_tensor(
                 region(u).rearrange("p (j h e) -> p j h e", h=2, e=2)[:, cols],
-                bounded[u][:].rearrange("p (h j e) -> p j h e", h=2, e=2)[:, cols],
+                bounded[u][:, 0:UNIT].rearrange("p (h j e) -> p j h e", h=2, e=2)[:, cols],
                 factors,
                 MULT,
             )
@@ -292,14 +292,11 @@ def tile_list_fresh_news_sections_kernel(
 
         def contract(u):
             q, b = divmod(u, 2)
-            if b == 0 and q < 3:
+            if b == 0:
                 bank = next_bank([P, 2, QUARTER])
                 sums[q] = [bank[:, 0, :], bank[:, 1, :], bank[:]]
-            elif b == 0:
-                sums[q] = [next_bank([P, QUARTER])[:] for n in range(2)]
             for n in range(2):
-                first, last = (b + n == 0, b + n == 2) if q < 3 else (b == 0, b == 1)
-                section_passes(sums[q][n], n, b, *quantised[u], first, last)
+                section_passes(sums[q][n], n, b, *quantised[u], b + n == 0, b + n == 2)
 
         for u in range(2):
             squash(u)
@@ -332,34 +329,46 @@ def tile_list_fresh_news_sections_kernel(
         rows32 = held("rows32", [P, PACK, QUARTER], F32)
         for part in range(2):
             nc.scalar.activation(out=rows32[:, 2 * part : 2 * part + 2, :], in_=matches[last, part][:], func=TANH)
-        rows16 = held("rows16", [P, PACK, OWN], BF16)
+        rows16 = reuse.tile([P, PACK, OWN], BF16, name="rows16", offset=0, align_bytes=256)
         for t in range(PACK):
             nc.scalar.activation(out=rows16[:, t, :], in_=rows32[:, t, 0:OWN], func=COPY, scale=fresh_sb[:, t : t + 1])
         nc.scalar.copy(
-            out=late[:, 0 : PACK * OWN].rearrange("p (g x t) -> p g t x", x=4, t=PACK),
+            out=region(last)[:, 0 : PACK * OWN].rearrange("p (g x t) -> p g t x", x=4, t=PACK),
             in_=rows16[:].rearrange("p t (g x) -> p g t x", x=4),
         )
-        spilled = held("spilled", [P, QUARTER], F32)
-        nc.scalar.copy(out=spilled[:], in_=sums[1][1])
-        scores = held("scores0", [P, 2, QUARTER], F32)
-        nc.vector.tensor_tensor(scores[:], sums[0][2], gate_sb[0], MULT)
-        nc.sync.dma_start(out[:, 0:QUARTER].rearrange("(n p) j -> p n j", p=P), scores[:])
         nc.vector.tensor_tensor(
-            late[:, PACK * OWN :].rearrange("p (j t) -> p j t", t=PACK),
+            region(last)[:, PACK * OWN :].rearrange("p (j t) -> p j t", t=PACK),
             rows32[:, :, OWN:].rearrange("p t j -> p j t"),
             fresh_ps[:, P - 1, :].unsqueeze(1).to_broadcast([P, QUARTER - OWN, PACK]),
             MULT,
         )
-        for u in (last - 1, last):
-            quantise_unit(u)
-            contract(u)
-        lower = region(last - 1)[:, 0:HALF].bitcast(F32)
-        nc.gpsimd.tensor_tensor(lower, spilled[:], gate_sb[1][:, 1, :], MULT)
-        nc.scalar.dma_start(out[P:, QUARTER:HALF], lower)
-        upper = fresh_wide[:, 0:QUARTER]
+        scores = bounded[last - 1][:, UNIT - P : UNIT - P + HALF].rearrange("p (n j) -> p n j", n=2)
+        nc.vector.tensor_tensor(scores, sums[0][2], gate_sb[0], MULT)
+        nc.sync.dma_start(out[:, 0:QUARTER].rearrange("(n p) j -> p n j", p=P), scores)
+        upper = rows32[:, PACK - 1, :]
         nc.vector.tensor_tensor(upper, sums[1][0], gate_sb[1][:, 0, :], MULT)
         nc.sync.dma_start(out[0:P, QUARTER:HALF], upper)
-        for q, n, queue in ((2, 0, nc.scalar), (2, 1, nc.sync), (3, 0, nc.scalar), (3, 1, nc.sync)):
-            scores = held("scores%d%d" % (q, n), [P, QUARTER], F32)
-            nc.vector.tensor_tensor(scores[:], sums[q][n], gate_sb[q][:, n, :], MULT)
-            queue.dma_start(out[P * n : P * (n + 1), QUARTER * q : QUARTER * (q + 1)], scores[:])
+        spilled = reuse.tile([P, QUARTER], F32, name="spilled", offset=0, align_bytes=256)
+        nc.scalar.copy(out=spilled[:], in_=sums[1][1])
+        for u in (last - 1, last):
+            quantise_unit(u)
+        ends = []
+        for n, first, count in ((0, 0, QUARTER), (1, 0, P), (1, P, P)):
+            bank = next_bank([P, count])[:]
+            for b in range(2):
+                codes, scales = quantised[last - 1 + b]
+                readers = slice(first, first + count)
+                section_passes(bank, n, b, codes[:, readers], scales[:, readers], b == 0, b == 1)
+            ends.append((n, first, count, bank))
+        lower = in_row("scores11", last - 1, 0, [P, QUARTER], F32)[:]
+        nc.gpsimd.tensor_tensor(lower, spilled[:], gate_sb[1][:, 1, :], MULT)
+        nc.scalar.dma_start(out[P:, QUARTER:HALF], lower)
+        for n, queue in ((0, nc.scalar), (1, nc.sync)):
+            scores = in_row("scores2%d" % n, last - 1 + n, HALF, [P, QUARTER], F32)[:]
+            nc.vector.tensor_tensor(scores, sums[2][n], gate_sb[2][:, n, :], MULT)
+            queue.dma_start(out[P * n : P * (n + 1), HALF : HALF + QUARTER], scores)
+        for (n, first, count, bank), queue in zip(ends, (nc.sync, nc.scalar, nc.sync)):
+            scores = held("scores3%d_%d" % (n, first), [P, count], F32)[:]
+            nc.vector.tensor_tensor(scores, bank, gate_sb[3][:, n, first : first + count], MULT)
+            column = 3 * QUARTER + first
+            queue.dma_start(out[P * n : P * (n + 1), column : column + count], scores)

@@ -33,7 +33,7 @@ UNITS = 8
 UNIT = QUARTER * PACK
 SLIDE = 32
 SHARE = {2: 136, 4: 136, 6: 148}
-OWN = 184
+OWN = 168
 
 
 def tile_list_fresh_news_sections_kernel(
@@ -82,7 +82,9 @@ def tile_list_fresh_news_sections_kernel(
         nc.sync.dma_start(art_list[:], offs)
         nc.scalar.dma_start(art_table_sc[SC_FIRST:P, :], tab_scales.rearrange("a s w -> (a s) w").bitcast(I32))
         nc.sync.dma_start(rdr_list[:], offs2)
-        nc.sync.dma_start(rdr_table_sc[RDR_FIRST : RDR_FIRST + 32, :], tab2_scales.rearrange("a s w -> (a s) w").bitcast(I32))
+        nc.sync.dma_start(
+            rdr_table_sc[RDR_FIRST : RDR_FIRST + 32, :], tab2_scales.rearrange("a s w -> (a s) w").bitcast(I32)
+        )
         nc.scalar.dma_start(fresh_rows[P - 2 : P, :], fresh.rearrange("(b i) -> b i", b=2))
         fresh_ps = psum.tile([P, P, PACK], F32, name="fresh_ps")
         for t in range(PACK):
@@ -202,17 +204,18 @@ def tile_list_fresh_news_sections_kernel(
         bounded = {}
 
         def squash(u):
-            bounded[u] = held("bounded%d" % u, [P, UNIT + (HALF if u == 6 else 0)], F32)
+            bounded[u] = held("bounded%d" % u, [P, UNIT + (HALF if u == UNITS - 2 else 0)], F32)
+            side_by_side = PACK if u < 2 else 2
             for part in range(2):
                 nc.scalar.activation(
-                    out=bounded[u][:, HALF * part : HALF * (part + 1)].rearrange("p (j e) -> p j e", e=PACK if u < 2 else 2),
+                    out=bounded[u][:, HALF * part : HALF * (part + 1)].rearrange("p (j e) -> p j e", e=side_by_side),
                     in_=matches[u, part][:].rearrange("p e j -> p j e"),
                     func=TANH,
                 )
 
-        def in_row(name, u, first, shape, dtype):
-            place = first + ((3 - u // 2) * SLIDE + u % 2 * UNIT if u < UNITS - 1 else 2 * UNIT + 3 * SLIDE)
-            return sliding.tile(shape, dtype, name=name, offset=2 * place, align_bytes=64)
+        def in_row(name, u, skip, shape, dtype):
+            place = (3 - u // 2) * SLIDE + u % 2 * UNIT if u < UNITS - 1 else 2 * UNIT + 3 * SLIDE
+            return sliding.tile(shape, dtype, name=name, offset=2 * (place + skip), align_bytes=64)
 
         values = {}
 
@@ -276,7 +279,6 @@ def tile_list_fresh_news_sections_kernel(
             )
 
         sums = {}
-
         quantised = {}
 
         def quantise_unit(u):

@@ -33,7 +33,7 @@ UNITS = 8
 UNIT = QUARTER * PACK
 SLIDE = 32
 SHARE = {2: 136, 4: 136, 6: 148}
-OWN = 168
+OWN = 200
 
 
 def tile_list_fresh_news_sections_kernel(

from contextlib import ExitStack

import concourse.mybir as mybir
from concourse.masks import make_identity

K, T, S, T2, S2, N = 1024, 2048, 1024, 4096, 1024, 256
FLOPS = 2 * K * S * S2 + 2 * 2 * S * N * S2

F32 = mybir.dt.float32
BF16 = mybir.dt.bfloat16
I32 = mybir.dt.int32
U32 = mybir.dt.uint32
U16 = mybir.dt.uint16
U8 = mybir.dt.uint8
FP8X4 = mybir.dt.float8_e4m3fn_x4
FP4X4 = mybir.dt.float4_e2m1fn_x4
MULT = mybir.AluOpType.mult
ADD = mybir.AluOpType.add
TANH = mybir.ActivationFunctionType.Tanh
IDENTITY = mybir.ActivationFunctionType.Identity
COPY = mybir.ActivationFunctionType.Copy

P = 128
PACK = 4
HALF = 512
QUARTER = 256
QUADRANTS = 4
BANKS = 7
SC_FIRST = 96
RDR_FIRST = 32
PLANE_ROW = (12, 0)
UNITS = 8
UNIT = QUARTER * PACK
SLIDE = 32
SHARE = {2: 136, 4: 136, 6: 148}
OWN = 200


def tile_list_fresh_news_sections_kernel(
    tc, tab_words, tab_scales, tab2_words, tab2_scales, offs, offs2, fresh, w4_words, w4_scales, wd, gate, out
):
    nc = tc.nc
    with ExitStack() as ctx:
        keep = ctx.enter_context(tc.tile_pool(name="keep", bufs=1))
        reuse = ctx.enter_context(tc.tile_pool(name="reuse", bufs=1))
        sliding = ctx.enter_context(tc.tile_pool(name="sliding", bufs=1))
        psum = ctx.enter_context(tc.psum_pool(name="psum", bufs=1))

        def held(name, shape, dtype):
            return keep.tile(shape, dtype, name=name, tag=name, align_bytes=256)

        art_list = keep.tile([P, S // 16], U16, name="art_list")
        rdr_list = keep.tile([P, S2 // 16], U16, name="rdr_list")
        art_table = [held("art_table%d" % a, [P, T], I32) for a in range(2)]
        rdr_table = [held("rdr_table%d" % a, [P, T2], I32) for a in range(2)]
        art_table_sc = held("art_table_sc", [P, T // 4], I32)
        rdr_table_sc = held("rdr_table_sc", [P, T2 // 4], I32)
        planes = [held("plane%d" % a, [P, (S + S2) // 4], I32) for a in range(2)]
        w4_sc = held("w4_sc", [P, 2, N // 4], I32)
        w4_codes = held("w4_codes", [P, 2, 2 * N], U8)
        wd_raw = [
            reuse.tile([P, PACK, N], F32, name="wd_raw%d" % b, offset=4 * UNIT * b, align_bytes=256) for b in range(2)
        ]
        gate_all = held("gate", [P, 2, S2], F32)
        fresh_rows = held("fresh_rows", [P, HALF], F32)
        fresh_sb = held("fresh_sb", [P, PACK], F32)
        fresh_wide = held("fresh_wide", [P, PACK * max(SHARE.values())], F32)
        identity = held("identity", [P, P], F32)

        nc.vector.memset(art_table_sc[0:SC_FIRST, :], 0)
        nc.gpsimd.memset(rdr_table_sc[64:P, :], 0)
        nc.gpsimd.memset(rdr_table_sc[0:RDR_FIRST, :], 0)
        nc.gpsimd.memset(planes[0][0:SC_FIRST, S // 4 :], 0)
        nc.gpsimd.memset(planes[1][:], 0)
        nc.gpsimd.memset(fresh_rows[0 : P - 2, :], 0.0)
        nc.gpsimd.memset(w4_sc[:], 0)
        make_identity(nc, identity[:])

        def table_words(table, a):
            return table[a].rearrange("p w t -> p (w t)").bitcast(I32)

        nc.sync.dma_start(art_list[:], offs)
        nc.scalar.dma_start(art_table_sc[SC_FIRST:P, :], tab_scales.rearrange("a s w -> (a s) w").bitcast(I32))
        nc.sync.dma_start(rdr_list[:], offs2)
        nc.sync.dma_start(
            rdr_table_sc[RDR_FIRST : RDR_FIRST + 32, :], tab2_scales.rearrange("a s w -> (a s) w").bitcast(I32)
        )
        nc.scalar.dma_start(fresh_rows[P - 2 : P, :], fresh.rearrange("(b i) -> b i", b=2))
        fresh_ps = psum.tile([P, P, PACK], F32, name="fresh_ps")
        for t in range(PACK):
            nc.tensor.transpose(fresh_ps[:, :, t], fresh_rows[:, t:HALF:PACK], identity[:])
        nc.scalar.activation(out=fresh_sb[:], in_=fresh_ps[:, P - 1, :], func=IDENTITY)
        nc.scalar.activation(
            out=fresh_wide[:].rearrange("p (j t) -> p j t", t=PACK),
            in_=fresh_ps[:, P - 2, :].unsqueeze(1).to_broadcast([P, max(SHARE.values()), PACK]),
            func=IDENTITY,
        )
        nc.sync.dma_start(art_table[0][:], table_words(tab_words, 0))
        nc.sync.dma_start(rdr_table[0][:], table_words(tab2_words, 0))
        nc.sync.dma_start(art_table[1][:], table_words(tab_words, 1))

        art_sc_listed = held("art_sc_listed", [P, S], U8)
        rdr_sc_listed = held("rdr_sc_listed", [P, S2], U8)
        art = [held("art%d" % a, [P, S], U32) for a in range(2)]
        pieces = (((0, HALF), (HALF, HALF)), ((0, QUARTER), (QUARTER, S2 - QUARTER)))
        rdr = {}

        def gather_readers(a):
            for first, count in pieces[a]:
                words = held("rdr%d_%d" % (a, first), [P, count], U32)
                nc.vector.tensor_copy(
                    words[:], rdr_table[a][:].bitcast(U32).indirect(rdr_list[:, first // 16 : (first + count) // 16])
                )
                for q in range(first // QUARTER, (first + count) // QUARTER):
                    rdr[a, q] = words[:, QUARTER * q - first : QUARTER * (q + 1) - first]

        for b in range(2):
            nc.vector.tensor_copy(
                art_sc_listed[:, HALF * b : HALF * (b + 1)],
                art_table_sc[:].bitcast(U8).indirect(art_list[:, 32 * b : 32 * (b + 1)]),
            )

        def sort_scales(b):
            nc.vector.tensor_copy(
                planes[0][:].bitcast(U8)[:, HALF * b : HALF * (b + 1)].rearrange("p (t m) -> p t m", t=PACK),
                art_sc_listed[:, HALF * b : HALF * (b + 1)].rearrange("p (m t) -> p t m", t=PACK),
            )

        sort_scales(0)
        nc.vector.tensor_copy(rdr_sc_listed[:], rdr_table_sc[:].bitcast(U8).indirect(rdr_list[:]))
        sort_scales(1)
        nc.vector.tensor_copy(
            planes[0][SC_FIRST:P, S // 4 :], rdr_sc_listed[:].bitcast(I32)[RDR_FIRST : RDR_FIRST + 32, :]
        )
        for c in range(QUADRANTS - 1):
            row = 32 * c + PLANE_ROW[0]
            nc.sync.dma_start(planes[0][row : row + 4, :], planes[0][SC_FIRST + 4 * c : SC_FIRST + 4 * c + 4, :])
        nc.sync.dma_start(rdr_table[1][:], table_words(tab2_words, 1))
        for r in range(4):
            nc.sync.dma_start(planes[1][r:P:32, :], planes[0][SC_FIRST + 16 + r : P : 4, :])

        def gather_articles(a):
            nc.vector.tensor_copy(
                art[a][:].rearrange("p (b t m) -> p b m t", b=2, t=PACK),
                art_table[a][:].bitcast(U32).indirect(art_list[:]),
            )

        gather_articles(0)
        gather_readers(0)
        gather_articles(1)

        for b in range(2):
            nc.sync.dma_start(
                wd_raw[b][:].rearrange("p t n -> p (t n)"),
                wd[HALF * b : HALF * (b + 1), :].rearrange("(p t) n -> p (t n)", t=PACK),
            )
        nc.sync.dma_start(w4_codes[:].bitcast(I32), w4_words.rearrange("b p w -> p b w").bitcast(I32))
        for c in range(QUADRANTS):
            nc.sync.dma_start(
                w4_sc[32 * c : 32 * c + 4, :, :],
                w4_scales[:, 4 * c : 4 * c + 4, :].rearrange("b r n -> r b n").bitcast(I32),
            )
        nc.sync.dma_start(gate_all[:], gate.rearrange("(n p) j -> p n j", p=P))
        gate_sb = [gate_all[:, :, QUARTER * q : QUARTER * (q + 1)] for q in range(4)]

        gather_readers(1)

        taken = []

        def next_bank(shape):
            taken.append(psum.tile(shape, F32, name="bank", tag="bank%d" % (len(taken) % BANKS)))
            return taken[-1]

        matches = {}

        def match_pass(a, u, part):
            q, b = divmod(u, 2)
            count, width = (PACK, P) if q == 0 else (2, QUARTER)
            first_t, first_j = (0, P * part) if q == 0 else (2 * part, 0)
            if a == 0:
                matches[u, part] = next_bank([P, count, width])
            plane = planes[a][:].bitcast(U8)
            readers = S + QUARTER * q + first_j
            for e in range(count):
                col = HALF * b + P * (first_t + e)
                nc.tensor.matmul_mx(
                    out=matches[u, part][:, e, :],
                    lhsT=art[a][:, col : col + P].bitcast(FP8X4),
                    lhsT_scale=plane[PLANE_ROW[a] :, col : col + P],
                    rhs=rdr[a, q][:, first_j : first_j + width].bitcast(FP8X4),
                    rhs_scale=plane[PLANE_ROW[a] :, readers : readers + width],
                    start=(a == 0 and e == 0),
                    stop=(a == 1 and e == count - 1),
                )

        keys = [(u, part) for u in range(UNITS) for part in range(2)]
        for key in keys[:BANKS]:
            match_pass(0, *key)
        for key in keys:
            if key not in matches:
                match_pass(0, *key)
            match_pass(1, *key)

        bounded = {}

        def squash(u):
            bounded[u] = held("bounded%d" % u, [P, UNIT + (HALF if u == UNITS - 2 else 0)], F32)
            side_by_side = PACK if u < 2 else 2
            for part in range(2):
                nc.scalar.activation(
                    out=bounded[u][:, HALF * part : HALF * (part + 1)].rearrange("p (j e) -> p j e", e=side_by_side),
                    in_=matches[u, part][:].rearrange("p e j -> p j e"),
                    func=TANH,
                )

        def in_row(name, u, skip, shape, dtype):
            place = (3 - u // 2) * SLIDE + u % 2 * UNIT if u < UNITS - 1 else 2 * UNIT + 3 * SLIDE
            return sliding.tile(shape, dtype, name=name, offset=2 * (place + skip), align_bytes=64)

        values = {}

        def region(u):
            if u not in values:
                values[u] = in_row("values%d" % u, u, 0, [P, UNIT], BF16)
            return values[u][:]

        def weigh(engine, u, cols, factors):
            engine.tensor_tensor(
                region(u).rearrange("p (j h e) -> p j h e", h=2, e=2)[:, cols],
                bounded[u][:, 0:UNIT].rearrange("p (h j e) -> p j h e", h=2, e=2)[:, cols],
                factors,
                MULT,
            )

        def weigh_vector(u):
            share = SHARE.get(u, 0)
            factors = fresh_ps[:, P - 2 + u % 2, :].rearrange("p (h e) -> p h e", e=2)
            weigh(nc.vector, u, slice(share, QUARTER), factors.unsqueeze(1).to_broadcast([P, QUARTER - share, 2, 2]))

        def weigh_gpsimd(u):
            wide = fresh_wide[:].rearrange("p (j h e) -> p j h e", h=2, e=2)[:, 0 : SHARE[u]]
            weigh(nc.gpsimd, u, slice(0, SHARE[u]), wide)

        def quantise(codes, scales, src):
            nc.vector.quantize_mx(out=codes.bitcast(FP8X4), scales=scales, in_=src)

        wd_codes = held("wd_codes", [P, 2 * N], U32)
        wd_sc = held("wd_sc", [P, 2 * N], U8)
        wd_rounded = held("wd_rounded", [P, 2 * UNIT], BF16)
        for b in range(2):
            nc.gpsimd.tensor_scalar(
                wd_rounded[:, UNIT * b : UNIT * (b + 1)].rearrange("p (g x t) -> p g t x", x=2, t=PACK),
                wd_raw[b][:].rearrange("p t (g x) -> p g t x", x=2),
                1.0,
                0.0,
                MULT,
                ADD,
            )

        def section_passes(acc, n, b, codes, scales, start, stop):
            sections = slice(P * n, P * (n + 1))
            nc.tensor.matmul_mx(
                out=acc,
                lhsT=w4_codes[:, b, 2 * P * n : 2 * P * (n + 1)].bitcast(FP4X4),
                lhsT_scale=w4_sc[:, b, :].bitcast(U8)[:, sections],
                rhs=codes.bitcast(FP8X4),
                rhs_scale=scales,
                start=start,
                stop=False,
            )
            nc.tensor.matmul_mx(
                out=acc,
                lhsT=wd_codes[:, N * b : N * (b + 1)][:, sections].bitcast(FP8X4),
                lhsT_scale=wd_sc[:, N * b : N * (b + 1)][:, sections],
                rhs=codes.bitcast(FP8X4),
                rhs_scale=scales,
                start=False,
                stop=stop,
            )

        sums = {}
        quantised = {}

        def quantise_unit(u):
            if u < 2:
                codes = reuse.tile(
                    [P, QUARTER], U32, name="z_codes%d" % u, offset=4 * UNIT + 4 * QUARTER * u, align_bytes=256
                )[:]
            else:
                codes = held("z_codes%d" % u, [P, QUARTER], U32)[:]
            scales = held("z_sc%d" % u, [P, QUARTER], U8)[:]
            quantise(codes, scales, region(u))
            quantised[u] = (codes, scales)

        def contract(u):
            q, b = divmod(u, 2)
            if b == 0:
                bank = next_bank([P, 2, QUARTER])
                sums[q] = [bank[:, 0, :], bank[:, 1, :], bank[:]]
            for n in range(2):
                section_passes(sums[q][n], n, b, *quantised[u], b + n == 0, b + n == 2)

        for u in range(2):
            squash(u)
            for part in range(2):
                cols = slice(HALF * part, HALF * (part + 1))
                nc.vector.tensor_tensor(
                    region(u)[:, cols].rearrange("p (j t) -> p j t", t=PACK),
                    bounded[u][:, cols].rearrange("p (j t) -> p j t", t=PACK),
                    fresh_ps[:, P - 2 + u, :].unsqueeze(1).to_broadcast([P, P, PACK]),
                    MULT,
                )
        quantise(wd_codes[:], wd_sc[:], wd_rounded[:])
        for u in range(2):
            quantise_unit(u)
            contract(u)
        for u in range(2, UNITS - 2, 2):
            squash(u)
            weigh_gpsimd(u)
            weigh_vector(u)
            squash(u + 1)
            weigh_vector(u + 1)
            for v in (u, u + 1):
                quantise_unit(v)
                contract(v)

        last = UNITS - 1
        squash(last - 1)
        weigh_gpsimd(last - 1)
        weigh_vector(last - 1)
        rows32 = held("rows32", [P, PACK, QUARTER], F32)
        for part in range(2):
            nc.scalar.activation(out=rows32[:, 2 * part : 2 * part + 2, :], in_=matches[last, part][:], func=TANH)
        rows16 = reuse.tile([P, PACK, OWN], BF16, name="rows16", offset=0, align_bytes=256)
        for t in range(PACK):
            nc.scalar.activation(out=rows16[:, t, :], in_=rows32[:, t, 0:OWN], func=COPY, scale=fresh_sb[:, t : t + 1])
        nc.scalar.copy(
            out=region(last)[:, 0 : PACK * OWN].rearrange("p (g x t) -> p g t x", x=4, t=PACK),
            in_=rows16[:].rearrange("p t (g x) -> p g t x", x=4),
        )
        nc.vector.tensor_tensor(
            region(last)[:, PACK * OWN :].rearrange("p (j t) -> p j t", t=PACK),
            rows32[:, :, OWN:].rearrange("p t j -> p j t"),
            fresh_ps[:, P - 1, :].unsqueeze(1).to_broadcast([P, QUARTER - OWN, PACK]),
            MULT,
        )
        scores = bounded[last - 1][:, UNIT - P : UNIT - P + HALF].rearrange("p (n j) -> p n j", n=2)
        nc.vector.tensor_tensor(scores, sums[0][2], gate_sb[0], MULT)
        nc.sync.dma_start(out[:, 0:QUARTER].rearrange("(n p) j -> p n j", p=P), scores)
        upper = rows32[:, PACK - 1, :]
        nc.vector.tensor_tensor(upper, sums[1][0], gate_sb[1][:, 0, :], MULT)
        nc.sync.dma_start(out[0:P, QUARTER:HALF], upper)
        spilled = reuse.tile([P, QUARTER], F32, name="spilled", offset=0, align_bytes=256)
        nc.scalar.copy(out=spilled[:], in_=sums[1][1])
        for u in (last - 1, last):
            quantise_unit(u)
        ends = []
        for n, first, count in ((0, 0, QUARTER), (1, 0, P), (1, P, P)):
            bank = next_bank([P, count])[:]
            for b in range(2):
                codes, scales = quantised[last - 1 + b]
                readers = slice(first, first + count)
                section_passes(bank, n, b, codes[:, readers], scales[:, readers], b == 0, b == 1)
            ends.append((n, first, count, bank))
        lower = in_row("scores11", last - 1, 0, [P, QUARTER], F32)[:]
        nc.gpsimd.tensor_tensor(lower, spilled[:], gate_sb[1][:, 1, :], MULT)
        nc.scalar.dma_start(out[P:, QUARTER:HALF], lower)
        for n, queue in ((0, nc.scalar), (1, nc.sync)):
            scores = in_row("scores2%d" % n, last - 1 + n, HALF, [P, QUARTER], F32)[:]
            nc.vector.tensor_tensor(scores, sums[2][n], gate_sb[2][:, n, :], MULT)
            queue.dma_start(out[P * n : P * (n + 1), HALF : HALF + QUARTER], scores)
        for (n, first, count, bank), queue in zip(ends, (nc.sync, nc.scalar, nc.sync)):
            scores = held("scores3%d_%d" % (n, first), [P, count], F32)[:]
            nc.vector.tensor_tensor(scores, bank, gate_sb[3][:, n, first : first + count], MULT)
            column = 3 * QUARTER + first
            queue.dma_start(out[P * n : P * (n + 1), column : column + count], scores)
